import numpy as np
import ml_dtypes


def mxq(x, axis, fmt="e4m3"):
    dtype, down = {"e4m3": (ml_dtypes.float8_e4m3fn, 7), "e5m2": (ml_dtypes.float8_e5m2, 14)}[fmt]
    v = np.moveaxis(np.asarray(x, np.float32).astype(ml_dtypes.bfloat16).astype(np.float64), axis, -1)
    blocks = v.reshape(v.shape[:-1] + (-1, 32))
    amax = np.abs(blocks).max(-1, keepdims=True)
    byte = np.maximum(np.where(amax > 0, np.frexp(amax)[1] - 1 + 127, 0) - down, 1)
    scale = np.exp2(byte - 127.0)
    codes = (blocks / scale).astype(np.float32).astype(dtype).astype(np.float64)
    return np.moveaxis((codes * scale).reshape(v.shape), -1, axis)


WIDE = False


def mx_kscale(k):
    if not WIDE:
        return np.ones(k)
    levels = np.array([10, -10, 5, -5, 0])
    if k % 512:
        return np.exp2(np.random.permutation(np.resize(levels, k // 32))).repeat(32)
    a = np.empty((k // 512, 16))
    for p in range(k // 512):
        a[p, :8] = np.random.permutation(np.resize(levels, 8))
        for g in range(8):
            far = levels[np.abs(levels - a[p, g]) >= 10]
            a[p, g + 8] = far[np.random.randint(len(far))]
    return np.exp2(a.ravel()).repeat(32)


def f64(x):
    return np.asarray(x).astype(np.float64)


def striped(idx):
    return np.tile(idx.reshape(-1, 16).T, (8, 1)).astype(np.uint16)


def unstriped(offs):
    return offs[:16].T.reshape(-1).astype(np.int64)


def pack_weight(w):
    k, n = w.shape
    w = f64(np.asarray(w, np.float32).astype(ml_dtypes.bfloat16)).reshape(k // 32, 32, n)
    amax = np.abs(w).max(1)
    byte = np.clip(np.where(amax > 0, np.frexp(amax)[1] - 1 + 127 - 7, 1), 1, 254)
    scaled = (w * np.exp2(127.0 - byte)[:, None, :]).reshape(k, n).astype(np.float32)
    words = np.ascontiguousarray(scaled.reshape(k // 512, 128, 4, n).transpose(0, 1, 3, 2)).astype(ml_dtypes.float8_e4m3fn).view(np.uint8)
    return words, np.ascontiguousarray(byte.astype(np.uint8).reshape(k // 512, 16, n))


def unpack_weight(words, scales):
    g, p, n, _ = words.shape
    vals = np.ascontiguousarray(words).view(ml_dtypes.float8_e4m3fn).astype(np.float64) * np.repeat(np.exp2(scales.astype(np.float64) - 127.0), 8, axis=1)[..., None]
    return vals.transpose(0, 1, 3, 2).reshape(g * 512, n)


K, T, E, C, N = 1024, 1536, 12, 128, 384


def by_expert(wq, xq):
    return np.concatenate([wq[e].T @ xq[:, e * C:(e + 1) * C] for e in range(E)], axis=1)


def setup_inputs():
    n = np.random.standard_normal
    s = mx_kscale(K)[:, None]
    packed = [pack_weight(m) for m in n((E, K, N)) / np.sqrt(K) / s[None]]
    return {
        "xT": (n((K, T)) * s).astype(np.float32),
        "w_words": np.stack([m[0] for m in packed]),
        "w_scales": np.stack([m[1] for m in packed]),
        "b": (0.3 * n((N, E))).astype(np.float32),
        "gate": np.tile(np.random.uniform(0.2, 1.0, E * C), (K, 1)).astype(np.float32),
        "offs": striped(np.random.permutation(T)[:E * C]),
    }


def reference(xT, w_words, w_scales, b, gate, offs):
    idx = unstriped(offs)
    w = np.stack([unpack_weight(w_words[e], w_scales[e]) for e in range(E)])
    xq = mxq(f64(gate) * f64(xT)[:, idx], 0, "e4m3")
    y = by_expert(w, xq)
    y = y + np.repeat(f64(b), C, axis=1)
    out = np.zeros((N, T))
    out[:, idx] = y
    return out

@@ -1,0 +1,166 @@
+from contextlib import ExitStack
+
+import concourse.mybir as mybir
+
+K, T, E, C, N = 1024, 1536, 12, 128, 384
+S = E * C
+FLOPS = 2 * K * N * S
+BYTES = 4 * K * T + E * K * N + E * K * N // 32 + 4 * N * E + 4 * S + 2 * S + 4 * N * T
+
+F32 = mybir.dt.float32
+BF16 = mybir.dt.bfloat16
+I32 = mybir.dt.int32
+U32 = mybir.dt.uint32
+U16 = mybir.dt.uint16
+U8 = mybir.dt.uint8
+FP8X4 = mybir.dt.float8_e4m3fn_x4
+MULT = mybir.AluOpType.mult
+COPY = mybir.ActivationFunctionType.Copy
+IDENT = mybir.ActivationFunctionType.Identity
+
+P = 128
+PACK = 4
+PASSES = K // (P * PACK)
+NT = N // P
+GROUP = 512
+GROUPS = S // GROUP
+EG = GROUP // C
+
+
+def tile_moe_pre_lin_bias_kernel(tc, xT, w_words, w_scales, b, gate, offs, out):
+    nc = tc.nc
+    with ExitStack() as ctx:
+        keep = ctx.enter_context(tc.tile_pool(name="keep", bufs=1))
+        psum = ctx.enter_context(tc.psum_pool(name="psum", bufs=8))
+
+        offsets = keep.tile([P, S // 16], U16, name="offsets")
+        planes = [keep.tile([P, T], F32, name="plane%d" % i) for i in range(PASSES * PACK)]
+        gates = keep.tile([P, S], F32, name="gates")
+        gathered = [keep.tile([P, PACK, S], F32, name="gathered%d" % a) for a in range(PASSES)]
+        rounded = [keep.tile([P, S, PACK], BF16, name="rounded%d" % a, align_bytes=64) for a in range(PASSES)]
+        x_codes = [keep.tile([P, S], U32, name="x_codes%d" % a, align_bytes=64) for a in range(PASSES)]
+        x_scales = [keep.tile([P, S], U8, name="x_scales%d" % a, align_bytes=64) for a in range(PASSES)]
+        w_codes = [keep.tile([P, EG * PASSES, N], U32, name="w_codes%d" % g, align_bytes=64) for g in range(GROUPS)]
+        w_planes = keep.tile([P, E, N], U8, name="w_planes", align_bytes=64)
+        bias = keep.tile([P, NT, E], F32, name="bias")
+        ys = [keep.tile([P, S], F32, name="y%d" % c) for c in range(NT)]
+        windows = [keep.tile([P, T], F32, name="window%d" % c) for c in range(NT)]
+
+        x_rows = xT.rearrange("(a p t) c -> a t p c", a=PASSES, t=PACK)
+
+        def load_plane(i):
+            nc.sync.dma_start(out=planes[i][:], in_=x_rows[i // PACK, i % PACK])
+
+        def load_gate(lo, hi):
+            nc.sync.dma_start(out=gates[:, lo:hi], in_=gate[0:P, lo:hi])
+
+        def gather(i, lo, hi):
+            nc.vector.tensor_tensor(
+                gathered[i // PACK][:, i % PACK, lo:hi],
+                planes[i][:].indirect(offsets[:, lo // 16:hi // 16]),
+                gates[:, lo:hi],
+                MULT,
+            )
+
+        def interleave(a, g):
+            cols = slice(g * GROUP, (g + 1) * GROUP)
+            nc.scalar.activation(
+                rounded[a][:, cols, :].rearrange("p (c i) t -> p c t i", i=4),
+                gathered[a][:, :, cols].rearrange("p t (c i) -> p c t i", i=4),
+                COPY,
+            )
+
+        def quantize(a, lo, hi):
+            nc.vector.quantize_mx(
+                out=x_codes[a][:, lo:hi].bitcast(FP8X4),
+                scales=x_scales[a][:, lo:hi],
+                in_=rounded[a][:, lo:hi, :].rearrange("p s t -> p (s t)"),
+            )
+
+        def multiply(g, c):
+            acc = psum.tile([P, GROUP], F32, name="acc")
+            ncols = slice(c * P, (c + 1) * P)
+            for le in range(EG):
+                e = g * EG + le
+                slots = slice(e * C, (e + 1) * C)
+                for a in range(PASSES):
+                    nc.tensor.matmul_mx(
+                        out=acc[:, le * C:(le + 1) * C],
+                        lhsT=w_codes[g][:, le * PASSES + a, ncols].bitcast(FP8X4),
+                        lhsT_scale=w_planes[4 * a:P, e, ncols],
+                        rhs=x_codes[a][:, slots].bitcast(FP8X4),
+                        rhs_scale=x_scales[a][:, slots],
+                        start=(a == 0),
+                        stop=(a == PASSES - 1),
+                    )
+            for le in range(EG):
+                e = g * EG + le
+                nc.scalar.activation(
+                    ys[c][:, e * C:(e + 1) * C], acc[:, le * C:(le + 1) * C], IDENT, bias=bias[:, c, e:e + 1]
+                )
+
+        def scatter(c, lo, hi):
+            nc.vector.tensor_copy(windows[c][:].indirect(offsets[:, lo // 16:hi // 16]), ys[c][:, lo:hi])
+
+        def store(c):
+            nc.sync.dma_start(out=out[c * P:(c + 1) * P, :], in_=windows[c][:])
+
+        plane_words = w_planes[:].bitcast(I32)
+        nc.vector.memset(plane_words, 0)
+
+        load_plane(0)
+        nc.sync.dma_start(offsets[:], offs)
+        first = [0, 256, 768, S]
+        for lo, hi in zip(first, first[1:]):
+            load_gate(lo, hi)
+        for i in range(1, PASSES * PACK):
+            load_plane(i)
+        for q in range(4):
+            for a in range(PASSES):
+                nc.sync.dma_start(
+                    out=plane_words[32 * q + 4 * a:32 * q + 4 * a + 4, :, :],
+                    in_=w_scales[:, a, 4 * q:4 * q + 4, :].rearrange("e r n -> r e n").bitcast(I32),
+                )
+        nc.sync.dma_start(out=bias[:], in_=b.rearrange("(c p) e -> p c e", p=P))
+        for g in range(GROUPS):
+            nc.sync.dma_start(
+                out=w_codes[g][:].bitcast(I32),
+                in_=w_words[g * EG:(g + 1) * EG].rearrange("e a p n r -> p (e a) (n r)").bitcast(I32),
+            )
+
+        for lo, hi in zip(first, first[1:]):
+            gather(0, lo, hi)
+        gather(1, 0, S // 2)
+        gather(1, S // 2, S)
+        for g in range(GROUPS):
+            gather(2, g * GROUP, (g + 1) * GROUP)
+            gather(3, g * GROUP, (g + 1) * GROUP)
+            interleave(0, g)
+
+        def gather_second(g):
+            for t in range(PACK):
+                gather(PACK + t, g * GROUP, (g + 1) * GROUP)
+            interleave(1, g)
+
+        gather_second(0)
+        quantize(0, 0, 2 * GROUP)
+        gather_second(1)
+        quantize(0, 2 * GROUP, S)
+        quantize(1, 0, GROUP)
+        for c in range(NT):
+            multiply(0, c)
+        gather_second(2)
+        quantize(1, GROUP, 2 * GROUP)
+        scatter(0, 0, GROUP)
+        quantize(1, 2 * GROUP, S)
+        for c in range(NT):
+            multiply(1, c)
+            multiply(2, c)
+        scatter(1, 0, GROUP)
+        scatter(0, GROUP, S)
+        store(0)
+        scatter(2, 0, GROUP)
+        scatter(1, GROUP, S)
+        store(1)
+        scatter(2, GROUP, S)
+        store(2)

@@ -25,71 +25,97 @@ NT = N // P
 GROUP = 512
 GROUPS = S // GROUP
 EG = GROUP // C
+GATHERED_BYTES = PACK * GROUP * 4
+WIDE = 2048
+OPENING = [(GROUP, GROUP + 320), (GROUP + 320, S), (0, GROUP)]
 
 
 def tile_moe_pre_lin_bias_kernel(tc, xT, w_words, w_scales, b, gate, offs, out):
     nc = tc.nc
     with ExitStack() as ctx:
         keep = ctx.enter_context(tc.tile_pool(name="keep", bufs=1))
+        shared = ctx.enter_context(tc.tile_pool(name="shared", bufs=1))
         psum = ctx.enter_context(tc.psum_pool(name="psum", bufs=8))
 
         offsets = keep.tile([P, S // 16], U16, name="offsets")
         planes = [keep.tile([P, T], F32, name="plane%d" % i) for i in range(PASSES * PACK)]
-        gates = keep.tile([P, S], F32, name="gates")
-        gathered = [keep.tile([P, PACK, S], F32, name="gathered%d" % a) for a in range(PASSES)]
-        rounded = [keep.tile([P, S, PACK], BF16, name="rounded%d" % a, align_bytes=64) for a in range(PASSES)]
-        x_codes = [keep.tile([P, S], U32, name="x_codes%d" % a, align_bytes=64) for a in range(PASSES)]
-        x_scales = [keep.tile([P, S], U8, name="x_scales%d" % a, align_bytes=64) for a in range(PASSES)]
+        gate_head = shared.tile([P, GROUP], F32, name="gate_head", offset=GATHERED_BYTES)
+        gate_rest = keep.tile([P, S - GROUP], F32, name="gate_rest")
+        first_head = keep.tile([P, PACK, GROUP], F32, name="first_head")
+        first_rest = keep.tile([P, PACK, S - GROUP], F32, name="first_rest")
+        second = [
+            shared.tile([P, PACK, GROUP], F32, name="second%d" % g, offset=(g % 2) * GATHERED_BYTES)
+            for g in range(GROUPS)
+        ]
+        rounded = [keep.tile([P, PASSES, GROUP, PACK], BF16, name="rounded%d" % g, align_bytes=64) for g in range(GROUPS)]
+        x_codes = [keep.tile([P, PASSES, GROUP], U32, name="x_codes%d" % g, align_bytes=64) for g in range(GROUPS)]
+        x_scales = [keep.tile([P, PASSES, GROUP], U8, name="x_scales%d" % g, align_bytes=64) for g in range(GROUPS)]
         w_codes = [keep.tile([P, EG * PASSES, N], U32, name="w_codes%d" % g, align_bytes=64) for g in range(GROUPS)]
         w_planes = keep.tile([P, E, N], U8, name="w_planes", align_bytes=64)
         bias = keep.tile([P, NT, E], F32, name="bias")
         ys = [keep.tile([P, S], F32, name="y%d" % c) for c in range(NT)]
-        windows = [keep.tile([P, T], F32, name="window%d" % c) for c in range(NT)]
+        windows = [
+            keep.tile([P, T], F32, name="window0"),
+            shared.tile([P, T], F32, name="window1", offset=0),
+            keep.tile([P, WIDE], F32, name="window2"),
+        ]
 
         x_rows = xT.rearrange("(a p t) c -> a t p c", a=PASSES, t=PACK)
+
+        def gates(lo, hi):
+            if hi <= GROUP:
+                return gate_head[:, lo:hi]
+            return gate_rest[:, lo - GROUP:hi - GROUP]
+
+        def gathered(a, lo, hi):
+            if a == 1:
+                return second[lo // GROUP][:]
+            if hi <= GROUP:
+                return first_head[:, :, lo:hi]
+            return first_rest[:, :, lo - GROUP:hi - GROUP]
 
         def load_plane(i):
             nc.sync.dma_start(out=planes[i][:], in_=x_rows[i // PACK, i % PACK])
 
-        def load_gate(lo, hi):
-            nc.sync.dma_start(out=gates[:, lo:hi], in_=gate[0:P, lo:hi])
-
         def gather(i, lo, hi):
             nc.vector.tensor_tensor(
-                gathered[i // PACK][:, i % PACK, lo:hi],
+                gathered(i // PACK, lo, hi)[:, i % PACK, :],
                 planes[i][:].indirect(offsets[:, lo // 16:hi // 16]),
-                gates[:, lo:hi],
+                gates(lo, hi),
                 MULT,
             )
 
         def interleave(a, g):
-            cols = slice(g * GROUP, (g + 1) * GROUP)
             nc.scalar.activation(
-                rounded[a][:, cols, :].rearrange("p (c i) t -> p c t i", i=4),
-                gathered[a][:, :, cols].rearrange("p t (c i) -> p c t i", i=4),
+                rounded[g][:, a, :, :].rearrange("p (c i) t -> p c t i", i=4),
+                gathered(a, g * GROUP, (g + 1) * GROUP).rearrange("p t (c i) -> p c t i", i=4),
                 COPY,
             )
 
-        def quantize(a, lo, hi):
+        def gather_second(g):
+            for t in range(PACK):
+                gather(PACK + t, g * GROUP, (g + 1) * GROUP)
+            interleave(1, g)
+
+        def quantize(g):
             nc.vector.quantize_mx(
-                out=x_codes[a][:, lo:hi].bitcast(FP8X4),
-                scales=x_scales[a][:, lo:hi],
-                in_=rounded[a][:, lo:hi, :].rearrange("p s t -> p (s t)"),
+                out=x_codes[g][:].rearrange("p a s -> p (a s)").bitcast(FP8X4),
+                scales=x_scales[g][:].rearrange("p a s -> p (a s)"),
+                in_=rounded[g][:].rearrange("p a s t -> p (a s t)"),
             )
 
         def multiply(g, c):
             acc = psum.tile([P, GROUP], F32, name="acc")
             ncols = slice(c * P, (c + 1) * P)
             for le in range(EG):
-                e = g * EG + le
-                slots = slice(e * C, (e + 1) * C)
+                slots = slice(le * C, (le + 1) * C)
                 for a in range(PASSES):
                     nc.tensor.matmul_mx(
-                        out=acc[:, le * C:(le + 1) * C],
+                        out=acc[:, slots],
                         lhsT=w_codes[g][:, le * PASSES + a, ncols].bitcast(FP8X4),
-                        lhsT_scale=w_planes[4 * a:P, e, ncols],
-                        rhs=x_codes[a][:, slots].bitcast(FP8X4),
-                        rhs_scale=x_scales[a][:, slots],
+                        lhsT_scale=w_planes[4 * a:P, g * EG + le, ncols],
+                        rhs=x_codes[g][:, a, slots].bitcast(FP8X4),
+                        rhs_scale=x_scales[g][:, a, slots],
                         start=(a == 0),
                         stop=(a == PASSES - 1),
                     )
@@ -103,16 +129,15 @@ def tile_moe_pre_lin_bias_kernel(tc, xT, w_words, w_scales, b, gate, offs, out):
             nc.vector.tensor_copy(windows[c][:].indirect(offsets[:, lo // 16:hi // 16]), ys[c][:, lo:hi])
 
         def store(c):
-            nc.sync.dma_start(out=out[c * P:(c + 1) * P, :], in_=windows[c][:])
+            nc.sync.dma_start(out=out[c * P:(c + 1) * P, :], in_=windows[c][:, 0:T])
 
         plane_words = w_planes[:].bitcast(I32)
         nc.vector.memset(plane_words, 0)
 
         load_plane(0)
         nc.sync.dma_start(offsets[:], offs)
-        first = [0, 256, 768, S]
-        for lo, hi in zip(first, first[1:]):
-            load_gate(lo, hi)
+        for lo, hi in OPENING:
+            nc.sync.dma_start(out=gates(lo, hi), in_=gate[0:P, lo:hi])
         for i in range(1, PASSES * PACK):
             load_plane(i)
         for q in range(4):
@@ -128,39 +153,34 @@ def tile_moe_pre_lin_bias_kernel(tc, xT, w_words, w_scales, b, gate, offs, out):
                 in_=w_words[g * EG:(g + 1) * EG].rearrange("e a p n r -> p (e a) (n r)").bitcast(I32),
             )
 
-        for lo, hi in zip(first, first[1:]):
+        for lo, hi in OPENING:
             gather(0, lo, hi)
-        gather(1, 0, S // 2)
-        gather(1, S // 2, S)
-        for g in range(GROUPS):
-            gather(2, g * GROUP, (g + 1) * GROUP)
-            gather(3, g * GROUP, (g + 1) * GROUP)
-            interleave(0, g)
-
-        def gather_second(g):
-            for t in range(PACK):
-                gather(PACK + t, g * GROUP, (g + 1) * GROUP)
-            interleave(1, g)
-
+        for t in range(1, PACK):
+            gather(t, 0, GROUP)
+            if t == PACK - 1:
+                interleave(0, 0)
+            gather(t, GROUP, S)
+        interleave(0, 1)
         gather_second(0)
-        quantize(0, 0, 2 * GROUP)
+        interleave(0, 2)
         gather_second(1)
-        quantize(0, 2 * GROUP, S)
-        quantize(1, 0, GROUP)
-        for c in range(NT):
-            multiply(0, c)
+        quantize(0)
+        multiply(0, 0)
         gather_second(2)
-        quantize(1, GROUP, 2 * GROUP)
+        quantize(1)
         scatter(0, 0, GROUP)
-        quantize(1, 2 * GROUP, S)
-        for c in range(NT):
-            multiply(1, c)
-            multiply(2, c)
-        scatter(1, 0, GROUP)
+        quantize(2)
+        multiply(0, 1)
+        multiply(1, 1)
+        scatter(1, 0, 2 * GROUP)
+        multiply(1, 0)
+        multiply(2, 0)
         scatter(0, GROUP, S)
         store(0)
-        scatter(2, 0, GROUP)
-        scatter(1, GROUP, S)
+        multiply(2, 1)
+        scatter(1, 2 * GROUP, S)
         store(1)
-        scatter(2, GROUP, S)
+        for g in range(GROUPS):
+            multiply(g, 2)
+        scatter(2, 0, S)
         store(2)

@@ -27,7 +27,7 @@ GROUPS = S // GROUP
 EG = GROUP // C
 GATHERED_BYTES = PACK * GROUP * 4
 WIDE = 2048
-OPENING = [(GROUP, GROUP + 320), (GROUP + 320, S), (0, GROUP)]
+OPENING = [(0, 256), (256, 768), (768, S)]
 
 
 def tile_moe_pre_lin_bias_kernel(tc, xT, w_words, w_scales, b, gate, offs, out):
@@ -38,16 +38,19 @@ def tile_moe_pre_lin_bias_kernel(tc, xT, w_words, w_scales, b, gate, offs, out):
         psum = ctx.enter_context(tc.psum_pool(name="psum", bufs=8))
 
         offsets = keep.tile([P, S // 16], U16, name="offsets")
-        planes = [keep.tile([P, T], F32, name="plane%d" % i) for i in range(PASSES * PACK)]
+        planes = [keep.tile([P, T + 16], F32, name="plane%d" % i) for i in range(PASSES * PACK)]
+        gate_all = keep.tile([P, S], F32, name="gate_all")
         gate_head = shared.tile([P, GROUP], F32, name="gate_head", offset=GATHERED_BYTES)
-        gate_rest = keep.tile([P, S - GROUP], F32, name="gate_rest")
-        first_head = keep.tile([P, PACK, GROUP], F32, name="first_head")
-        first_rest = keep.tile([P, PACK, S - GROUP], F32, name="first_rest")
+        first = keep.tile([P, PACK, S], F32, name="first")
         second = [
             shared.tile([P, PACK, GROUP], F32, name="second%d" % g, offset=(g % 2) * GATHERED_BYTES)
             for g in range(GROUPS)
         ]
-        rounded = [keep.tile([P, PASSES, GROUP, PACK], BF16, name="rounded%d" % g, align_bytes=64) for g in range(GROUPS)]
+        rounded = [keep.tile([P, PASSES, GROUP, PACK], BF16, name="rounded%d" % g, align_bytes=64) for g in range(GROUPS - 1)]
+        bias_head = shared.tile([P, EG], F32, name="bias_head", offset=2 * GATHERED_BYTES)
+        rounded.append(
+            shared.tile([P, PASSES, GROUP, PACK], BF16, name="rounded_last", align_bytes=64, offset=2 * GATHERED_BYTES)
+        )
         x_codes = [keep.tile([P, PASSES, GROUP], U32, name="x_codes%d" % g, align_bytes=64) for g in range(GROUPS)]
         x_scales = [keep.tile([P, PASSES, GROUP], U8, name="x_scales%d" % g, align_bytes=64) for g in range(GROUPS)]
         w_codes = [keep.tile([P, EG * PASSES, N], U32, name="w_codes%d" % g, align_bytes=64) for g in range(GROUPS)]
@@ -62,26 +65,29 @@ def tile_moe_pre_lin_bias_kernel(tc, xT, w_words, w_scales, b, gate, offs, out):
 
         x_rows = xT.rearrange("(a p t) c -> a t p c", a=PASSES, t=PACK)
 
-        def gates(lo, hi):
-            if hi <= GROUP:
+        def gates(a, lo, hi):
+            if a == 1 and hi <= GROUP:
                 return gate_head[:, lo:hi]
-            return gate_rest[:, lo - GROUP:hi - GROUP]
+            return gate_all[:, lo:hi]
 
         def gathered(a, lo, hi):
             if a == 1:
                 return second[lo // GROUP][:]
-            if hi <= GROUP:
-                return first_head[:, :, lo:hi]
-            return first_rest[:, :, lo - GROUP:hi - GROUP]
+            return first[:, :, lo:hi]
+
+        def bias_of(c, e):
+            if c == 0 and e < EG:
+                return bias_head[:, e:e + 1]
+            return bias[:, c, e:e + 1]
 
         def load_plane(i):
-            nc.sync.dma_start(out=planes[i][:], in_=x_rows[i // PACK, i % PACK])
+            nc.sync.dma_start(out=planes[i][:, 0:T], in_=x_rows[i // PACK, i % PACK])
 
         def gather(i, lo, hi):
             nc.vector.tensor_tensor(
                 gathered(i // PACK, lo, hi)[:, i % PACK, :],
                 planes[i][:].indirect(offsets[:, lo // 16:hi // 16]),
-                gates(lo, hi),
+                gates(i // PACK, lo, hi),
                 MULT,
             )
 
@@ -122,7 +128,7 @@ def tile_moe_pre_lin_bias_kernel(tc, xT, w_words, w_scales, b, gate, offs, out):
             for le in range(EG):
                 e = g * EG + le
                 nc.scalar.activation(
-                    ys[c][:, e * C:(e + 1) * C], acc[:, le * C:(le + 1) * C], IDENT, bias=bias[:, c, e:e + 1]
+                    ys[c][:, e * C:(e + 1) * C], acc[:, le * C:(le + 1) * C], IDENT, bias=bias_of(c, e)
                 )
 
         def scatter(c, lo, hi):
@@ -137,8 +143,10 @@ def tile_moe_pre_lin_bias_kernel(tc, xT, w_words, w_scales, b, gate, offs, out):
         load_plane(0)
         nc.sync.dma_start(offsets[:], offs)
         for lo, hi in OPENING:
-            nc.sync.dma_start(out=gates(lo, hi), in_=gate[0:P, lo:hi])
+            nc.sync.dma_start(out=gate_all[:, lo:hi], in_=gate[0:P, lo:hi])
         for i in range(1, PASSES * PACK):
+            if i == PACK:
+                nc.sync.dma_start(out=gate_head[:], in_=gate[P:2 * P, 0:GROUP])
             load_plane(i)
         for q in range(4):
             for a in range(PASSES):
@@ -146,6 +154,7 @@ def tile_moe_pre_lin_bias_kernel(tc, xT, w_words, w_scales, b, gate, offs, out):
                     out=plane_words[32 * q + 4 * a:32 * q + 4 * a + 4, :, :],
                     in_=w_scales[:, a, 4 * q:4 * q + 4, :].rearrange("e r n -> r e n").bitcast(I32),
                 )
+        nc.sync.dma_start(out=bias_head[:], in_=b[0:P, 0:EG])
         nc.sync.dma_start(out=bias[:], in_=b.rearrange("(c p) e -> p c e", p=P))
         for g in range(GROUPS):
             nc.sync.dma_start(
@@ -156,16 +165,14 @@ def tile_moe_pre_lin_bias_kernel(tc, xT, w_words, w_scales, b, gate, offs, out):
         for lo, hi in OPENING:
             gather(0, lo, hi)
         for t in range(1, PACK):
-            gather(t, 0, GROUP)
-            if t == PACK - 1:
-                interleave(0, 0)
-            gather(t, GROUP, S)
+            gather(t, 0, S)
+        interleave(0, 0)
         interleave(0, 1)
         gather_second(0)
-        interleave(0, 2)
         gather_second(1)
         quantize(0)
         multiply(0, 0)
+        interleave(0, 2)
         gather_second(2)
         quantize(1)
         scatter(0, 0, GROUP)

@@ -1,6 +1,7 @@
 from contextlib import ExitStack
 
 import concourse.mybir as mybir
+from concourse.masks import make_identity
 
 K, T, E, C, N = 1024, 1536, 12, 128, 384
 S = E * C
@@ -14,9 +15,9 @@ U32 = mybir.dt.uint32
 U16 = mybir.dt.uint16
 U8 = mybir.dt.uint8
 FP8X4 = mybir.dt.float8_e4m3fn_x4
-MULT = mybir.AluOpType.mult
 COPY = mybir.ActivationFunctionType.Copy
 IDENT = mybir.ActivationFunctionType.Identity
+MULT = mybir.AluOpType.mult
 
 P = 128
 PACK = 4
@@ -25,83 +26,91 @@ NT = N // P
 GROUP = 512
 GROUPS = S // GROUP
 EG = GROUP // C
-GATHERED_BYTES = PACK * GROUP * 4
 WIDE = 2048
-OPENING = [(0, 256), (256, 768), (768, S)]
 
 
 def tile_moe_pre_lin_bias_kernel(tc, xT, w_words, w_scales, b, gate, offs, out):
     nc = tc.nc
     with ExitStack() as ctx:
         keep = ctx.enter_context(tc.tile_pool(name="keep", bufs=1))
-        shared = ctx.enter_context(tc.tile_pool(name="shared", bufs=1))
-        psum = ctx.enter_context(tc.psum_pool(name="psum", bufs=8))
+        stage = ctx.enter_context(tc.tile_pool(name="stage", bufs=3))
+        turn_psum = ctx.enter_context(tc.psum_pool(name="turn_psum", bufs=4))
+        back_psum = ctx.enter_context(tc.psum_pool(name="back_psum", bufs=2))
+        acc_psum = ctx.enter_context(tc.psum_pool(name="acc_psum", bufs=2))
 
         offsets = keep.tile([P, S // 16], U16, name="offsets")
-        planes = [keep.tile([P, T + 16], F32, name="plane%d" % i) for i in range(PASSES * PACK)]
-        gate_all = keep.tile([P, S], F32, name="gate_all")
-        gate_head = shared.tile([P, GROUP], F32, name="gate_head", offset=GATHERED_BYTES)
+        planes = [keep.tile([P, WIDE if i < PACK else T], F32, name="plane%d" % i) for i in range(PASSES * PACK)]
+        identity = keep.tile([P, P], F32, name="identity")
+        gate_head = keep.tile([P, GROUP], F32, name="gate_head")
+        gate_rest = keep.tile([P, S - GROUP], F32, name="gate_rest")
+        gate_rows = keep.tile([P, C], F32, name="gate_rows")
+        gate_cols = keep.tile([P, E], F32, name="gate_cols")
         first = keep.tile([P, PACK, S], F32, name="first")
-        second = [
-            shared.tile([P, PACK, GROUP], F32, name="second%d" % g, offset=(g % 2) * GATHERED_BYTES)
-            for g in range(GROUPS)
-        ]
-        rounded = [keep.tile([P, PASSES, GROUP, PACK], BF16, name="rounded%d" % g, align_bytes=64) for g in range(GROUPS - 1)]
-        bias_head = shared.tile([P, EG], F32, name="bias_head", offset=2 * GATHERED_BYTES)
-        rounded.append(
-            shared.tile([P, PASSES, GROUP, PACK], BF16, name="rounded_last", align_bytes=64, offset=2 * GATHERED_BYTES)
-        )
+        second_head = keep.tile([P, PACK, GROUP], F32, name="second_head")
+        second_rest = keep.tile([P, PACK, S - GROUP], F32, name="second_rest")
+        rounded = [keep.tile([P, PASSES, GROUP, PACK], BF16, name="rounded%d" % g, align_bytes=64) for g in range(GROUPS)]
         x_codes = [keep.tile([P, PASSES, GROUP], U32, name="x_codes%d" % g, align_bytes=64) for g in range(GROUPS)]
         x_scales = [keep.tile([P, PASSES, GROUP], U8, name="x_scales%d" % g, align_bytes=64) for g in range(GROUPS)]
-        w_codes = [keep.tile([P, EG * PASSES, N], U32, name="w_codes%d" % g, align_bytes=64) for g in range(GROUPS)]
+        w_head = keep.tile([P, EG * PASSES, P], U32, name="w_head", align_bytes=64)
+        w_codes = [
+            keep.tile([P, EG * PASSES, N - P if g == 0 else N], U32, name="w_codes%d" % g, align_bytes=64)
+            for g in range(GROUPS)
+        ]
         w_planes = keep.tile([P, E, N], U8, name="w_planes", align_bytes=64)
         bias = keep.tile([P, NT, E], F32, name="bias")
         ys = [keep.tile([P, S], F32, name="y%d" % c) for c in range(NT)]
-        windows = [
-            keep.tile([P, T], F32, name="window0"),
-            shared.tile([P, T], F32, name="window1", offset=0),
-            keep.tile([P, WIDE], F32, name="window2"),
-        ]
+        windows = [keep.tile([P, T], F32, name="window%d" % c) for c in range(NT)]
 
-        x_rows = xT.rearrange("(a p t) c -> a t p c", a=PASSES, t=PACK)
-
-        def gates(a, lo, hi):
-            if a == 1 and hi <= GROUP:
-                return gate_head[:, lo:hi]
-            return gate_all[:, lo:hi]
-
-        def gathered(a, lo, hi):
-            if a == 1:
-                return second[lo // GROUP][:]
-            return first[:, :, lo:hi]
-
-        def bias_of(c, e):
-            if c == 0 and e < EG:
-                return bias_head[:, e:e + 1]
-            return bias[:, c, e:e + 1]
+        late_rows = xT[P * PACK:K, :].rearrange("(p t) c -> t p c", t=PACK)
 
         def load_plane(i):
-            nc.sync.dma_start(out=planes[i][:, 0:T], in_=x_rows[i // PACK, i % PACK])
+            rows = xT[i * P:(i + 1) * P, :] if i < PACK else late_rows[i - PACK]
+            nc.sync.dma_start(out=planes[i][:, 0:T], in_=rows)
 
-        def gather(i, lo, hi):
-            nc.vector.tensor_tensor(
-                gathered(i // PACK, lo, hi)[:, i % PACK, :],
-                planes[i][:].indirect(offsets[:, lo // 16:hi // 16]),
-                gates(i // PACK, lo, hi),
-                MULT,
+        def load_weights(tile, g, lo, hi):
+            words = w_words[g * EG:(g + 1) * EG].rearrange("e a p n r -> p (e a) (n r)")
+            nc.sync.dma_start(out=tile[:].bitcast(I32), in_=words[:, :, lo * PACK:hi * PACK].bitcast(I32))
+
+        def turn_gate():
+            bank = turn_psum.tile([P, PACK, P], F32, name="turned")
+            nc.tensor.transpose(bank[:, 0, :], gate_rows[:], identity[:])
+            nc.scalar.copy(gate_cols[:], bank[:, 0, 0:E])
+
+        def scale_first(g, pair):
+            back = back_psum.tile([P, 2, 2, C], F32, name="back")
+            for h in range(2):
+                le = 2 * pair + h
+                e = g * EG + le
+                bank = turn_psum.tile([P, PACK, P], F32, name="turned")
+                for j in range(PACK):
+                    nc.tensor.transpose(bank[:, j, :], first[:, j, e * C:(e + 1) * C], identity[:])
+                staged = stage.tile([P, 2, P, 2], BF16, name="staged")
+                nc.scalar.activation(
+                    staged[:],
+                    bank[:].rearrange("s j (q u v) -> s u (j q) v", u=2, v=2),
+                    COPY,
+                    scale=gate_cols[:, e:e + 1],
+                )
+                words = staged[:].rearrange("s u p v -> s (u p v)").bitcast(F32)
+                for u in range(2):
+                    nc.tensor.transpose(back[:, h, u, :], words[:, u * P:(u + 1) * P], identity[:])
+            target = rounded[g][:, 0, 2 * pair * C:(2 * pair + 2) * C, :].rearrange("p s t -> p (s t)").bitcast(F32)
+            nc.scalar.copy(
+                target.rearrange("p (h s u) -> p h s u", h=2, u=2), back[:].rearrange("p h u s -> p h s u")
             )
 
-        def interleave(a, g):
+        def gather_second(t, tile, gates, lo, hi):
+            nc.vector.tensor_tensor(
+                tile[:, t, :], planes[PACK + t][:].indirect(offsets[:, lo // 16:hi // 16]), gates, MULT
+            )
+
+        def interleave(g):
+            source = second_head[:] if g == 0 else second_rest[:, :, (g - 1) * GROUP:g * GROUP]
             nc.scalar.activation(
-                rounded[g][:, a, :, :].rearrange("p (c i) t -> p c t i", i=4),
-                gathered(a, g * GROUP, (g + 1) * GROUP).rearrange("p t (c i) -> p c t i", i=4),
+                rounded[g][:, 1, :, :].rearrange("p (c i) t -> p c t i", i=4),
+                source.rearrange("p t (c i) -> p c t i", i=4),
                 COPY,
             )
-
-        def gather_second(g):
-            for t in range(PACK):
-                gather(PACK + t, g * GROUP, (g + 1) * GROUP)
-            interleave(1, g)
 
         def quantize(g):
             nc.vector.quantize_mx(
@@ -110,16 +119,22 @@ def tile_moe_pre_lin_bias_kernel(tc, xT, w_words, w_scales, b, gate, offs, out):
                 in_=rounded[g][:].rearrange("p a s t -> p (a s t)"),
             )
 
+        def weights(g, c, row):
+            if g > 0:
+                return w_codes[g][:, row, c * P:(c + 1) * P]
+            if c == 0:
+                return w_head[:, row, :]
+            return w_codes[0][:, row, (c - 1) * P:c * P]
+
         def multiply(g, c):
-            acc = psum.tile([P, GROUP], F32, name="acc")
-            ncols = slice(c * P, (c + 1) * P)
+            acc = acc_psum.tile([P, GROUP], F32, name="acc")
             for le in range(EG):
                 slots = slice(le * C, (le + 1) * C)
                 for a in range(PASSES):
                     nc.tensor.matmul_mx(
                         out=acc[:, slots],
-                        lhsT=w_codes[g][:, le * PASSES + a, ncols].bitcast(FP8X4),
-                        lhsT_scale=w_planes[4 * a:P, g * EG + le, ncols],
+                        lhsT=weights(g, c, le * PASSES + a).bitcast(FP8X4),
+                        lhsT_scale=w_planes[4 * a:P, g * EG + le, c * P:(c + 1) * P],
                         rhs=x_codes[g][:, a, slots].bitcast(FP8X4),
                         rhs_scale=x_scales[g][:, a, slots],
                         start=(a == 0),
@@ -128,66 +143,76 @@ def tile_moe_pre_lin_bias_kernel(tc, xT, w_words, w_scales, b, gate, offs, out):
             for le in range(EG):
                 e = g * EG + le
                 nc.scalar.activation(
-                    ys[c][:, e * C:(e + 1) * C], acc[:, le * C:(le + 1) * C], IDENT, bias=bias_of(c, e)
+                    ys[c][:, e * C:(e + 1) * C], acc[:, le * C:(le + 1) * C], IDENT, bias=bias[:, c, e:e + 1]
                 )
 
         def scatter(c, lo, hi):
             nc.vector.tensor_copy(windows[c][:].indirect(offsets[:, lo // 16:hi // 16]), ys[c][:, lo:hi])
 
         def store(c):
-            nc.sync.dma_start(out=out[c * P:(c + 1) * P, :], in_=windows[c][:, 0:T])
+            nc.sync.dma_start(out=out[c * P:(c + 1) * P, :], in_=windows[c][:])
 
         plane_words = w_planes[:].bitcast(I32)
         nc.vector.memset(plane_words, 0)
+        make_identity(nc, identity[:])
+        nc.gpsimd.memset(gate_rows[:], 0.0)
 
         load_plane(0)
         nc.sync.dma_start(offsets[:], offs)
-        for lo, hi in OPENING:
-            nc.sync.dma_start(out=gate_all[:, lo:hi], in_=gate[0:P, lo:hi])
-        for i in range(1, PASSES * PACK):
-            if i == PACK:
-                nc.sync.dma_start(out=gate_head[:], in_=gate[P:2 * P, 0:GROUP])
-            load_plane(i)
+        load_plane(1)
         for q in range(4):
             for a in range(PASSES):
                 nc.sync.dma_start(
                     out=plane_words[32 * q + 4 * a:32 * q + 4 * a + 4, :, :],
                     in_=w_scales[:, a, 4 * q:4 * q + 4, :].rearrange("e r n -> r e n").bitcast(I32),
                 )
-        nc.sync.dma_start(out=bias_head[:], in_=b[0:P, 0:EG])
         nc.sync.dma_start(out=bias[:], in_=b.rearrange("(c p) e -> p c e", p=P))
-        for g in range(GROUPS):
-            nc.sync.dma_start(
-                out=w_codes[g][:].bitcast(I32),
-                in_=w_words[g * EG:(g + 1) * EG].rearrange("e a p n r -> p (e a) (n r)").bitcast(I32),
-            )
+        load_plane(2)
+        nc.sync.dma_start(out=gate_rows[0:E, :], in_=gate[0, :].rearrange("(e c) -> e c", c=C))
+        nc.sync.dma_start(out=gate_head[:], in_=gate[0:P, 0:GROUP])
+        load_plane(3)
+        load_weights(w_head, 0, 0, P)
+        for i in range(PACK, PASSES * PACK):
+            load_plane(i)
+        nc.sync.dma_start(out=gate_rest[:], in_=gate[0:P, GROUP:S])
+        load_weights(w_codes[1], 1, 0, N)
+        load_weights(w_codes[0], 0, P, N)
+        load_weights(w_codes[2], 2, 0, N)
 
-        for lo, hi in OPENING:
-            gather(0, lo, hi)
-        for t in range(1, PACK):
-            gather(t, 0, S)
-        interleave(0, 0)
-        interleave(0, 1)
-        gather_second(0)
-        gather_second(1)
+        turn_gate()
+        for j in range(PACK):
+            nc.vector.tensor_copy(first[:, j, :], planes[j][:].indirect(offsets[:]))
+        scale_first(0, 0)
+        scale_first(0, 1)
+        for t in range(PACK):
+            gather_second(t, second_head, gate_head[:], 0, GROUP)
+        interleave(0)
+        for g in range(1, GROUPS):
+            scale_first(g, 0)
+            scale_first(g, 1)
+        for t in range(PACK - 1):
+            gather_second(t, second_rest, gate_rest[:], GROUP, S)
         quantize(0)
+        gather_second(PACK - 1, second_rest, gate_rest[:], GROUP, S)
         multiply(0, 0)
-        interleave(0, 2)
-        gather_second(2)
-        quantize(1)
+        interleave(1)
         scatter(0, 0, GROUP)
-        quantize(2)
+        quantize(1)
         multiply(0, 1)
-        multiply(1, 1)
-        scatter(1, 0, 2 * GROUP)
+        interleave(2)
+        scatter(1, 0, GROUP)
+        quantize(2)
+        multiply(0, 2)
+        multiply(1, 2)
+        scatter(2, 0, 2 * GROUP)
         multiply(1, 0)
         multiply(2, 0)
         scatter(0, GROUP, S)
         store(0)
+        multiply(1, 1)
         multiply(2, 1)
-        scatter(1, 2 * GROUP, S)
+        scatter(1, GROUP, S)
         store(1)
-        for g in range(GROUPS):
-            multiply(g, 2)
-        scatter(2, 0, S)
+        multiply(2, 2)
+        scatter(2, 2 * GROUP, S)
         store(2)

@@ -27,38 +27,54 @@ GROUP = 512
 GROUPS = S // GROUP
 EG = GROUP // C
 WIDE = 2048
+HEAD = 2 * GROUP
+ROWS = EG * PASSES
+STAGED_BYTES = PACK * P * 2
+ROUNDED_BYTES = PASSES * GROUP * PACK * 2
 
 
 def tile_moe_pre_lin_bias_kernel(tc, xT, w_words, w_scales, b, gate, offs, out):
     nc = tc.nc
     with ExitStack() as ctx:
         keep = ctx.enter_context(tc.tile_pool(name="keep", bufs=1))
+        shared = ctx.enter_context(tc.tile_pool(name="shared", bufs=1))
         stage = ctx.enter_context(tc.tile_pool(name="stage", bufs=3))
-        turn_psum = ctx.enter_context(tc.psum_pool(name="turn_psum", bufs=4))
+        turn_psum = ctx.enter_context(tc.psum_pool(name="turn_psum", bufs=3))
         back_psum = ctx.enter_context(tc.psum_pool(name="back_psum", bufs=2))
-        acc_psum = ctx.enter_context(tc.psum_pool(name="acc_psum", bufs=2))
+        acc_psum = ctx.enter_context(tc.psum_pool(name="acc_psum", bufs=3))
 
         offsets = keep.tile([P, S // 16], U16, name="offsets")
         planes = [keep.tile([P, WIDE if i < PACK else T], F32, name="plane%d" % i) for i in range(PASSES * PACK)]
         identity = keep.tile([P, P], F32, name="identity")
-        gate_head = keep.tile([P, GROUP], F32, name="gate_head")
-        gate_rest = keep.tile([P, S - GROUP], F32, name="gate_rest")
+        gate_head = keep.tile([P, HEAD], F32, name="gate_head")
+        gate_rest = keep.tile([P, S - HEAD], F32, name="gate_rest")
         gate_rows = keep.tile([P, C], F32, name="gate_rows")
         gate_cols = keep.tile([P, E], F32, name="gate_cols")
         first = keep.tile([P, PACK, S], F32, name="first")
-        second_head = keep.tile([P, PACK, GROUP], F32, name="second_head")
-        second_rest = keep.tile([P, PACK, S - GROUP], F32, name="second_rest")
-        rounded = [keep.tile([P, PASSES, GROUP, PACK], BF16, name="rounded%d" % g, align_bytes=64) for g in range(GROUPS)]
+        second_head = keep.tile([P, PACK, HEAD], F32, name="second_head")
+        second_rest = keep.tile([P, PACK, S - HEAD], F32, name="second_rest")
+        rounded = [keep.tile([P, PASSES, GROUP, PACK], BF16, name="rounded%d" % g, align_bytes=64) for g in range(GROUPS - 1)]
+        rounded.append(shared.tile([P, PASSES, GROUP, PACK], BF16, name="rounded_last", align_bytes=64, offset=0))
+        staged_last = [
+            shared.tile([P, 2, P, 2], BF16, name="staged_last%d" % le, offset=ROUNDED_BYTES + le * STAGED_BYTES)
+            for le in range(EG)
+        ]
         x_codes = [keep.tile([P, PASSES, GROUP], U32, name="x_codes%d" % g, align_bytes=64) for g in range(GROUPS)]
         x_scales = [keep.tile([P, PASSES, GROUP], U8, name="x_scales%d" % g, align_bytes=64) for g in range(GROUPS)]
-        w_head = keep.tile([P, EG * PASSES, P], U32, name="w_head", align_bytes=64)
-        w_codes = [
-            keep.tile([P, EG * PASSES, N - P if g == 0 else N], U32, name="w_codes%d" % g, align_bytes=64)
-            for g in range(GROUPS)
+        w_early = shared.tile([P, ROWS * N], U32, name="w_early", align_bytes=64, offset=0)
+        w_late = keep.tile([P, ROWS * N], U32, name="w_late", align_bytes=64)
+        w_last = keep.tile([P, ROWS * N], U32, name="w_last", align_bytes=64)
+        w_parts = [
+            (0, 0, 2, w_early[:, 0:ROWS * 2 * P]),
+            (1, 0, 1, w_early[:, ROWS * 2 * P:ROWS * N]),
+            (1, 1, 3, w_late[:, 0:ROWS * 2 * P]),
+            (0, 2, 3, w_late[:, ROWS * 2 * P:ROWS * N]),
+            (2, 0, 3, w_last[:]),
         ]
         w_planes = keep.tile([P, E, N], U8, name="w_planes", align_bytes=64)
         bias = keep.tile([P, NT, E], F32, name="bias")
-        ys = [keep.tile([P, S], F32, name="y%d" % c) for c in range(NT)]
+        ys = [keep.tile([P, S], F32, name="y%d" % c) for c in range(NT - 1)]
+        ys.append(shared.tile([P, S], F32, name="y_last", offset=ROUNDED_BYTES))
         windows = [keep.tile([P, T], F32, name="window%d" % c) for c in range(NT)]
 
         late_rows = xT[P * PACK:K, :].rearrange("(p t) c -> t p c", t=PACK)
@@ -67,14 +83,18 @@ def tile_moe_pre_lin_bias_kernel(tc, xT, w_words, w_scales, b, gate, offs, out):
             rows = xT[i * P:(i + 1) * P, :] if i < PACK else late_rows[i - PACK]
             nc.sync.dma_start(out=planes[i][:, 0:T], in_=rows)
 
-        def load_weights(tile, g, lo, hi):
-            words = w_words[g * EG:(g + 1) * EG].rearrange("e a p n r -> p (e a) (n r)")
-            nc.sync.dma_start(out=tile[:].bitcast(I32), in_=words[:, :, lo * PACK:hi * PACK].bitcast(I32))
+        def load_weights(part):
+            g, lo, hi, words = part
+            source = w_words[g * EG:(g + 1) * EG].rearrange("e a p n r -> p (e a) (n r)")
+            nc.sync.dma_start(
+                out=words.bitcast(I32).rearrange("p (r n) -> p r n", r=ROWS),
+                in_=source[:, :, lo * P * PACK:hi * P * PACK].bitcast(I32),
+            )
 
         def turn_gate():
-            bank = turn_psum.tile([P, PACK, P], F32, name="turned")
-            nc.tensor.transpose(bank[:, 0, :], gate_rows[:], identity[:])
-            nc.scalar.copy(gate_cols[:], bank[:, 0, 0:E])
+            bank = acc_psum.tile([P, GROUP], F32, name="acc")
+            nc.tensor.transpose(bank[:, 0:P], gate_rows[:], identity[:])
+            nc.scalar.copy(gate_cols[:], bank[:, 0:E])
 
         def scale_first(g, pair):
             back = back_psum.tile([P, 2, 2, C], F32, name="back")
@@ -84,7 +104,7 @@ def tile_moe_pre_lin_bias_kernel(tc, xT, w_words, w_scales, b, gate, offs, out):
                 bank = turn_psum.tile([P, PACK, P], F32, name="turned")
                 for j in range(PACK):
                     nc.tensor.transpose(bank[:, j, :], first[:, j, e * C:(e + 1) * C], identity[:])
-                staged = stage.tile([P, 2, P, 2], BF16, name="staged")
+                staged = staged_last[le] if g == GROUPS - 1 else stage.tile([P, 2, P, 2], BF16, name="staged")
                 nc.scalar.activation(
                     staged[:],
                     bank[:].rearrange("s j (q u v) -> s u (j q) v", u=2, v=2),
@@ -105,7 +125,7 @@ def tile_moe_pre_lin_bias_kernel(tc, xT, w_words, w_scales, b, gate, offs, out):
             )
 
         def interleave(g):
-            source = second_head[:] if g == 0 else second_rest[:, :, (g - 1) * GROUP:g * GROUP]
+            source = second_head[:, :, g * GROUP:(g + 1) * GROUP] if g * GROUP < HEAD else second_rest[:]
             nc.scalar.activation(
                 rounded[g][:, 1, :, :].rearrange("p (c i) t -> p c t i", i=4),
                 source.rearrange("p t (c i) -> p c t i", i=4),
@@ -120,15 +140,13 @@ def tile_moe_pre_lin_bias_kernel(tc, xT, w_words, w_scales, b, gate, offs, out):
             )
 
         def weights(g, c, row):
-            if g > 0:
-                return w_codes[g][:, row, c * P:(c + 1) * P]
-            if c == 0:
-                return w_head[:, row, :]
-            return w_codes[0][:, row, (c - 1) * P:c * P]
+            lo, hi, words = [part[1:] for part in w_parts if part[0] == g and part[1] <= c < part[2]][0]
+            start = (row * (hi - lo) + c - lo) * P
+            return words[:, start:start + P]
 
-        def multiply(g, c):
+        def multiply_experts(g, c, experts):
             acc = acc_psum.tile([P, GROUP], F32, name="acc")
-            for le in range(EG):
+            for le in experts:
                 slots = slice(le * C, (le + 1) * C)
                 for a in range(PASSES):
                     nc.tensor.matmul_mx(
@@ -140,11 +158,14 @@ def tile_moe_pre_lin_bias_kernel(tc, xT, w_words, w_scales, b, gate, offs, out):
                         start=(a == 0),
                         stop=(a == PASSES - 1),
                     )
-            for le in range(EG):
+            for le in experts:
                 e = g * EG + le
                 nc.scalar.activation(
                     ys[c][:, e * C:(e + 1) * C], acc[:, le * C:(le + 1) * C], IDENT, bias=bias[:, c, e:e + 1]
                 )
+
+        def multiply(g, c):
+            multiply_experts(g, c, range(EG))
 
         def scatter(c, lo, hi):
             nc.vector.tensor_copy(windows[c][:].indirect(offsets[:, lo // 16:hi // 16]), ys[c][:, lo:hi])
@@ -169,50 +190,50 @@ def tile_moe_pre_lin_bias_kernel(tc, xT, w_words, w_scales, b, gate, offs, out):
         nc.sync.dma_start(out=bias[:], in_=b.rearrange("(c p) e -> p c e", p=P))
         load_plane(2)
         nc.sync.dma_start(out=gate_rows[0:E, :], in_=gate[0, :].rearrange("(e c) -> e c", c=C))
-        nc.sync.dma_start(out=gate_head[:], in_=gate[0:P, 0:GROUP])
         load_plane(3)
-        load_weights(w_head, 0, 0, P)
+        nc.sync.dma_start(out=gate_head[:], in_=gate[0:P, 0:HEAD])
         for i in range(PACK, PASSES * PACK):
             load_plane(i)
-        nc.sync.dma_start(out=gate_rest[:], in_=gate[0:P, GROUP:S])
-        load_weights(w_codes[1], 1, 0, N)
-        load_weights(w_codes[0], 0, P, N)
-        load_weights(w_codes[2], 2, 0, N)
+        load_weights(w_parts[0])
+        nc.sync.dma_start(out=gate_rest[:], in_=gate[0:P, HEAD:S])
+        for part in w_parts[1:]:
+            load_weights(part)
 
         turn_gate()
         for j in range(PACK):
             nc.vector.tensor_copy(first[:, j, :], planes[j][:].indirect(offsets[:]))
-        scale_first(0, 0)
-        scale_first(0, 1)
-        for t in range(PACK):
-            gather_second(t, second_head, gate_head[:], 0, GROUP)
-        interleave(0)
-        for g in range(1, GROUPS):
+        for g in range(GROUPS - 1):
             scale_first(g, 0)
             scale_first(g, 1)
-        for t in range(PACK - 1):
-            gather_second(t, second_rest, gate_rest[:], GROUP, S)
-        quantize(0)
-        gather_second(PACK - 1, second_rest, gate_rest[:], GROUP, S)
-        multiply(0, 0)
+        for t in range(PACK):
+            gather_second(t, second_head, gate_head[:], 0, HEAD)
+        interleave(0)
         interleave(1)
-        scatter(0, 0, GROUP)
+        for t in range(PACK - 1):
+            gather_second(t, second_rest, gate_rest[:], HEAD, S)
+        quantize(0)
+        gather_second(PACK - 1, second_rest, gate_rest[:], HEAD, S)
         quantize(1)
-        multiply(0, 1)
-        interleave(2)
+        multiply_experts(0, 1, range(0, EG // 2))
+        multiply_experts(0, 1, range(EG // 2, EG))
         scatter(1, 0, GROUP)
+        multiply(0, 0)
+        multiply(1, 0)
+        scatter(0, 0, HEAD)
+        interleave(2)
+        scale_first(2, 0)
+        scale_first(2, 1)
         quantize(2)
         multiply(0, 2)
         multiply(1, 2)
-        scatter(2, 0, 2 * GROUP)
-        multiply(1, 0)
-        multiply(2, 0)
-        scatter(0, GROUP, S)
-        store(0)
+        scatter(2, 0, HEAD)
         multiply(1, 1)
         multiply(2, 1)
         scatter(1, GROUP, S)
         store(1)
+        multiply(2, 0)
+        scatter(0, HEAD, S)
+        store(0)
         multiply(2, 2)
-        scatter(2, 2 * GROUP, S)
+        scatter(2, HEAD, S)
         store(2)

@@ -178,9 +178,12 @@ def tile_moe_pre_lin_bias_kernel(tc, xT, w_words, w_scales, b, gate, offs, out):
         make_identity(nc, identity[:])
         nc.gpsimd.memset(gate_rows[:], 0.0)
 
-        load_plane(0)
         nc.sync.dma_start(offsets[:], offs)
+        nc.sync.dma_start(out=planes[0][:, 0:T // 2], in_=xT[0:P, 0:T // 2])
+        nc.scalar.dma_start(out=planes[0][:, T // 2:T], in_=xT[0:P, T // 2:T])
         load_plane(1)
+        load_plane(2)
+        load_plane(3)
         for q in range(4):
             for a in range(PASSES):
                 nc.sync.dma_start(
@@ -188,9 +191,7 @@ def tile_moe_pre_lin_bias_kernel(tc, xT, w_words, w_scales, b, gate, offs, out):
                     in_=w_scales[:, a, 4 * q:4 * q + 4, :].rearrange("e r n -> r e n").bitcast(I32),
                 )
         nc.sync.dma_start(out=bias[:], in_=b.rearrange("(c p) e -> p c e", p=P))
-        load_plane(2)
         nc.sync.dma_start(out=gate_rows[0:E, :], in_=gate[0, :].rearrange("(e c) -> e c", c=C))
-        load_plane(3)
         nc.sync.dma_start(out=gate_head[:], in_=gate[0:P, 0:HEAD])
         for i in range(PACK, PASSES * PACK):
             load_plane(i)
@@ -236,4 +237,5 @@ def tile_moe_pre_lin_bias_kernel(tc, xT, w_words, w_scales, b, gate, offs, out):
         store(0)
         multiply(2, 2)
         scatter(2, HEAD, S)
-        store(2)
+        nc.sync.dma_start(out=out[2 * P:N, 0:T // 2], in_=windows[2][:, 0:T // 2])
+        nc.scalar.dma_start(out=out[2 * P:N, T // 2:T], in_=windows[2][:, T // 2:T])

@@ -38,13 +38,15 @@ def tile_moe_pre_lin_bias_kernel(tc, xT, w_words, w_scales, b, gate, offs, out):
     with ExitStack() as ctx:
         keep = ctx.enter_context(tc.tile_pool(name="keep", bufs=1))
         shared = ctx.enter_context(tc.tile_pool(name="shared", bufs=1))
+        reused = ctx.enter_context(tc.tile_pool(name="reused", bufs=1))
         stage = ctx.enter_context(tc.tile_pool(name="stage", bufs=3))
         turn_psum = ctx.enter_context(tc.psum_pool(name="turn_psum", bufs=3))
         back_psum = ctx.enter_context(tc.psum_pool(name="back_psum", bufs=2))
         acc_psum = ctx.enter_context(tc.psum_pool(name="acc_psum", bufs=3))
 
         offsets = keep.tile([P, S // 16], U16, name="offsets")
-        planes = [keep.tile([P, WIDE if i < PACK else T], F32, name="plane%d" % i) for i in range(PASSES * PACK)]
+        planes = [keep.tile([P, WIDE], F32, name="plane%d" % i) for i in range(PACK)]
+        planes.extend(reused.tile([P, T], F32, name="plane%d" % (PACK + t), offset=t * T * 4) for t in range(PACK))
         identity = keep.tile([P, P], F32, name="identity")
         gate_head = keep.tile([P, HEAD], F32, name="gate_head")
         gate_rest = keep.tile([P, S - HEAD], F32, name="gate_rest")
@@ -53,7 +55,9 @@ def tile_moe_pre_lin_bias_kernel(tc, xT, w_words, w_scales, b, gate, offs, out):
         first = keep.tile([P, PACK, S], F32, name="first")
         second_head = keep.tile([P, PACK, HEAD], F32, name="second_head")
         second_rest = keep.tile([P, PACK, S - HEAD], F32, name="second_rest")
-        rounded = [keep.tile([P, PASSES, GROUP, PACK], BF16, name="rounded%d" % g, align_bytes=64) for g in range(GROUPS - 1)]
+        rounded = [
+            keep.tile([P, PASSES, GROUP, PACK], BF16, name="rounded%d" % g, align_bytes=64) for g in range(GROUPS - 1)
+        ]
         rounded.append(shared.tile([P, PASSES, GROUP, PACK], BF16, name="rounded_last", align_bytes=64, offset=0))
         staged_last = [
             shared.tile([P, 2, P, 2], BF16, name="staged_last%d" % le, offset=ROUNDED_BYTES + le * STAGED_BYTES)
@@ -62,8 +66,8 @@ def tile_moe_pre_lin_bias_kernel(tc, xT, w_words, w_scales, b, gate, offs, out):
         x_codes = [keep.tile([P, PASSES, GROUP], U32, name="x_codes%d" % g, align_bytes=64) for g in range(GROUPS)]
         x_scales = [keep.tile([P, PASSES, GROUP], U8, name="x_scales%d" % g, align_bytes=64) for g in range(GROUPS)]
         w_early = shared.tile([P, ROWS * N], U32, name="w_early", align_bytes=64, offset=0)
-        w_late = keep.tile([P, ROWS * N], U32, name="w_late", align_bytes=64)
-        w_last = keep.tile([P, ROWS * N], U32, name="w_last", align_bytes=64)
+        w_late = reused.tile([P, ROWS * N], U32, name="w_late", align_bytes=64, offset=0)
+        w_last = reused.tile([P, ROWS * N], U32, name="w_last", align_bytes=64, offset=ROWS * N * 4)
         w_parts = [
             (0, 0, 2, w_early[:, 0:ROWS * 2 * P]),
             (1, 0, 1, w_early[:, ROWS * 2 * P:ROWS * N]),
@@ -71,16 +75,16 @@ def tile_moe_pre_lin_bias_kernel(tc, xT, w_words, w_scales, b, gate, offs, out):
             (0, 2, 3, w_late[:, ROWS * 2 * P:ROWS * N]),
             (2, 0, 3, w_last[:]),
         ]
-        w_planes = keep.tile([P, E, N], U8, name="w_planes", align_bytes=64)
+        w_scale_rows = keep.tile([P, E, N], U8, name="w_scale_rows", align_bytes=64)
         bias = keep.tile([P, NT, E], F32, name="bias")
         ys = [keep.tile([P, S], F32, name="y%d" % c) for c in range(NT - 1)]
         ys.append(shared.tile([P, S], F32, name="y_last", offset=ROUNDED_BYTES))
         windows = [keep.tile([P, T], F32, name="window%d" % c) for c in range(NT)]
 
-        late_rows = xT[P * PACK:K, :].rearrange("(p t) c -> t p c", t=PACK)
+        second_rows = xT[P * PACK:K, :].rearrange("(p t) c -> t p c", t=PACK)
 
         def load_plane(i):
-            rows = xT[i * P:(i + 1) * P, :] if i < PACK else late_rows[i - PACK]
+            rows = xT[i * P:(i + 1) * P, :] if i < PACK else second_rows[i - PACK]
             nc.sync.dma_start(out=planes[i][:, 0:T], in_=rows)
 
         def load_weights(part):
@@ -101,19 +105,19 @@ def tile_moe_pre_lin_bias_kernel(tc, xT, w_words, w_scales, b, gate, offs, out):
             for h in range(2):
                 le = 2 * pair + h
                 e = g * EG + le
-                bank = turn_psum.tile([P, PACK, P], F32, name="turned")
+                turned = turn_psum.tile([P, PACK, P], F32, name="turned")
                 for j in range(PACK):
-                    nc.tensor.transpose(bank[:, j, :], first[:, j, e * C:(e + 1) * C], identity[:])
+                    nc.tensor.transpose(turned[:, j, :], first[:, j, e * C:(e + 1) * C], identity[:])
                 staged = staged_last[le] if g == GROUPS - 1 else stage.tile([P, 2, P, 2], BF16, name="staged")
                 nc.scalar.activation(
                     staged[:],
-                    bank[:].rearrange("s j (q u v) -> s u (j q) v", u=2, v=2),
+                    turned[:].rearrange("s j (q u v) -> s u (j q) v", u=2, v=2),
                     COPY,
                     scale=gate_cols[:, e:e + 1],
                 )
-                words = staged[:].rearrange("s u p v -> s (u p v)").bitcast(F32)
+                pairs = staged[:].rearrange("s u p v -> s (u p v)").bitcast(F32)
                 for u in range(2):
-                    nc.tensor.transpose(back[:, h, u, :], words[:, u * P:(u + 1) * P], identity[:])
+                    nc.tensor.transpose(back[:, h, u, :], pairs[:, u * P:(u + 1) * P], identity[:])
             target = rounded[g][:, 0, 2 * pair * C:(2 * pair + 2) * C, :].rearrange("p s t -> p (s t)").bitcast(F32)
             nc.scalar.copy(
                 target.rearrange("p (h s u) -> p h s u", h=2, u=2), back[:].rearrange("p h u s -> p h s u")
@@ -152,7 +156,7 @@ def tile_moe_pre_lin_bias_kernel(tc, xT, w_words, w_scales, b, gate, offs, out):
                     nc.tensor.matmul_mx(
                         out=acc[:, slots],
                         lhsT=weights(g, c, le * PASSES + a).bitcast(FP8X4),
-                        lhsT_scale=w_planes[4 * a:P, g * EG + le, c * P:(c + 1) * P],
+                        lhsT_scale=w_scale_rows[4 * a:P, g * EG + le, c * P:(c + 1) * P],
                         rhs=x_codes[g][:, a, slots].bitcast(FP8X4),
                         rhs_scale=x_scales[g][:, a, slots],
                         start=(a == 0),
@@ -173,22 +177,21 @@ def tile_moe_pre_lin_bias_kernel(tc, xT, w_words, w_scales, b, gate, offs, out):
         def store(c):
             nc.sync.dma_start(out=out[c * P:(c + 1) * P, :], in_=windows[c][:])
 
-        plane_words = w_planes[:].bitcast(I32)
-        nc.vector.memset(plane_words, 0)
+        scale_words = w_scale_rows[:].bitcast(I32)
+        nc.vector.memset(scale_words, 0)
         make_identity(nc, identity[:])
         nc.gpsimd.memset(gate_rows[:], 0.0)
 
         nc.sync.dma_start(offsets[:], offs)
         nc.sync.dma_start(out=planes[0][:, 0:T // 2], in_=xT[0:P, 0:T // 2])
         nc.scalar.dma_start(out=planes[0][:, T // 2:T], in_=xT[0:P, T // 2:T])
-        load_plane(1)
-        load_plane(2)
-        load_plane(3)
-        for q in range(4):
+        for i in range(1, PACK):
+            load_plane(i)
+        for quad in range(4):
             for a in range(PASSES):
                 nc.sync.dma_start(
-                    out=plane_words[32 * q + 4 * a:32 * q + 4 * a + 4, :, :],
-                    in_=w_scales[:, a, 4 * q:4 * q + 4, :].rearrange("e r n -> r e n").bitcast(I32),
+                    out=scale_words[32 * quad + 4 * a:32 * quad + 4 * a + 4, :, :],
+                    in_=w_scales[:, a, 4 * quad:4 * quad + 4, :].rearrange("e r n -> r e n").bitcast(I32),
                 )
         nc.sync.dma_start(out=bias[:], in_=b.rearrange("(c p) e -> p c e", p=P))
         nc.sync.dma_start(out=gate_rows[0:E, :], in_=gate[0, :].rearrange("(e c) -> e c", c=C))
@@ -197,8 +200,7 @@ def tile_moe_pre_lin_bias_kernel(tc, xT, w_words, w_scales, b, gate, offs, out):
             load_plane(i)
         load_weights(w_parts[0])
         nc.sync.dma_start(out=gate_rest[:], in_=gate[0:P, HEAD:S])
-        for part in w_parts[1:]:
-            load_weights(part)
+        load_weights(w_parts[1])
 
         turn_gate()
         for j in range(PACK):
@@ -214,6 +216,8 @@ def tile_moe_pre_lin_bias_kernel(tc, xT, w_words, w_scales, b, gate, offs, out):
             gather_second(t, second_rest, gate_rest[:], HEAD, S)
         quantize(0)
         gather_second(PACK - 1, second_rest, gate_rest[:], HEAD, S)
+        for part in w_parts[2:]:
+            load_weights(part)
         quantize(1)
         multiply_experts(0, 1, range(0, EG // 2))
         multiply_experts(0, 1, range(EG // 2, EG))
@@ -228,14 +232,14 @@ def tile_moe_pre_lin_bias_kernel(tc, xT, w_words, w_scales, b, gate, offs, out):
         multiply(0, 2)
         multiply(1, 2)
         scatter(2, 0, HEAD)
-        multiply(1, 1)
-        multiply(2, 1)
-        scatter(1, GROUP, S)
-        store(1)
         multiply(2, 0)
         scatter(0, HEAD, S)
         store(0)
         multiply(2, 2)
         scatter(2, HEAD, S)
-        nc.sync.dma_start(out=out[2 * P:N, 0:T // 2], in_=windows[2][:, 0:T // 2])
-        nc.scalar.dma_start(out=out[2 * P:N, T // 2:T], in_=windows[2][:, T // 2:T])
+        store(2)
+        multiply(1, 1)
+        multiply(2, 1)
+        scatter(1, GROUP, S)
+        nc.sync.dma_start(out=out[P:2 * P, 0:T // 2], in_=windows[1][:, 0:T // 2])
+        nc.scalar.dma_start(out=out[P:2 * P, T // 2:T], in_=windows[1][:, T // 2:T])

@@ -28,7 +28,7 @@ GROUPS = S // GROUP
 EG = GROUP // C
 WIDE = 2048
 HEAD = 2 * GROUP
-ROWS = EG * PASSES
+MATRICES = EG * PASSES
 STAGED_BYTES = PACK * P * 2
 ROUNDED_BYTES = PASSES * GROUP * PACK * 2
 
@@ -65,14 +65,14 @@ def tile_moe_pre_lin_bias_kernel(tc, xT, w_words, w_scales, b, gate, offs, out):
         ]
         x_codes = [keep.tile([P, PASSES, GROUP], U32, name="x_codes%d" % g, align_bytes=64) for g in range(GROUPS)]
         x_scales = [keep.tile([P, PASSES, GROUP], U8, name="x_scales%d" % g, align_bytes=64) for g in range(GROUPS)]
-        w_early = shared.tile([P, ROWS * N], U32, name="w_early", align_bytes=64, offset=0)
-        w_late = reused.tile([P, ROWS * N], U32, name="w_late", align_bytes=64, offset=0)
-        w_last = reused.tile([P, ROWS * N], U32, name="w_last", align_bytes=64, offset=ROWS * N * 4)
+        w_early = shared.tile([P, MATRICES * N], U32, name="w_early", align_bytes=64, offset=0)
+        w_late = reused.tile([P, MATRICES * N], U32, name="w_late", align_bytes=64, offset=0)
+        w_last = reused.tile([P, MATRICES * N], U32, name="w_last", align_bytes=64, offset=MATRICES * N * 4)
         w_parts = [
-            (0, 0, 2, w_early[:, 0:ROWS * 2 * P]),
-            (1, 0, 1, w_early[:, ROWS * 2 * P:ROWS * N]),
-            (1, 1, 3, w_late[:, 0:ROWS * 2 * P]),
-            (0, 2, 3, w_late[:, ROWS * 2 * P:ROWS * N]),
+            (0, 0, 2, w_early[:, 0:MATRICES * 2 * P]),
+            (1, 0, 1, w_early[:, MATRICES * 2 * P:MATRICES * N]),
+            (1, 1, 3, w_late[:, 0:MATRICES * 2 * P]),
+            (0, 2, 3, w_late[:, MATRICES * 2 * P:MATRICES * N]),
             (2, 0, 3, w_last[:]),
         ]
         w_scale_rows = keep.tile([P, E, N], U8, name="w_scale_rows", align_bytes=64)
@@ -81,18 +81,18 @@ def tile_moe_pre_lin_bias_kernel(tc, xT, w_words, w_scales, b, gate, offs, out):
         ys.append(shared.tile([P, S], F32, name="y_last", offset=ROUNDED_BYTES))
         windows = [keep.tile([P, T], F32, name="window%d" % c) for c in range(NT)]
 
-        second_rows = xT[P * PACK:K, :].rearrange("(p t) c -> t p c", t=PACK)
+        second_rows = xT[P * PACK:K, :].rearrange("(p t) token -> t p token", t=PACK)
 
         def load_plane(i):
             rows = xT[i * P:(i + 1) * P, :] if i < PACK else second_rows[i - PACK]
             nc.sync.dma_start(out=planes[i][:, 0:T], in_=rows)
 
         def load_weights(part):
-            g, lo, hi, words = part
-            source = w_words[g * EG:(g + 1) * EG].rearrange("e a p n r -> p (e a) (n r)")
+            g, c_first, c_end, words = part
+            source = w_words[g * EG:(g + 1) * EG].rearrange("e a p n t -> p (e a) (n t)")
             nc.sync.dma_start(
-                out=words.bitcast(I32).rearrange("p (r n) -> p r n", r=ROWS),
-                in_=source[:, :, lo * P * PACK:hi * P * PACK].bitcast(I32),
+                out=words.bitcast(I32).rearrange("p (m n) -> p m n", m=MATRICES),
+                in_=source[:, :, c_first * P * PACK:c_end * P * PACK].bitcast(I32),
             )
 
         def turn_gate():
@@ -100,10 +100,10 @@ def tile_moe_pre_lin_bias_kernel(tc, xT, w_words, w_scales, b, gate, offs, out):
             nc.tensor.transpose(bank[:, 0:P], gate_rows[:], identity[:])
             nc.scalar.copy(gate_cols[:], bank[:, 0:E])
 
-        def scale_first(g, pair):
+        def scale_first(g, half):
             back = back_psum.tile([P, 2, 2, C], F32, name="back")
             for h in range(2):
-                le = 2 * pair + h
+                le = 2 * half + h
                 e = g * EG + le
                 turned = turn_psum.tile([P, PACK, P], F32, name="turned")
                 for j in range(PACK):
@@ -111,14 +111,14 @@ def tile_moe_pre_lin_bias_kernel(tc, xT, w_words, w_scales, b, gate, offs, out):
                 staged = staged_last[le] if g == GROUPS - 1 else stage.tile([P, 2, P, 2], BF16, name="staged")
                 nc.scalar.activation(
                     staged[:],
-                    turned[:].rearrange("s j (q u v) -> s u (j q) v", u=2, v=2),
+                    turned[:].rearrange("s j (w u v) -> s u (j w) v", u=2, v=2),
                     COPY,
                     scale=gate_cols[:, e:e + 1],
                 )
                 pairs = staged[:].rearrange("s u p v -> s (u p v)").bitcast(F32)
                 for u in range(2):
                     nc.tensor.transpose(back[:, h, u, :], pairs[:, u * P:(u + 1) * P], identity[:])
-            target = rounded[g][:, 0, 2 * pair * C:(2 * pair + 2) * C, :].rearrange("p s t -> p (s t)").bitcast(F32)
+            target = rounded[g][:, 0, 2 * half * C:(2 * half + 2) * C, :].rearrange("p s t -> p (s t)").bitcast(F32)
             nc.scalar.copy(
                 target.rearrange("p (h s u) -> p h s u", h=2, u=2), back[:].rearrange("p h u s -> p h s u")
             )
@@ -131,8 +131,8 @@ def tile_moe_pre_lin_bias_kernel(tc, xT, w_words, w_scales, b, gate, offs, out):
         def interleave(g):
             source = second_head[:, :, g * GROUP:(g + 1) * GROUP] if g * GROUP < HEAD else second_rest[:]
             nc.scalar.activation(
-                rounded[g][:, 1, :, :].rearrange("p (c i) t -> p c t i", i=4),
-                source.rearrange("p t (c i) -> p c t i", i=4),
+                rounded[g][:, 1, :, :].rearrange("p (line i) t -> p line t i", i=4),
+                source.rearrange("p t (line i) -> p line t i", i=4),
                 COPY,
             )
 
@@ -143,9 +143,9 @@ def tile_moe_pre_lin_bias_kernel(tc, xT, w_words, w_scales, b, gate, offs, out):
                 in_=rounded[g][:].rearrange("p a s t -> p (a s t)"),
             )
 
-        def weights(g, c, row):
-            lo, hi, words = [part[1:] for part in w_parts if part[0] == g and part[1] <= c < part[2]][0]
-            start = (row * (hi - lo) + c - lo) * P
+        def weights(g, c, matrix):
+            c_first, c_end, words = [part[1:] for part in w_parts if part[0] == g and part[1] <= c < part[2]][0]
+            start = (matrix * (c_end - c_first) + c - c_first) * P
             return words[:, start:start + P]
 
         def multiply_experts(g, c, experts):
@@ -194,7 +194,7 @@ def tile_moe_pre_lin_bias_kernel(tc, xT, w_words, w_scales, b, gate, offs, out):
                     in_=w_scales[:, a, 4 * quad:4 * quad + 4, :].rearrange("e r n -> r e n").bitcast(I32),
                 )
         nc.sync.dma_start(out=bias[:], in_=b.rearrange("(c p) e -> p c e", p=P))
-        nc.sync.dma_start(out=gate_rows[0:E, :], in_=gate[0, :].rearrange("(e c) -> e c", c=C))
+        nc.sync.dma_start(out=gate_rows[0:E, :], in_=gate[0, :].rearrange("(e place) -> e place", place=C))
         nc.sync.dma_start(out=gate_head[:], in_=gate[0:P, 0:HEAD])
         for i in range(PACK, PASSES * PACK):
             load_plane(i)
@@ -219,11 +219,12 @@ def tile_moe_pre_lin_bias_kernel(tc, xT, w_words, w_scales, b, gate, offs, out):
         for part in w_parts[2:]:
             load_weights(part)
         quantize(1)
-        multiply_experts(0, 1, range(0, EG // 2))
-        multiply_experts(0, 1, range(EG // 2, EG))
+        for le in range(EG):
+            multiply_experts(0, 1, [le])
         scatter(1, 0, GROUP)
         multiply(0, 0)
-        multiply(1, 0)
+        multiply_experts(1, 0, range(0, EG // 2))
+        multiply_experts(1, 0, range(EG // 2, EG))
         scatter(0, 0, HEAD)
         interleave(2)
         scale_first(2, 0)

@@ -26,11 +26,12 @@ NT = N // P
 GROUP = 512
 GROUPS = S // GROUP
 EG = GROUP // C
+REST = S - GROUP
 WIDE = 2048
-HEAD = 2 * GROUP
+ROOMY = T + 16
+WHOLE = PACK - 1
 MATRICES = EG * PASSES
-STAGED_BYTES = PACK * P * 2
-ROUNDED_BYTES = PASSES * GROUP * PACK * 2
+HEAD_AT = PACK * S - S - PACK * GROUP
 
 
 def tile_moe_pre_lin_bias_kernel(tc, xT, w_words, w_scales, b, gate, offs, out):
@@ -38,54 +39,56 @@ def tile_moe_pre_lin_bias_kernel(tc, xT, w_words, w_scales, b, gate, offs, out):
     with ExitStack() as ctx:
         keep = ctx.enter_context(tc.tile_pool(name="keep", bufs=1))
         shared = ctx.enter_context(tc.tile_pool(name="shared", bufs=1))
-        reused = ctx.enter_context(tc.tile_pool(name="reused", bufs=1))
-        stage = ctx.enter_context(tc.tile_pool(name="stage", bufs=3))
+        stage = ctx.enter_context(tc.tile_pool(name="stage", bufs=4))
         turn_psum = ctx.enter_context(tc.psum_pool(name="turn_psum", bufs=3))
         back_psum = ctx.enter_context(tc.psum_pool(name="back_psum", bufs=2))
         acc_psum = ctx.enter_context(tc.psum_pool(name="acc_psum", bufs=3))
 
         offsets = keep.tile([P, S // 16], U16, name="offsets")
         planes = [keep.tile([P, WIDE], F32, name="plane%d" % i) for i in range(PACK)]
-        planes.extend(reused.tile([P, T], F32, name="plane%d" % (PACK + t), offset=t * T * 4) for t in range(PACK))
+        planes.extend(keep.tile([P, ROOMY if t == WHOLE else T], F32, name="plane%d" % (PACK + t)) for t in range(PACK))
         identity = keep.tile([P, P], F32, name="identity")
-        gate_head = keep.tile([P, HEAD], F32, name="gate_head")
-        gate_rest = keep.tile([P, S - HEAD], F32, name="gate_rest")
+        gates = keep.tile([P, S], F32, name="gates")
         gate_rows = keep.tile([P, C], F32, name="gate_rows")
         gate_cols = keep.tile([P, E], F32, name="gate_cols")
         first = keep.tile([P, PACK, S], F32, name="first")
-        second_head = keep.tile([P, PACK, HEAD], F32, name="second_head")
-        second_rest = keep.tile([P, PACK, S - HEAD], F32, name="second_rest")
-        rounded = [
-            keep.tile([P, PASSES, GROUP, PACK], BF16, name="rounded%d" % g, align_bytes=64) for g in range(GROUPS - 1)
-        ]
-        rounded.append(shared.tile([P, PASSES, GROUP, PACK], BF16, name="rounded_last", align_bytes=64, offset=0))
-        staged_last = [
-            shared.tile([P, 2, P, 2], BF16, name="staged_last%d" % le, offset=ROUNDED_BYTES + le * STAGED_BYTES)
-            for le in range(EG)
-        ]
-        x_codes = [keep.tile([P, PASSES, GROUP], U32, name="x_codes%d" % g, align_bytes=64) for g in range(GROUPS)]
-        x_scales = [keep.tile([P, PASSES, GROUP], U8, name="x_scales%d" % g, align_bytes=64) for g in range(GROUPS)]
-        w_early = shared.tile([P, MATRICES * N], U32, name="w_early", align_bytes=64, offset=0)
-        w_late = reused.tile([P, MATRICES * N], U32, name="w_late", align_bytes=64, offset=0)
-        w_last = reused.tile([P, MATRICES * N], U32, name="w_last", align_bytes=64, offset=MATRICES * N * 4)
-        w_parts = [
-            (0, 0, 2, w_early[:, 0:MATRICES * 2 * P]),
-            (1, 0, 1, w_early[:, MATRICES * 2 * P:MATRICES * N]),
-            (1, 1, 3, w_late[:, 0:MATRICES * 2 * P]),
-            (0, 2, 3, w_late[:, MATRICES * 2 * P:MATRICES * N]),
-            (2, 0, 3, w_last[:]),
-        ]
+        second = keep.tile([P, PACK * S], F32, name="second")
+        second_head = second[:, HEAD_AT:HEAD_AT + PACK * GROUP].rearrange("p (t s) -> p t s", t=PACK)
+        second_rest = second[:].rearrange("p (t s) -> p t s", t=PACK)[:, :, 0:REST]
+        low = [keep.tile([P, P], F32, name="low%d" % e) for e in range(E)]
+        rounded_head = keep.tile([P, PASSES, GROUP, PACK], BF16, name="rounded_head", align_bytes=64)
+        rounded_rest = keep.tile([P, REST, PACK], BF16, name="rounded_rest", align_bytes=64)
+        w_first = shared.tile([P, MATRICES * P], U32, name="w_first", align_bytes=64, offset=0)
+        rounded_mid = shared.tile([P, GROUP, PACK], BF16, name="rounded_mid", align_bytes=64, offset=0)
+        bias_second = shared.tile([P, EG], F32, name="bias_second", offset=MATRICES * P * 4)
+        rounded_last = shared.tile([P, GROUP, PACK], BF16, name="rounded_last", align_bytes=64, offset=MATRICES * P * 4)
+        calls = []
+        for name, tile, width in (
+            ("head", rounded_head[:].rearrange("p a s t -> p (a s t)"), PASSES * GROUP),
+            ("rest", rounded_rest[:].rearrange("p s t -> p (s t)"), REST),
+            ("mid", rounded_mid[:].rearrange("p s t -> p (s t)"), GROUP),
+            ("last", rounded_last[:].rearrange("p s t -> p (s t)"), GROUP),
+        ):
+            codes = keep.tile([P, width], U32, name="codes_" + name, align_bytes=64)
+            scales = keep.tile([P, width], U8, name="scales_" + name, align_bytes=64)
+            calls.append((tile, codes, scales))
+        w_head = keep.tile([P, MATRICES * (N - P)], U32, name="w_head", align_bytes=64)
+        w_mid = keep.tile([P, MATRICES * N], U32, name="w_mid", align_bytes=64)
+        w_last = keep.tile([P, MATRICES * N], U32, name="w_last", align_bytes=64)
+        w_parts = [(0, 0, 1, w_first[:]), (0, 1, NT, w_head[:]), (1, 0, NT, w_mid[:]), (2, 0, NT, w_last[:])]
         w_scale_rows = keep.tile([P, E, N], U8, name="w_scale_rows", align_bytes=64)
-        bias = keep.tile([P, NT, E], F32, name="bias")
-        ys = [keep.tile([P, S], F32, name="y%d" % c) for c in range(NT - 1)]
-        ys.append(shared.tile([P, S], F32, name="y_last", offset=ROUNDED_BYTES))
+        bias_outer = keep.tile([P, 2, EG], F32, name="bias_outer")
+        bias_head = [bias_outer[:, 0, :], bias_second[:], bias_outer[:, 1, :]]
+        bias_rest = keep.tile([P, NT, E - EG], F32, name="bias_rest")
+        y_first = keep.tile([P, GROUP], F32, name="y_first")
+        y_head = [y_first[:], second[:, 0:GROUP], second[:, GROUP:2 * GROUP]]
+        y_rest = [keep.tile([P, REST], F32, name="y_rest%d" % c) for c in range(NT)]
         windows = [keep.tile([P, T], F32, name="window%d" % c) for c in range(NT)]
 
-        second_rows = xT[P * PACK:K, :].rearrange("(p t) token -> t p token", t=PACK)
+        rows = xT.rearrange("(a p t) token -> a t p token", a=PASSES, t=PACK)
 
-        def load_plane(i):
-            rows = xT[i * P:(i + 1) * P, :] if i < PACK else second_rows[i - PACK]
-            nc.sync.dma_start(out=planes[i][:, 0:T], in_=rows)
+        def load_plane(a, t):
+            nc.sync.dma_start(out=planes[a * PACK + t][:, 0:T], in_=rows[a, t])
 
         def load_weights(part):
             g, c_first, c_end, words = part
@@ -100,82 +103,97 @@ def tile_moe_pre_lin_bias_kernel(tc, xT, w_words, w_scales, b, gate, offs, out):
             nc.tensor.transpose(bank[:, 0:P], gate_rows[:], identity[:])
             nc.scalar.copy(gate_cols[:], bank[:, 0:E])
 
-        def scale_first(g, half):
-            back = back_psum.tile([P, 2, 2, C], F32, name="back")
+        def scale_pairs(u, e0, targets):
+            turned = turn_psum.tile([P, 2, 2, P], F32, name="turned")
             for h in range(2):
-                le = 2 * half + h
-                e = g * EG + le
-                turned = turn_psum.tile([P, PACK, P], F32, name="turned")
-                for j in range(PACK):
-                    nc.tensor.transpose(turned[:, j, :], first[:, j, e * C:(e + 1) * C], identity[:])
-                staged = staged_last[le] if g == GROUPS - 1 else stage.tile([P, 2, P, 2], BF16, name="staged")
+                e = e0 + h
+                for v in range(2):
+                    nc.tensor.transpose(turned[:, h, v, :], first[:, 2 * u + v, e * C:(e + 1) * C], identity[:])
+            for h in range(2):
+                e = e0 + h
                 nc.scalar.activation(
-                    staged[:],
-                    turned[:].rearrange("s j (w u v) -> s u (j w) v", u=2, v=2),
+                    targets[h].bitcast(BF16).rearrange("s (line i v) -> s line v i", i=4, v=2),
+                    turned[:, h, :, :].rearrange("s v (line i) -> s line v i", i=4),
                     COPY,
                     scale=gate_cols[:, e:e + 1],
                 )
-                pairs = staged[:].rearrange("s u p v -> s (u p v)").bitcast(F32)
-                for u in range(2):
-                    nc.tensor.transpose(back[:, h, u, :], pairs[:, u * P:(u + 1) * P], identity[:])
-            target = rounded[g][:, 0, 2 * half * C:(2 * half + 2) * C, :].rearrange("p s t -> p (s t)").bitcast(F32)
+
+        def finish_first(e0):
+            if e0 < E - EG:
+                high = [stage.tile([P, P], F32, name="high")[:] for h in range(2)]
+            else:
+                at = HEAD_AT + (e0 - (E - EG)) * P
+                high = [second[:, at + h * P:at + (h + 1) * P] for h in range(2)]
+            scale_pairs(1, e0, high)
+            back = back_psum.tile([P, 2, 2, C], F32, name="back")
+            for h in range(2):
+                nc.tensor.transpose(back[:, h, 0, :], low[e0 + h][:], identity[:])
+                nc.tensor.transpose(back[:, h, 1, :], high[h], identity[:])
+            if e0 < EG:
+                target = rounded_head[:, 0, e0 * C:(e0 + 2) * C, :]
+            else:
+                target = rounded_rest[:, (e0 - EG) * C:(e0 - EG + 2) * C, :]
+            target = target.rearrange("p s t -> p (s t)").bitcast(F32)
             nc.scalar.copy(
                 target.rearrange("p (h s u) -> p h s u", h=2, u=2), back[:].rearrange("p h u s -> p h s u")
             )
 
-        def gather_second(t, tile, gates, lo, hi):
+        def gather_second(t, target, lo, hi):
             nc.vector.tensor_tensor(
-                tile[:, t, :], planes[PACK + t][:].indirect(offsets[:, lo // 16:hi // 16]), gates, MULT
+                target, planes[PACK + t][:].indirect(offsets[:, lo // 16:hi // 16]), gates[:, lo:hi], MULT
             )
 
-        def interleave(g):
-            source = second_head[:, :, g * GROUP:(g + 1) * GROUP] if g * GROUP < HEAD else second_rest[:]
+        def interleave(target, source):
             nc.scalar.activation(
-                rounded[g][:, 1, :, :].rearrange("p (line i) t -> p line t i", i=4),
+                target.rearrange("p (line i) t -> p line t i", i=4),
                 source.rearrange("p t (line i) -> p line t i", i=4),
                 COPY,
             )
 
-        def quantize(g):
-            nc.vector.quantize_mx(
-                out=x_codes[g][:].rearrange("p a s -> p (a s)").bitcast(FP8X4),
-                scales=x_scales[g][:].rearrange("p a s -> p (a s)"),
-                in_=rounded[g][:].rearrange("p a s t -> p (a s t)"),
-            )
+        def quantize(call):
+            rounded, codes, scales = calls[call]
+            nc.vector.quantize_mx(out=codes[:].bitcast(FP8X4), scales=scales[:], in_=rounded)
+
+        def quantized(g, a, le):
+            if g == 0:
+                call, start = 0, a * GROUP + le * C
+            elif a == 0:
+                call, start = 1, (g - 1) * GROUP + le * C
+            else:
+                call, start = 1 + g, le * C
+            return calls[call][1][:, start:start + C], calls[call][2][:, start:start + C]
 
         def weights(g, c, matrix):
             c_first, c_end, words = [part[1:] for part in w_parts if part[0] == g and part[1] <= c < part[2]][0]
             start = (matrix * (c_end - c_first) + c - c_first) * P
             return words[:, start:start + P]
 
-        def multiply_experts(g, c, experts):
+        def multiply(g, c):
             acc = acc_psum.tile([P, GROUP], F32, name="acc")
-            for le in experts:
-                slots = slice(le * C, (le + 1) * C)
+            for le in range(EG):
                 for a in range(PASSES):
+                    codes, scales = quantized(g, a, le)
                     nc.tensor.matmul_mx(
-                        out=acc[:, slots],
+                        out=acc[:, le * C:(le + 1) * C],
                         lhsT=weights(g, c, le * PASSES + a).bitcast(FP8X4),
                         lhsT_scale=w_scale_rows[4 * a:P, g * EG + le, c * P:(c + 1) * P],
-                        rhs=x_codes[g][:, a, slots].bitcast(FP8X4),
-                        rhs_scale=x_scales[g][:, a, slots],
+                        rhs=codes.bitcast(FP8X4),
+                        rhs_scale=scales,
                         start=(a == 0),
                         stop=(a == PASSES - 1),
                     )
-            for le in experts:
-                e = g * EG + le
+            return acc
+
+        def add_bias(g, c, acc):
+            y = y_head[c] if g == 0 else y_rest[c][:, (g - 1) * GROUP:g * GROUP]
+            columns = bias_head[c] if g == 0 else bias_rest[:, c, (g - 1) * EG:g * EG]
+            for le in range(EG):
                 nc.scalar.activation(
-                    ys[c][:, e * C:(e + 1) * C], acc[:, le * C:(le + 1) * C], IDENT, bias=bias[:, c, e:e + 1]
+                    y[:, le * C:(le + 1) * C], acc[:, le * C:(le + 1) * C], IDENT, bias=columns[:, le:le + 1]
                 )
 
-        def multiply(g, c):
-            multiply_experts(g, c, range(EG))
-
-        def scatter(c, lo, hi):
-            nc.vector.tensor_copy(windows[c][:].indirect(offsets[:, lo // 16:hi // 16]), ys[c][:, lo:hi])
-
-        def store(c):
-            nc.sync.dma_start(out=out[c * P:(c + 1) * P, :], in_=windows[c][:])
+        def scatter(c, y, lo, hi):
+            nc.vector.tensor_copy(windows[c][:].indirect(offsets[:, lo // 16:hi // 16]), y)
 
         scale_words = w_scale_rows[:].bitcast(I32)
         nc.vector.memset(scale_words, 0)
@@ -183,64 +201,67 @@ def tile_moe_pre_lin_bias_kernel(tc, xT, w_words, w_scales, b, gate, offs, out):
         nc.gpsimd.memset(gate_rows[:], 0.0)
 
         nc.sync.dma_start(offsets[:], offs)
-        nc.sync.dma_start(out=planes[0][:, 0:T // 2], in_=xT[0:P, 0:T // 2])
-        nc.scalar.dma_start(out=planes[0][:, T // 2:T], in_=xT[0:P, T // 2:T])
-        for i in range(1, PACK):
-            load_plane(i)
+        nc.sync.dma_start(out=planes[0][:, 0:T // 2], in_=rows[0, 0][:, 0:T // 2])
+        nc.scalar.dma_start(out=planes[0][:, T // 2:T], in_=rows[0, 0][:, T // 2:T])
+        load_plane(0, 1)
+        nc.sync.dma_start(out=gate_rows[0:E, :], in_=gate[0, :].rearrange("(e place) -> e place", place=C))
+        load_plane(0, 2)
+        load_plane(0, 3)
+        load_plane(1, WHOLE)
+        load_plane(1, 0)
+        load_plane(1, 1)
+        nc.sync.dma_start(out=gates[:], in_=gate[0:P, :])
+        load_plane(1, 2)
+        for part in w_parts[:2]:
+            load_weights(part)
         for quad in range(4):
             for a in range(PASSES):
                 nc.sync.dma_start(
                     out=scale_words[32 * quad + 4 * a:32 * quad + 4 * a + 4, :, :],
                     in_=w_scales[:, a, 4 * quad:4 * quad + 4, :].rearrange("e r n -> r e n").bitcast(I32),
                 )
-        nc.sync.dma_start(out=bias[:], in_=b.rearrange("(c p) e -> p c e", p=P))
-        nc.sync.dma_start(out=gate_rows[0:E, :], in_=gate[0, :].rearrange("(e place) -> e place", place=C))
-        nc.sync.dma_start(out=gate_head[:], in_=gate[0:P, 0:HEAD])
-        for i in range(PACK, PASSES * PACK):
-            load_plane(i)
-        load_weights(w_parts[0])
-        nc.sync.dma_start(out=gate_rest[:], in_=gate[0:P, HEAD:S])
-        load_weights(w_parts[1])
-
-        turn_gate()
-        for j in range(PACK):
-            nc.vector.tensor_copy(first[:, j, :], planes[j][:].indirect(offsets[:]))
-        for g in range(GROUPS - 1):
-            scale_first(g, 0)
-            scale_first(g, 1)
-        for t in range(PACK):
-            gather_second(t, second_head, gate_head[:], 0, HEAD)
-        interleave(0)
-        interleave(1)
-        for t in range(PACK - 1):
-            gather_second(t, second_rest, gate_rest[:], HEAD, S)
-        quantize(0)
-        gather_second(PACK - 1, second_rest, gate_rest[:], HEAD, S)
+        bias_rows = b.rearrange("(c p) e -> p c e", p=P)
+        nc.sync.dma_start(out=bias_outer[:], in_=bias_rows[:, 0:NT:2, 0:EG])
+        nc.sync.dma_start(out=bias_second[:], in_=bias_rows[:, 1, 0:EG])
+        nc.sync.dma_start(out=bias_rest[:], in_=bias_rows[:, :, EG:E])
         for part in w_parts[2:]:
             load_weights(part)
+
+        turn_gate()
+        for t in range(PACK):
+            nc.vector.tensor_copy(first[:, t, :], planes[t][:].indirect(offsets[:]))
+        for e0 in range(0, E, 2):
+            scale_pairs(0, e0, [low[e0][:], low[e0 + 1][:]])
+        for e0 in range(0, E - EG, 2):
+            finish_first(e0)
+        gather_second(WHOLE, second[:, HEAD_AT + WHOLE * GROUP:HEAD_AT + WHOLE * GROUP + S], 0, S)
+        for t in range(WHOLE):
+            gather_second(t, second_head[:, t, :], 0, GROUP)
+        interleave(rounded_head[:, 1, :, :], second_head)
+        for t in range(WHOLE - 1):
+            gather_second(t, second_rest[:, t, :], GROUP, S)
+        quantize(0)
+        gather_second(WHOLE - 1, second_rest[:, WHOLE - 1, :], GROUP, S)
+        for e0 in range(E - EG, E, 2):
+            finish_first(e0)
         quantize(1)
-        for le in range(EG):
-            multiply_experts(0, 1, [le])
-        scatter(1, 0, GROUP)
-        multiply(0, 0)
-        multiply_experts(1, 0, range(0, EG // 2))
-        multiply_experts(1, 0, range(EG // 2, EG))
-        scatter(0, 0, HEAD)
-        interleave(2)
-        scale_first(2, 0)
-        scale_first(2, 1)
+        sums = [multiply(0, c) for c in range(NT)]
+        add_bias(0, 0, sums[0])
+        scatter(0, y_head[0], 0, GROUP)
+        interleave(rounded_mid[:], second_rest[:, :, 0:GROUP])
         quantize(2)
-        multiply(0, 2)
-        multiply(1, 2)
-        scatter(2, 0, HEAD)
-        multiply(2, 0)
-        scatter(0, HEAD, S)
-        store(0)
-        multiply(2, 2)
-        scatter(2, HEAD, S)
-        store(2)
-        multiply(1, 1)
-        multiply(2, 1)
-        scatter(1, GROUP, S)
-        nc.sync.dma_start(out=out[P:2 * P, 0:T // 2], in_=windows[1][:, 0:T // 2])
-        nc.scalar.dma_start(out=out[P:2 * P, T // 2:T], in_=windows[1][:, T // 2:T])
+        add_bias(0, 1, sums[1])
+        scatter(1, y_head[1], 0, GROUP)
+        interleave(rounded_last[:], second_rest[:, :, GROUP:REST])
+        quantize(3)
+        add_bias(0, 2, sums[2])
+        scatter(2, y_head[2], 0, GROUP)
+        for c in range(NT):
+            for g in range(1, GROUPS):
+                add_bias(g, c, multiply(g, c))
+            scatter(c, y_rest[c][:], GROUP, S)
+            if c < NT - 1:
+                nc.sync.dma_start(out=out[c * P:(c + 1) * P, :], in_=windows[c][:])
+        last = slice((NT - 1) * P, N)
+        nc.sync.dma_start(out=out[last, 0:T // 2], in_=windows[NT - 1][:, 0:T // 2])
+        nc.scalar.dma_start(out=out[last, T // 2:T], in_=windows[NT - 1][:, T // 2:T])

@@ -45,10 +45,13 @@ def tile_moe_pre_lin_bias_kernel(tc, xT, w_words, w_scales, b, gate, offs, out):
         acc_psum = ctx.enter_context(tc.psum_pool(name="acc_psum", bufs=3))
 
         offsets = keep.tile([P, S // 16], U16, name="offsets")
-        planes = [keep.tile([P, WIDE], F32, name="plane%d" % i) for i in range(PACK)]
-        planes.extend(keep.tile([P, ROOMY if t == WHOLE else T], F32, name="plane%d" % (PACK + t)) for t in range(PACK))
+        planes = [keep.tile([P, WIDE], F32, name="plane%d" % i, align_bytes=256) for i in range(PACK)]
+        planes.extend(
+            keep.tile([P, ROOMY if t == WHOLE else T], F32, name="plane%d" % (PACK + t), align_bytes=256)
+            for t in range(PACK)
+        )
         identity = keep.tile([P, P], F32, name="identity")
-        gates = keep.tile([P, S], F32, name="gates")
+        gates = keep.tile([P, S], F32, name="gates", align_bytes=256)
         gate_rows = keep.tile([P, C], F32, name="gate_rows")
         gate_cols = keep.tile([P, E], F32, name="gate_cols")
         first = keep.tile([P, PACK, S], F32, name="first")
@@ -83,7 +86,7 @@ def tile_moe_pre_lin_bias_kernel(tc, xT, w_words, w_scales, b, gate, offs, out):
         y_first = keep.tile([P, GROUP], F32, name="y_first")
         y_head = [y_first[:], second[:, 0:GROUP], second[:, GROUP:2 * GROUP]]
         y_rest = [keep.tile([P, REST], F32, name="y_rest%d" % c) for c in range(NT)]
-        windows = [keep.tile([P, T], F32, name="window%d" % c) for c in range(NT)]
+        windows = [keep.tile([P, T], F32, name="window%d" % c, align_bytes=256) for c in range(NT)]
 
         rows = xT.rearrange("(a p t) token -> a t p token", a=PASSES, t=PACK)
 

@@ -31,7 +31,8 @@ WIDE = 2048
 ROOMY = T + 16
 WHOLE = PACK - 1
 MATRICES = EG * PASSES
-HEAD_AT = PACK * S - S - PACK * GROUP
+HEAD_AT = WHOLE * S - PACK * GROUP
+DMA_ALIGN = 256
 
 
 def tile_moe_pre_lin_bias_kernel(tc, xT, w_words, w_scales, b, gate, offs, out):
@@ -45,13 +46,13 @@ def tile_moe_pre_lin_bias_kernel(tc, xT, w_words, w_scales, b, gate, offs, out):
         acc_psum = ctx.enter_context(tc.psum_pool(name="acc_psum", bufs=3))
 
         offsets = keep.tile([P, S // 16], U16, name="offsets")
-        planes = [keep.tile([P, WIDE], F32, name="plane%d" % i, align_bytes=256) for i in range(PACK)]
+        planes = [keep.tile([P, WIDE], F32, name="plane%d" % t, align_bytes=DMA_ALIGN) for t in range(PACK)]
         planes.extend(
-            keep.tile([P, ROOMY if t == WHOLE else T], F32, name="plane%d" % (PACK + t), align_bytes=256)
+            keep.tile([P, ROOMY if t == WHOLE else T], F32, name="plane%d" % (PACK + t), align_bytes=DMA_ALIGN)
             for t in range(PACK)
         )
         identity = keep.tile([P, P], F32, name="identity")
-        gates = keep.tile([P, S], F32, name="gates", align_bytes=256)
+        gates = keep.tile([P, S], F32, name="gates", align_bytes=DMA_ALIGN)
         gate_rows = keep.tile([P, C], F32, name="gate_rows")
         gate_cols = keep.tile([P, E], F32, name="gate_cols")
         first = keep.tile([P, PACK, S], F32, name="first")
@@ -86,7 +87,7 @@ def tile_moe_pre_lin_bias_kernel(tc, xT, w_words, w_scales, b, gate, offs, out):
         y_first = keep.tile([P, GROUP], F32, name="y_first")
         y_head = [y_first[:], second[:, 0:GROUP], second[:, GROUP:2 * GROUP]]
         y_rest = [keep.tile([P, REST], F32, name="y_rest%d" % c) for c in range(NT)]
-        windows = [keep.tile([P, T], F32, name="window%d" % c, align_bytes=256) for c in range(NT)]
+        windows = [keep.tile([P, T], F32, name="window%d" % c, align_bytes=DMA_ALIGN) for c in range(NT)]
 
         rows = xT.rearrange("(a p t) token -> a t p token", a=PASSES, t=PACK)
 
@@ -263,8 +264,4 @@ def tile_moe_pre_lin_bias_kernel(tc, xT, w_words, w_scales, b, gate, offs, out):
             for g in range(1, GROUPS):
                 add_bias(g, c, multiply(g, c))
             scatter(c, y_rest[c][:], GROUP, S)
-            if c < NT - 1:
-                nc.sync.dma_start(out=out[c * P:(c + 1) * P, :], in_=windows[c][:])
-        last = slice((NT - 1) * P, N)
-        nc.sync.dma_start(out=out[last, 0:T // 2], in_=windows[NT - 1][:, 0:T // 2])
-        nc.scalar.dma_start(out=out[last, T // 2:T], in_=windows[NT - 1][:, T // 2:T])
+            nc.sync.dma_start(out=out[c * P:(c + 1) * P, :], in_=windows[c][:])

@@ -55,19 +55,19 @@ def tile_moe_pre_lin_bias_kernel(tc, xT, w_words, w_scales, b, gate, offs, out):
         gates = keep.tile([P, S], F32, name="gates", align_bytes=DMA_ALIGN)
         gate_rows = keep.tile([P, C], F32, name="gate_rows")
         gate_cols = keep.tile([P, E], F32, name="gate_cols")
-        first = keep.tile([P, PACK, S], F32, name="first")
-        second = keep.tile([P, PACK * S], F32, name="second")
-        second_head = second[:, HEAD_AT:HEAD_AT + PACK * GROUP].rearrange("p (t s) -> p t s", t=PACK)
-        second_rest = second[:].rearrange("p (t s) -> p t s", t=PACK)[:, :, 0:REST]
+        pass0 = keep.tile([P, PACK, S], F32, name="pass0")
+        pass1 = keep.tile([P, PACK * S], F32, name="pass1")
+        pass1_head = pass1[:, HEAD_AT:HEAD_AT + PACK * GROUP].rearrange("p (t s) -> p t s", t=PACK)
+        pass1_rest = pass1[:].rearrange("p (t s) -> p t s", t=PACK)[:, :, 0:REST]
         low = [keep.tile([P, P], F32, name="low%d" % e) for e in range(E)]
         rounded_head = keep.tile([P, PASSES, GROUP, PACK], BF16, name="rounded_head", align_bytes=64)
         rounded_rest = keep.tile([P, REST, PACK], BF16, name="rounded_rest", align_bytes=64)
-        w_first = shared.tile([P, MATRICES * P], U32, name="w_first", align_bytes=64, offset=0)
+        w_tile0 = shared.tile([P, MATRICES * P], U32, name="w_tile0", align_bytes=64, offset=0)
         rounded_mid = shared.tile([P, GROUP, PACK], BF16, name="rounded_mid", align_bytes=64, offset=0)
-        bias_second = shared.tile([P, EG], F32, name="bias_second", offset=MATRICES * P * 4)
+        bias_tile1 = shared.tile([P, EG], F32, name="bias_tile1", offset=MATRICES * P * 4)
         rounded_last = shared.tile([P, GROUP, PACK], BF16, name="rounded_last", align_bytes=64, offset=MATRICES * P * 4)
         calls = []
-        for name, tile, width in (
+        for name, rounded, width in (
             ("head", rounded_head[:].rearrange("p a s t -> p (a s t)"), PASSES * GROUP),
             ("rest", rounded_rest[:].rearrange("p s t -> p (s t)"), REST),
             ("mid", rounded_mid[:].rearrange("p s t -> p (s t)"), GROUP),
@@ -75,17 +75,17 @@ def tile_moe_pre_lin_bias_kernel(tc, xT, w_words, w_scales, b, gate, offs, out):
         ):
             codes = keep.tile([P, width], U32, name="codes_" + name, align_bytes=64)
             scales = keep.tile([P, width], U8, name="scales_" + name, align_bytes=64)
-            calls.append((tile, codes, scales))
-        w_head = keep.tile([P, MATRICES * (N - P)], U32, name="w_head", align_bytes=64)
+            calls.append((rounded, codes, scales))
+        w_tiles12 = keep.tile([P, MATRICES * (N - P)], U32, name="w_tiles12", align_bytes=64)
         w_mid = keep.tile([P, MATRICES * N], U32, name="w_mid", align_bytes=64)
         w_last = keep.tile([P, MATRICES * N], U32, name="w_last", align_bytes=64)
-        w_parts = [(0, 0, 1, w_first[:]), (0, 1, NT, w_head[:]), (1, 0, NT, w_mid[:]), (2, 0, NT, w_last[:])]
+        w_parts = [(0, 0, 1, w_tile0[:]), (0, 1, NT, w_tiles12[:]), (1, 0, NT, w_mid[:]), (2, 0, NT, w_last[:])]
         w_scale_rows = keep.tile([P, E, N], U8, name="w_scale_rows", align_bytes=64)
-        bias_outer = keep.tile([P, 2, EG], F32, name="bias_outer")
-        bias_head = [bias_outer[:, 0, :], bias_second[:], bias_outer[:, 1, :]]
+        bias_tiles02 = keep.tile([P, 2, EG], F32, name="bias_tiles02")
+        bias_head = [bias_tiles02[:, 0, :], bias_tile1[:], bias_tiles02[:, 1, :]]
         bias_rest = keep.tile([P, NT, E - EG], F32, name="bias_rest")
-        y_first = keep.tile([P, GROUP], F32, name="y_first")
-        y_head = [y_first[:], second[:, 0:GROUP], second[:, GROUP:2 * GROUP]]
+        y_tile0 = keep.tile([P, GROUP], F32, name="y_tile0")
+        y_head = [y_tile0[:], pass1[:, 0:GROUP], pass1[:, GROUP:2 * GROUP]]
         y_rest = [keep.tile([P, REST], F32, name="y_rest%d" % c) for c in range(NT)]
         windows = [keep.tile([P, T], F32, name="window%d" % c, align_bytes=DMA_ALIGN) for c in range(NT)]
 
@@ -107,12 +107,12 @@ def tile_moe_pre_lin_bias_kernel(tc, xT, w_words, w_scales, b, gate, offs, out):
             nc.tensor.transpose(bank[:, 0:P], gate_rows[:], identity[:])
             nc.scalar.copy(gate_cols[:], bank[:, 0:E])
 
-        def scale_pairs(u, e0, targets):
+        def gate_pairs(u, e0, targets):
             turned = turn_psum.tile([P, 2, 2, P], F32, name="turned")
             for h in range(2):
                 e = e0 + h
                 for v in range(2):
-                    nc.tensor.transpose(turned[:, h, v, :], first[:, 2 * u + v, e * C:(e + 1) * C], identity[:])
+                    nc.tensor.transpose(turned[:, h, v, :], pass0[:, 2 * u + v, e * C:(e + 1) * C], identity[:])
             for h in range(2):
                 e = e0 + h
                 nc.scalar.activation(
@@ -122,13 +122,13 @@ def tile_moe_pre_lin_bias_kernel(tc, xT, w_words, w_scales, b, gate, offs, out):
                     scale=gate_cols[:, e:e + 1],
                 )
 
-        def finish_first(e0):
+        def finish_pass0(e0):
             if e0 < E - EG:
                 high = [stage.tile([P, P], F32, name="high")[:] for h in range(2)]
             else:
                 at = HEAD_AT + (e0 - (E - EG)) * P
-                high = [second[:, at + h * P:at + (h + 1) * P] for h in range(2)]
-            scale_pairs(1, e0, high)
+                high = [pass1[:, at + h * P:at + (h + 1) * P] for h in range(2)]
+            gate_pairs(1, e0, high)
             back = back_psum.tile([P, 2, 2, C], F32, name="back")
             for h in range(2):
                 nc.tensor.transpose(back[:, h, 0, :], low[e0 + h][:], identity[:])
@@ -142,7 +142,7 @@ def tile_moe_pre_lin_bias_kernel(tc, xT, w_words, w_scales, b, gate, offs, out):
                 target.rearrange("p (h s u) -> p h s u", h=2, u=2), back[:].rearrange("p h u s -> p h s u")
             )
 
-        def gather_second(t, target, lo, hi):
+        def gather_pass1(t, target, lo, hi):
             nc.vector.tensor_tensor(
                 target, planes[PACK + t][:].indirect(offsets[:, lo // 16:hi // 16]), gates[:, lo:hi], MULT
             )
@@ -225,38 +225,38 @@ def tile_moe_pre_lin_bias_kernel(tc, xT, w_words, w_scales, b, gate, offs, out):
                     in_=w_scales[:, a, 4 * quad:4 * quad + 4, :].rearrange("e r n -> r e n").bitcast(I32),
                 )
         bias_rows = b.rearrange("(c p) e -> p c e", p=P)
-        nc.sync.dma_start(out=bias_outer[:], in_=bias_rows[:, 0:NT:2, 0:EG])
-        nc.sync.dma_start(out=bias_second[:], in_=bias_rows[:, 1, 0:EG])
+        nc.sync.dma_start(out=bias_tiles02[:], in_=bias_rows[:, 0:NT:2, 0:EG])
+        nc.sync.dma_start(out=bias_tile1[:], in_=bias_rows[:, 1, 0:EG])
         nc.sync.dma_start(out=bias_rest[:], in_=bias_rows[:, :, EG:E])
         for part in w_parts[2:]:
             load_weights(part)
 
         turn_gate()
         for t in range(PACK):
-            nc.vector.tensor_copy(first[:, t, :], planes[t][:].indirect(offsets[:]))
+            nc.vector.tensor_copy(pass0[:, t, :], planes[t][:].indirect(offsets[:]))
         for e0 in range(0, E, 2):
-            scale_pairs(0, e0, [low[e0][:], low[e0 + 1][:]])
+            gate_pairs(0, e0, [low[e0][:], low[e0 + 1][:]])
         for e0 in range(0, E - EG, 2):
-            finish_first(e0)
-        gather_second(WHOLE, second[:, HEAD_AT + WHOLE * GROUP:HEAD_AT + WHOLE * GROUP + S], 0, S)
+            finish_pass0(e0)
+        gather_pass1(WHOLE, pass1[:, HEAD_AT + WHOLE * GROUP:HEAD_AT + WHOLE * GROUP + S], 0, S)
         for t in range(WHOLE):
-            gather_second(t, second_head[:, t, :], 0, GROUP)
-        interleave(rounded_head[:, 1, :, :], second_head)
+            gather_pass1(t, pass1_head[:, t, :], 0, GROUP)
+        interleave(rounded_head[:, 1, :, :], pass1_head)
         for t in range(WHOLE - 1):
-            gather_second(t, second_rest[:, t, :], GROUP, S)
+            gather_pass1(t, pass1_rest[:, t, :], GROUP, S)
         quantize(0)
-        gather_second(WHOLE - 1, second_rest[:, WHOLE - 1, :], GROUP, S)
+        gather_pass1(WHOLE - 1, pass1_rest[:, WHOLE - 1, :], GROUP, S)
         for e0 in range(E - EG, E, 2):
-            finish_first(e0)
+            finish_pass0(e0)
         quantize(1)
         sums = [multiply(0, c) for c in range(NT)]
         add_bias(0, 0, sums[0])
         scatter(0, y_head[0], 0, GROUP)
-        interleave(rounded_mid[:], second_rest[:, :, 0:GROUP])
+        interleave(rounded_mid[:], pass1_rest[:, :, 0:GROUP])
         quantize(2)
         add_bias(0, 1, sums[1])
         scatter(1, y_head[1], 0, GROUP)
-        interleave(rounded_last[:], second_rest[:, :, GROUP:REST])
+        interleave(rounded_last[:], pass1_rest[:, :, GROUP:REST])
         quantize(3)
         add_bias(0, 2, sums[2])
         scatter(2, y_head[2], 0, GROUP)

@@ -21,7 +21,7 @@ MULT = mybir.AluOpType.mult
 
 P = 128
 PACK = 4
-PASSES = K // (P * PACK)
+PASSES = 2
 NT = N // P
 GROUP = 512
 GROUPS = S // GROUP
@@ -29,10 +29,12 @@ EG = GROUP // C
 REST = S - GROUP
 WIDE = 2048
 ROOMY = T + 16
-WHOLE = PACK - 1
+COPIED = 2
 MATRICES = EG * PASSES
-HEAD_AT = WHOLE * S - PACK * GROUP
 DMA_ALIGN = 256
+HEAD_STEP = 6
+REST_STEP = 7
+ORDER1 = (0, 2, 3, 1)
 
 
 def tile_moe_pre_lin_bias_kernel(tc, xT, w_words, w_scales, b, gate, offs, out):
@@ -40,160 +42,142 @@ def tile_moe_pre_lin_bias_kernel(tc, xT, w_words, w_scales, b, gate, offs, out):
     with ExitStack() as ctx:
         keep = ctx.enter_context(tc.tile_pool(name="keep", bufs=1))
         shared = ctx.enter_context(tc.tile_pool(name="shared", bufs=1))
-        stage = ctx.enter_context(tc.tile_pool(name="stage", bufs=4))
-        turn_psum = ctx.enter_context(tc.psum_pool(name="turn_psum", bufs=3))
+        stage = ctx.enter_context(tc.tile_pool(name="stage", bufs=2))
+        turn_psum = ctx.enter_context(tc.psum_pool(name="turn_psum", bufs=2))
         back_psum = ctx.enter_context(tc.psum_pool(name="back_psum", bufs=2))
-        acc_psum = ctx.enter_context(tc.psum_pool(name="acc_psum", bufs=3))
+        acc_psum = ctx.enter_context(tc.psum_pool(name="acc_psum", bufs=4))
 
         offsets = keep.tile([P, S // 16], U16, name="offsets")
-        planes = [keep.tile([P, WIDE], F32, name="plane%d" % t, align_bytes=DMA_ALIGN) for t in range(PACK)]
-        planes.extend(
-            keep.tile([P, ROOMY if t == WHOLE else T], F32, name="plane%d" % (PACK + t), align_bytes=DMA_ALIGN)
-            for t in range(PACK)
-        )
+        widths = [WIDE] * COPIED + [ROOMY] * (6 - COPIED) + [T, T]
+        planes = [keep.tile([P, widths[i]], F32, name="plane%d" % i, align_bytes=DMA_ALIGN) for i in range(8)]
         identity = keep.tile([P, P], F32, name="identity")
-        gates = keep.tile([P, S], F32, name="gates", align_bytes=DMA_ALIGN)
+        gates = keep.tile([P, S], F32, name="gates")
         gate_rows = keep.tile([P, C], F32, name="gate_rows")
         gate_cols = keep.tile([P, E], F32, name="gate_cols")
-        pass0 = keep.tile([P, PACK, S], F32, name="pass0")
-        pass1 = keep.tile([P, PACK * S], F32, name="pass1")
-        pass1_head = pass1[:, HEAD_AT:HEAD_AT + PACK * GROUP].rearrange("p (t s) -> p t s", t=PACK)
-        pass1_rest = pass1[:].rearrange("p (t s) -> p t s", t=PACK)[:, :, 0:REST]
-        low = [keep.tile([P, P], F32, name="low%d" % e) for e in range(E)]
-        rounded_head = keep.tile([P, PASSES, GROUP, PACK], BF16, name="rounded_head", align_bytes=64)
-        rounded_rest = keep.tile([P, REST, PACK], BF16, name="rounded_rest", align_bytes=64)
-        w_tile0 = shared.tile([P, MATRICES * P], U32, name="w_tile0", align_bytes=64, offset=0)
-        rounded_mid = shared.tile([P, GROUP, PACK], BF16, name="rounded_mid", align_bytes=64, offset=0)
-        bias_tile1 = shared.tile([P, EG], F32, name="bias_tile1", offset=MATRICES * P * 4)
-        rounded_last = shared.tile([P, GROUP, PACK], BF16, name="rounded_last", align_bytes=64, offset=MATRICES * P * 4)
-        calls = []
-        for name, rounded, width in (
-            ("head", rounded_head[:].rearrange("p a s t -> p (a s t)"), PASSES * GROUP),
-            ("rest", rounded_rest[:].rearrange("p s t -> p (s t)"), REST),
-            ("mid", rounded_mid[:].rearrange("p s t -> p (s t)"), GROUP),
-            ("last", rounded_last[:].rearrange("p s t -> p (s t)"), GROUP),
-        ):
-            codes = keep.tile([P, width], U32, name="codes_" + name, align_bytes=64)
-            scales = keep.tile([P, width], U8, name="scales_" + name, align_bytes=64)
-            calls.append((rounded, codes, scales))
-        w_tiles12 = keep.tile([P, MATRICES * (N - P)], U32, name="w_tiles12", align_bytes=64)
-        w_mid = keep.tile([P, MATRICES * N], U32, name="w_mid", align_bytes=64)
-        w_last = keep.tile([P, MATRICES * N], U32, name="w_last", align_bytes=64)
-        w_parts = [(0, 0, 1, w_tile0[:]), (0, 1, NT, w_tiles12[:]), (1, 0, NT, w_mid[:]), (2, 0, NT, w_last[:])]
+        pass0 = keep.tile([P, PACK * S + 2 * GROUP], F32, name="pass0", align_bytes=64)
+        pass1 = keep.tile([P, (1 + 2 * REST_STEP) * GROUP], F32, name="pass1")
+        bias_held = shared.tile([P, EG], F32, name="bias_held", offset=0)
+        rounded_last = shared.tile([P, 2 * GROUP, PACK], BF16, name="rounded_last", align_bytes=64, offset=0)
+        rounded = [keep.tile([P, 2 * GROUP, PACK], BF16, name="rounded0", align_bytes=64)[:], rounded_last[:]]
+        rounded.insert(1, pass0[:, PACK * S - 2 * GROUP:].bitcast(BF16).rearrange("p (s t) -> p s t", t=PACK))
+        codes = [keep.tile([P, 2 * GROUP], U32, name="codes%d" % q, align_bytes=64) for q in range(3)]
+        scales = [keep.tile([P, 2 * GROUP], U8, name="scales%d" % q, align_bytes=64) for q in range(3)]
+        place = {(0, 0): (0, 0), (0, 1): (0, GROUP), (1, 0): (1, 0), (0, 2): (1, GROUP), (1, 1): (2, 0), (1, 2): (2, GROUP)}
+        words = [keep.tile([P, MATRICES * N], U32, name="words%d" % g, align_bytes=64) for g in range(GROUPS)]
         w_scale_rows = keep.tile([P, E, N], U8, name="w_scale_rows", align_bytes=64)
         bias_tiles02 = keep.tile([P, 2, EG], F32, name="bias_tiles02")
-        bias_head = [bias_tiles02[:, 0, :], bias_tile1[:], bias_tiles02[:, 1, :]]
+        bias_head = [bias_tiles02[:, 0, :], bias_held[:], bias_tiles02[:, 1, :]]
         bias_rest = keep.tile([P, NT, E - EG], F32, name="bias_rest")
-        y_tile0 = keep.tile([P, GROUP], F32, name="y_tile0")
-        y_head = [y_tile0[:], pass1[:, 0:GROUP], pass1[:, GROUP:2 * GROUP]]
-        y_rest = [keep.tile([P, REST], F32, name="y_rest%d" % c) for c in range(NT)]
+        y_head = [pass1[:, blk * GROUP:(blk + 1) * GROUP] for blk in (13, 14, 2)]
+        y_rest = [pass0[:, c * S:c * S + REST] for c in range(NT)]
         windows = [keep.tile([P, T], F32, name="window%d" % c, align_bytes=DMA_ALIGN) for c in range(NT)]
 
         rows = xT.rearrange("(a p t) token -> a t p token", a=PASSES, t=PACK)
 
-        def load_plane(a, t):
-            nc.sync.dma_start(out=planes[a * PACK + t][:, 0:T], in_=rows[a, t])
+        def load_plane(i):
+            nc.sync.dma_start(out=planes[i][:, 0:T], in_=rows[0, i] if i < PACK else rows[1, ORDER1[i - PACK]])
 
-        def load_weights(part):
-            g, c_first, c_end, words = part
+        def load_weights(g):
             source = w_words[g * EG:(g + 1) * EG].rearrange("e a p n t -> p (e a) (n t)")
             nc.sync.dma_start(
-                out=words.bitcast(I32).rearrange("p (m n) -> p m n", m=MATRICES),
-                in_=source[:, :, c_first * P * PACK:c_end * P * PACK].bitcast(I32),
+                out=words[g][:].bitcast(I32).rearrange("p (m n) -> p m n", m=MATRICES), in_=source.bitcast(I32)
             )
 
-        def turn_gate():
-            bank = acc_psum.tile([P, GROUP], F32, name="acc")
+        def spread_gate():
+            bank = turn_psum.tile([P, GROUP], F32, name="turned")
             nc.tensor.transpose(bank[:, 0:P], gate_rows[:], identity[:])
             nc.scalar.copy(gate_cols[:], bank[:, 0:E])
+            for g in range(GROUPS):
+                bank = turn_psum.tile([P, GROUP], F32, name="turned")
+                for le in range(EG):
+                    e = g * EG + le
+                    nc.tensor.transpose(
+                        bank[:, le * C:(le + 1) * C], gate_cols[:, e:e + 1].to_broadcast([P, P]), identity[:]
+                    )
+                nc.scalar.copy(gates[:, g * GROUP:(g + 1) * GROUP], bank[:])
 
-        def gate_pairs(u, e0, targets):
-            turned = turn_psum.tile([P, 2, 2, P], F32, name="turned")
-            for h in range(2):
-                e = e0 + h
-                for v in range(2):
-                    nc.tensor.transpose(turned[:, h, v, :], pass0[:, 2 * u + v, e * C:(e + 1) * C], identity[:])
-            for h in range(2):
-                e = e0 + h
+        def gate_copied(t, g):
+            at = t * S + g * GROUP
+            turned = turn_psum.tile([P, GROUP], F32, name="turned")
+            for le in range(EG):
+                nc.tensor.transpose(turned[:, le * P:(le + 1) * P], pass0[:, at + le * C:at + (le + 1) * C], identity[:])
+            staged = stage.tile([P, GROUP], F32, name="staged")
+            for le in range(EG):
+                e = g * EG + le
                 nc.scalar.activation(
-                    targets[h].bitcast(BF16).rearrange("s (line i v) -> s line v i", i=4, v=2),
-                    turned[:, h, :, :].rearrange("s v (line i) -> s line v i", i=4),
-                    COPY,
-                    scale=gate_cols[:, e:e + 1],
+                    staged[:, le * P:(le + 1) * P], turned[:, le * P:(le + 1) * P], COPY, scale=gate_cols[:, e:e + 1]
                 )
+            back = back_psum.tile([P, GROUP], F32, name="back")
+            for le in range(EG):
+                nc.tensor.transpose(back[:, le * C:(le + 1) * C], staged[:, le * P:(le + 1) * P], identity[:])
+            nc.scalar.copy(pass0[:, at:at + GROUP], back[:])
 
-        def finish_pass0(e0):
-            if e0 < E - EG:
-                high = [stage.tile([P, P], F32, name="high")[:] for h in range(2)]
-            else:
-                at = HEAD_AT + (e0 - (E - EG)) * P
-                high = [pass1[:, at + h * P:at + (h + 1) * P] for h in range(2)]
-            gate_pairs(1, e0, high)
-            back = back_psum.tile([P, 2, 2, C], F32, name="back")
-            for h in range(2):
-                nc.tensor.transpose(back[:, h, 0, :], low[e0 + h][:], identity[:])
-                nc.tensor.transpose(back[:, h, 1, :], high[h], identity[:])
-            if e0 < EG:
-                target = rounded_head[:, 0, e0 * C:(e0 + 2) * C, :]
-            else:
-                target = rounded_rest[:, (e0 - EG) * C:(e0 - EG + 2) * C, :]
-            target = target.rearrange("p s t -> p (s t)").bitcast(F32)
-            nc.scalar.copy(
-                target.rearrange("p (h s u) -> p h s u", h=2, u=2), back[:].rearrange("p h u s -> p h s u")
-            )
+        def gather(i, target, lo, hi):
+            nc.vector.tensor_tensor(target, planes[i][:].indirect(offsets[:, lo // 16:hi // 16]), gates[:, lo:hi], MULT)
 
-        def gather_pass1(t, target, lo, hi):
-            nc.vector.tensor_tensor(
-                target, planes[PACK + t][:].indirect(offsets[:, lo // 16:hi // 16]), gates[:, lo:hi], MULT
-            )
+        def target_of(a, g):
+            call, start = place[(a, g)]
+            return rounded[call][:, start:start + GROUP, :]
 
-        def interleave(target, source):
+        def round_pass0(g):
+            source = pass0[:, 0:PACK * S].rearrange("p (t s) -> p t s", t=PACK)[:, :, g * GROUP:(g + 1) * GROUP]
             nc.scalar.activation(
-                target.rearrange("p (line i) t -> p line t i", i=4),
+                target_of(0, g).rearrange("p (line i) t -> p line t i", i=4),
                 source.rearrange("p t (line i) -> p line t i", i=4),
                 COPY,
             )
 
-        def quantize(call):
-            rounded, codes, scales = calls[call]
-            nc.vector.quantize_mx(out=codes[:].bitcast(FP8X4), scales=scales[:], in_=rounded)
+        def round_pass1(g):
+            first, step = (0, HEAD_STEP) if g == 0 else (1, REST_STEP)
+            blocks = pass1[:, first * GROUP:(first + 2 * step) * GROUP].rearrange("p (v blk s) -> p v blk s", v=2, s=GROUP)
+            at = g - first
+            nc.scalar.copy(
+                target_of(1, g).rearrange("p (line i) (u v) -> p line u v i", i=4, u=2),
+                blocks[:, :, at:at + 4:3, :].rearrange("p v u (line i) -> p line u v i", i=4),
+            )
 
-        def quantized(g, a, le):
-            if g == 0:
-                call, start = 0, a * GROUP + le * C
-            elif a == 0:
-                call, start = 1, (g - 1) * GROUP + le * C
-            else:
-                call, start = 1 + g, le * C
-            return calls[call][1][:, start:start + C], calls[call][2][:, start:start + C]
+        def block(t, g, count):
+            u, v = divmod(t, 2)
+            at = g + 3 * u + (HEAD_STEP if g == 0 else REST_STEP) * v
+            return pass1[:, at * GROUP:(at + count) * GROUP]
 
-        def weights(g, c, matrix):
-            c_first, c_end, words = [part[1:] for part in w_parts if part[0] == g and part[1] <= c < part[2]][0]
-            start = (matrix * (c_end - c_first) + c - c_first) * P
-            return words[:, start:start + P]
+        def quantize(q):
+            nc.vector.quantize_mx(
+                out=codes[q][:].bitcast(FP8X4), scales=scales[q][:], in_=rounded[q].rearrange("p s t -> p (s t)")
+            )
 
-        def multiply(g, c):
-            acc = acc_psum.tile([P, GROUP], F32, name="acc")
-            for le in range(EG):
-                for a in range(PASSES):
-                    codes, scales = quantized(g, a, le)
-                    nc.tensor.matmul_mx(
-                        out=acc[:, le * C:(le + 1) * C],
-                        lhsT=weights(g, c, le * PASSES + a).bitcast(FP8X4),
-                        lhsT_scale=w_scale_rows[4 * a:P, g * EG + le, c * P:(c + 1) * P],
-                        rhs=codes.bitcast(FP8X4),
-                        rhs_scale=scales,
-                        start=(a == 0),
-                        stop=(a == PASSES - 1),
-                    )
-            return acc
+        def product(acc, column, g, c, le, a, start, stop):
+            call, first = place[(a, g)]
+            lo = first + le * C
+            at = (le * PASSES + a) * N + c * P
+            nc.tensor.matmul_mx(
+                out=acc[:, column:column + C],
+                lhsT=words[g][:, at:at + P].bitcast(FP8X4),
+                lhsT_scale=w_scale_rows[4 * a:P, g * EG + le, c * P:(c + 1) * P],
+                rhs=codes[call][:, lo:lo + C].bitcast(FP8X4),
+                rhs_scale=scales[call][:, lo:lo + C],
+                start=start,
+                stop=stop,
+            )
 
-        def add_bias(g, c, acc):
+        def open_sums(g, c, experts):
+            acc = acc_psum.tile([P, len(experts) * C], F32, name="acc")
+            for i, le in enumerate(experts):
+                product(acc, i * C, g, c, le, 0, i == 0, False)
+            return acc, g, c, experts
+
+        def close_sums(sums):
+            acc, g, c, experts = sums
+            for i, le in enumerate(experts):
+                product(acc, i * C, g, c, le, 1, False, i == len(experts) - 1)
+
+        def add_bias(sums):
+            acc, g, c, experts = sums
             y = y_head[c] if g == 0 else y_rest[c][:, (g - 1) * GROUP:g * GROUP]
             columns = bias_head[c] if g == 0 else bias_rest[:, c, (g - 1) * EG:g * EG]
-            for le in range(EG):
+            for i, le in enumerate(experts):
                 nc.scalar.activation(
-                    y[:, le * C:(le + 1) * C], acc[:, le * C:(le + 1) * C], IDENT, bias=columns[:, le:le + 1]
+                    y[:, le * C:(le + 1) * C], acc[:, i * C:(i + 1) * C], IDENT, bias=columns[:, le:le + 1]
                 )
 
         def scatter(c, y, lo, hi):
@@ -201,23 +185,17 @@ def tile_moe_pre_lin_bias_kernel(tc, xT, w_words, w_scales, b, gate, offs, out):
 
         scale_words = w_scale_rows[:].bitcast(I32)
         nc.vector.memset(scale_words, 0)
-        make_identity(nc, identity[:])
         nc.gpsimd.memset(gate_rows[:], 0.0)
+        make_identity(nc, identity[:])
 
         nc.sync.dma_start(offsets[:], offs)
         nc.sync.dma_start(out=planes[0][:, 0:T // 2], in_=rows[0, 0][:, 0:T // 2])
         nc.scalar.dma_start(out=planes[0][:, T // 2:T], in_=rows[0, 0][:, T // 2:T])
-        load_plane(0, 1)
         nc.sync.dma_start(out=gate_rows[0:E, :], in_=gate[0, :].rearrange("(e place) -> e place", place=C))
-        load_plane(0, 2)
-        load_plane(0, 3)
-        load_plane(1, WHOLE)
-        load_plane(1, 0)
-        load_plane(1, 1)
-        nc.sync.dma_start(out=gates[:], in_=gate[0:P, :])
-        load_plane(1, 2)
-        for part in w_parts[:2]:
-            load_weights(part)
+        load_plane(1)
+        for i in range(2, 2 * PACK):
+            load_plane(i)
+        load_weights(0)
         for quad in range(4):
             for a in range(PASSES):
                 nc.sync.dma_start(
@@ -226,42 +204,49 @@ def tile_moe_pre_lin_bias_kernel(tc, xT, w_words, w_scales, b, gate, offs, out):
                 )
         bias_rows = b.rearrange("(c p) e -> p c e", p=P)
         nc.sync.dma_start(out=bias_tiles02[:], in_=bias_rows[:, 0:NT:2, 0:EG])
-        nc.sync.dma_start(out=bias_tile1[:], in_=bias_rows[:, 1, 0:EG])
+        nc.sync.dma_start(out=bias_held[:], in_=bias_rows[:, 1, 0:EG])
         nc.sync.dma_start(out=bias_rest[:], in_=bias_rows[:, :, EG:E])
-        for part in w_parts[2:]:
-            load_weights(part)
+        for g in range(1, GROUPS):
+            load_weights(g)
 
-        turn_gate()
-        for t in range(PACK):
-            nc.vector.tensor_copy(pass0[:, t, :], planes[t][:].indirect(offsets[:]))
-        for e0 in range(0, E, 2):
-            gate_pairs(0, e0, [low[e0][:], low[e0 + 1][:]])
-        for e0 in range(0, E - EG, 2):
-            finish_pass0(e0)
-        gather_pass1(WHOLE, pass1[:, HEAD_AT + WHOLE * GROUP:HEAD_AT + WHOLE * GROUP + S], 0, S)
-        for t in range(WHOLE):
-            gather_pass1(t, pass1_head[:, t, :], 0, GROUP)
-        interleave(rounded_head[:, 1, :, :], pass1_head)
-        for t in range(WHOLE - 1):
-            gather_pass1(t, pass1_rest[:, t, :], GROUP, S)
+        spread_gate()
+        for t in range(COPIED):
+            nc.vector.tensor_copy(pass0[:, t * S:(t + 1) * S], planes[t][:].indirect(offsets[:]))
+        for t in range(COPIED):
+            for g in range(GROUPS):
+                gate_copied(t, g)
+        for t in range(COPIED, PACK):
+            gather(t, pass0[:, t * S:(t + 1) * S], 0, S)
+        for g in range(GROUPS):
+            round_pass0(g)
+        for i in (4, 5):
+            gather(i, block(ORDER1[i - PACK], 0, GROUPS), 0, S)
+        for i in (6, 7):
+            gather(i, block(ORDER1[i - PACK], 0, 1), 0, GROUP)
+        round_pass1(0)
+        gather(6, block(ORDER1[2], 1, 2), GROUP, S)
         quantize(0)
-        gather_pass1(WHOLE - 1, pass1_rest[:, WHOLE - 1, :], GROUP, S)
-        for e0 in range(E - EG, E, 2):
-            finish_pass0(e0)
+        every = list(range(EG))
+        first = [open_sums(0, 0, every[:2]), open_sums(0, 0, every[2:]), open_sums(0, 1, every)]
         quantize(1)
-        sums = [multiply(0, c) for c in range(NT)]
-        add_bias(0, 0, sums[0])
+        gather(7, block(ORDER1[3], 1, 2), GROUP, S)
+        for sums in first:
+            close_sums(sums)
+            add_bias(sums)
+        third = open_sums(0, 2, every)
+        close_sums(third)
+        ahead = [open_sums(g, 0, every) for g in range(1, GROUPS)]
+        for g in range(1, GROUPS):
+            round_pass1(g)
         scatter(0, y_head[0], 0, GROUP)
-        interleave(rounded_mid[:], pass1_rest[:, :, 0:GROUP])
-        quantize(2)
-        add_bias(0, 1, sums[1])
         scatter(1, y_head[1], 0, GROUP)
-        interleave(rounded_last[:], pass1_rest[:, :, GROUP:REST])
-        quantize(3)
-        add_bias(0, 2, sums[2])
+        quantize(2)
+        add_bias(third)
         scatter(2, y_head[2], 0, GROUP)
         for c in range(NT):
             for g in range(1, GROUPS):
-                add_bias(g, c, multiply(g, c))
-            scatter(c, y_rest[c][:], GROUP, S)
+                sums = ahead[g - 1] if c == 0 else open_sums(g, c, every)
+                close_sums(sums)
+                add_bias(sums)
+            scatter(c, y_rest[c], GROUP, S)
             nc.sync.dma_start(out=out[c * P:(c + 1) * P, :], in_=windows[c][:])

@@ -32,6 +32,7 @@ ROOMY = T + 16
 COPIED = 2
 MATRICES = EG * PASSES
 DMA_ALIGN = 256
+CUT = 512
 HEAD_STEP = 6
 REST_STEP = 7
 ORDER1 = (0, 2, 3, 1)
@@ -189,8 +190,8 @@ def tile_moe_pre_lin_bias_kernel(tc, xT, w_words, w_scales, b, gate, offs, out):
         make_identity(nc, identity[:])
 
         nc.sync.dma_start(offsets[:], offs)
-        nc.sync.dma_start(out=planes[0][:, 0:T // 2], in_=rows[0, 0][:, 0:T // 2])
-        nc.scalar.dma_start(out=planes[0][:, T // 2:T], in_=rows[0, 0][:, T // 2:T])
+        nc.sync.dma_start(out=planes[0][:, 0:CUT], in_=rows[0, 0][:, 0:CUT])
+        nc.scalar.dma_start(out=planes[0][:, CUT:T], in_=rows[0, 0][:, CUT:T])
         nc.sync.dma_start(out=gate_rows[0:E, :], in_=gate[0, :].rearrange("(e place) -> e place", place=C))
         load_plane(1)
         for i in range(2, 2 * PACK):
@@ -249,4 +250,8 @@ def tile_moe_pre_lin_bias_kernel(tc, xT, w_words, w_scales, b, gate, offs, out):
                 close_sums(sums)
                 add_bias(sums)
             scatter(c, y_rest[c], GROUP, S)
-            nc.sync.dma_start(out=out[c * P:(c + 1) * P, :], in_=windows[c][:])
+            if c < NT - 1:
+                nc.sync.dma_start(out=out[c * P:(c + 1) * P, :], in_=windows[c][:])
+            else:
+                nc.sync.dma_start(out=out[c * P:(c + 1) * P, CUT:T], in_=windows[c][:, CUT:T])
+                nc.scalar.dma_start(out=out[c * P:(c + 1) * P, 0:CUT], in_=windows[c][:, 0:CUT])

@@ -18,184 +18,160 @@ FP8X4 = mybir.dt.float8_e4m3fn_x4
 COPY = mybir.ActivationFunctionType.Copy
 IDENT = mybir.ActivationFunctionType.Identity
 MULT = mybir.AluOpType.mult
+ADD = mybir.AluOpType.add
 
 P = 128
 PACK = 4
 PASSES = 2
 NT = N // P
-GROUP = 512
+EG = 3
+GROUP = EG * C
 GROUPS = S // GROUP
-EG = GROUP // C
-REST = S - GROUP
-WIDE = 2048
-ROOMY = T + 16
-COPIED = 2
-MATRICES = EG * PASSES
+VECTOR_GROUPS = (2, 1)
+RUN = 4
 DMA_ALIGN = 256
 CUT = 512
-HEAD_STEP = 6
-REST_STEP = 7
-ORDER1 = (0, 2, 3, 1)
 
 
 def tile_moe_pre_lin_bias_kernel(tc, xT, w_words, w_scales, b, gate, offs, out):
     nc = tc.nc
     with ExitStack() as ctx:
         keep = ctx.enter_context(tc.tile_pool(name="keep", bufs=1))
-        shared = ctx.enter_context(tc.tile_pool(name="shared", bufs=1))
-        stage = ctx.enter_context(tc.tile_pool(name="stage", bufs=2))
-        turn_psum = ctx.enter_context(tc.psum_pool(name="turn_psum", bufs=2))
-        back_psum = ctx.enter_context(tc.psum_pool(name="back_psum", bufs=2))
-        acc_psum = ctx.enter_context(tc.psum_pool(name="acc_psum", bufs=4))
+        gate_psum = ctx.enter_context(tc.psum_pool(name="gate_psum", bufs=1))
+        acc_psum = ctx.enter_context(tc.psum_pool(name="acc_psum", bufs=6))
 
         offsets = keep.tile([P, S // 16], U16, name="offsets")
-        widths = [WIDE] * COPIED + [ROOMY] * (6 - COPIED) + [T, T]
-        planes = [keep.tile([P, widths[i]], F32, name="plane%d" % i, align_bytes=DMA_ALIGN) for i in range(8)]
+        planes = [keep.tile([P, T], F32, name="plane%d" % i, align_bytes=DMA_ALIGN) for i in range(PASSES * PACK)]
         identity = keep.tile([P, P], F32, name="identity")
-        gates = keep.tile([P, S], F32, name="gates")
         gate_rows = keep.tile([P, C], F32, name="gate_rows")
         gate_cols = keep.tile([P, E], F32, name="gate_cols")
-        pass0 = keep.tile([P, PACK * S + 2 * GROUP], F32, name="pass0", align_bytes=64)
-        pass1 = keep.tile([P, (1 + 2 * REST_STEP) * GROUP], F32, name="pass1")
-        bias_held = shared.tile([P, EG], F32, name="bias_held", offset=0)
-        rounded_last = shared.tile([P, 2 * GROUP, PACK], BF16, name="rounded_last", align_bytes=64, offset=0)
-        rounded = [keep.tile([P, 2 * GROUP, PACK], BF16, name="rounded0", align_bytes=64)[:], rounded_last[:]]
-        rounded.insert(1, pass0[:, PACK * S - 2 * GROUP:].bitcast(BF16).rearrange("p (s t) -> p s t", t=PACK))
-        codes = [keep.tile([P, 2 * GROUP], U32, name="codes%d" % q, align_bytes=64) for q in range(3)]
-        scales = [keep.tile([P, 2 * GROUP], U8, name="scales%d" % q, align_bytes=64) for q in range(3)]
-        place = {(0, 0): (0, 0), (0, 1): (0, GROUP), (1, 0): (1, 0), (0, 2): (1, GROUP), (1, 1): (2, 0), (1, 2): (2, GROUP)}
-        words = [keep.tile([P, MATRICES * N], U32, name="words%d" % g, align_bytes=64) for g in range(GROUPS)]
+        gates = keep.tile([P, VECTOR_GROUPS[0] * GROUP], F32, name="gates")
+        cut = [n * GROUP for n in VECTOR_GROUPS]
+        gated = [keep.tile([P, PACK * cut[a]], F32, name="gated%d" % a, align_bytes=64) for a in range(PASSES)]
+        plain = [keep.tile([P, PACK * (S - cut[a])], F32, name="plain%d" % a) for a in range(PASSES)]
+        rounded0 = keep.tile([P, PACK * cut[0]], BF16, name="rounded0", align_bytes=64)
+        width = PACK * GROUP
+        rounded = {(0, g): rounded0[:, g * width:(g + 1) * width] for g in range(2)}
+        reused = gated[1][:].bitcast(BF16)
+        rounded[(0, 2)] = reused[:, 0:width]
+        rounded[(0, 3)] = reused[:, width:2 * width]
+        for g in range(GROUPS):
+            rounded[(1, g)] = keep.tile([P, width], BF16, name="rounded1%d" % g, align_bytes=64)[:]
+        codes = {
+            (a, g): keep.tile([P, GROUP], U32, name="codes%d%d" % (a, g), align_bytes=64)
+            for a in range(PASSES) for g in range(GROUPS)
+        }
+        scales = {
+            (a, g): keep.tile([P, GROUP], U8, name="scales%d%d" % (a, g), align_bytes=64)
+            for a in range(PASSES) for g in range(GROUPS)
+        }
+        words = [keep.tile([P, EG * PASSES * N], U32, name="words%d" % g, align_bytes=64) for g in range(GROUPS)]
         w_scale_rows = keep.tile([P, E, N], U8, name="w_scale_rows", align_bytes=64)
-        bias_tiles02 = keep.tile([P, 2, EG], F32, name="bias_tiles02")
-        bias_head = [bias_tiles02[:, 0, :], bias_held[:], bias_tiles02[:, 1, :]]
-        bias_rest = keep.tile([P, NT, E - EG], F32, name="bias_rest")
-        y_head = [pass1[:, blk * GROUP:(blk + 1) * GROUP] for blk in (13, 14, 2)]
-        y_rest = [pass0[:, c * S:c * S + REST] for c in range(NT)]
+        bias = keep.tile([P, NT, E], F32, name="bias")
+        y = [keep.tile([P, S], F32, name="y%d" % c) for c in range(NT)]
         windows = [keep.tile([P, T], F32, name="window%d" % c, align_bytes=DMA_ALIGN) for c in range(NT)]
 
         rows = xT.rearrange("(a p t) token -> a t p token", a=PASSES, t=PACK)
 
-        def load_plane(i):
-            nc.sync.dma_start(out=planes[i][:, 0:T], in_=rows[0, i] if i < PACK else rows[1, ORDER1[i - PACK]])
-
         def load_weights(g):
             source = w_words[g * EG:(g + 1) * EG].rearrange("e a p n t -> p (e a) (n t)")
             nc.sync.dma_start(
-                out=words[g][:].bitcast(I32).rearrange("p (m n) -> p m n", m=MATRICES), in_=source.bitcast(I32)
+                out=words[g][:].bitcast(I32).rearrange("p (m n) -> p m n", m=EG * PASSES), in_=source.bitcast(I32)
             )
 
-        def spread_gate():
-            bank = turn_psum.tile([P, GROUP], F32, name="turned")
-            nc.tensor.transpose(bank[:, 0:P], gate_rows[:], identity[:])
-            nc.scalar.copy(gate_cols[:], bank[:, 0:E])
-            for g in range(GROUPS):
-                bank = turn_psum.tile([P, GROUP], F32, name="turned")
-                for le in range(EG):
-                    e = g * EG + le
-                    nc.tensor.transpose(
-                        bank[:, le * C:(le + 1) * C], gate_cols[:, e:e + 1].to_broadcast([P, P]), identity[:]
-                    )
-                nc.scalar.copy(gates[:, g * GROUP:(g + 1) * GROUP], bank[:])
-
-        def gate_copied(t, g):
-            at = t * S + g * GROUP
-            turned = turn_psum.tile([P, GROUP], F32, name="turned")
+        def spread_gate(g, bank):
             for le in range(EG):
-                nc.tensor.transpose(turned[:, le * P:(le + 1) * P], pass0[:, at + le * C:at + (le + 1) * C], identity[:])
-            staged = stage.tile([P, GROUP], F32, name="staged")
+                e = g * EG + le
+                nc.tensor.transpose(
+                    bank[:, le * C:(le + 1) * C], gate_cols[:, e:e + 1].to_broadcast([P, P]), identity[:]
+                )
+
+        def listed(lo, hi):
+            return offsets[:, lo // 16:hi // 16]
+
+        def gather(a, t):
+            plane = planes[a * PACK + t]
+            rest = S - cut[a]
+            nc.vector.tensor_tensor(
+                gated[a][:, t * cut[a]:(t + 1) * cut[a]], plane[:].indirect(listed(0, cut[a])), gates[:, 0:cut[a]], MULT
+            )
+            nc.scalar.activation(plain[a][:, t * rest:(t + 1) * rest], plane[:].indirect(listed(cut[a], S)), COPY)
+
+        def woven(target):
+            return target.rearrange("p (line i t) -> p line t i", i=RUN, t=PACK)
+
+        def by_runs(source):
+            return source.rearrange("p t (line i) -> p line t i", i=RUN)
+
+        def round_gated(a, target):
+            nc.vector.tensor_copy(woven(target), by_runs(gated[a][:].rearrange("p (t s) -> p t s", t=PACK)))
+
+        def gate_and_round(a, g, factor):
+            lo = g * GROUP - cut[a]
+            source = plain[a][:].rearrange("p (t s) -> p t s", t=PACK)[:, :, lo:lo + GROUP]
+            spread = factor.rearrange("p (line i) -> p line i", i=RUN).unsqueeze(2)
+            nc.vector.tensor_tensor(
+                woven(rounded[(a, g)]), by_runs(source), spread.to_broadcast([P, GROUP // RUN, PACK, RUN]), MULT
+            )
+
+        def quantize(a, g):
+            nc.vector.quantize_mx(out=codes[(a, g)][:].bitcast(FP8X4), scales=scales[(a, g)][:], in_=rounded[(a, g)])
+
+        def products(g, c):
+            acc = acc_psum.tile([P, GROUP], F32, name="acc")
+            for a in range(PASSES):
+                for le in range(EG):
+                    at = (le * PASSES + a) * N + c * P
+                    nc.tensor.matmul_mx(
+                        out=acc[:, le * C:(le + 1) * C],
+                        lhsT=words[g][:, at:at + P].bitcast(FP8X4),
+                        lhsT_scale=w_scale_rows[4 * a:P, g * EG + le, c * P:(c + 1) * P],
+                        rhs=codes[(a, g)][:, le * C:(le + 1) * C].bitcast(FP8X4),
+                        rhs_scale=scales[(a, g)][:, le * C:(le + 1) * C],
+                        start=(a == 0 and le == 0),
+                        stop=(a == PASSES - 1 and le == EG - 1),
+                    )
+            return acc
+
+        def sums_for_scalar(g, c):
+            acc = products(g, c)
             for le in range(EG):
                 e = g * EG + le
                 nc.scalar.activation(
-                    staged[:, le * P:(le + 1) * P], turned[:, le * P:(le + 1) * P], COPY, scale=gate_cols[:, e:e + 1]
-                )
-            back = back_psum.tile([P, GROUP], F32, name="back")
-            for le in range(EG):
-                nc.tensor.transpose(back[:, le * C:(le + 1) * C], staged[:, le * P:(le + 1) * P], identity[:])
-            nc.scalar.copy(pass0[:, at:at + GROUP], back[:])
-
-        def gather(i, target, lo, hi):
-            nc.vector.tensor_tensor(target, planes[i][:].indirect(offsets[:, lo // 16:hi // 16]), gates[:, lo:hi], MULT)
-
-        def target_of(a, g):
-            call, start = place[(a, g)]
-            return rounded[call][:, start:start + GROUP, :]
-
-        def round_pass0(g):
-            source = pass0[:, 0:PACK * S].rearrange("p (t s) -> p t s", t=PACK)[:, :, g * GROUP:(g + 1) * GROUP]
-            nc.scalar.activation(
-                target_of(0, g).rearrange("p (line i) t -> p line t i", i=4),
-                source.rearrange("p t (line i) -> p line t i", i=4),
-                COPY,
-            )
-
-        def round_pass1(g):
-            first, step = (0, HEAD_STEP) if g == 0 else (1, REST_STEP)
-            blocks = pass1[:, first * GROUP:(first + 2 * step) * GROUP].rearrange("p (v blk s) -> p v blk s", v=2, s=GROUP)
-            at = g - first
-            nc.scalar.copy(
-                target_of(1, g).rearrange("p (line i) (u v) -> p line u v i", i=4, u=2),
-                blocks[:, :, at:at + 4:3, :].rearrange("p v u (line i) -> p line u v i", i=4),
-            )
-
-        def block(t, g, count):
-            u, v = divmod(t, 2)
-            at = g + 3 * u + (HEAD_STEP if g == 0 else REST_STEP) * v
-            return pass1[:, at * GROUP:(at + count) * GROUP]
-
-        def quantize(q):
-            nc.vector.quantize_mx(
-                out=codes[q][:].bitcast(FP8X4), scales=scales[q][:], in_=rounded[q].rearrange("p s t -> p (s t)")
-            )
-
-        def product(acc, column, g, c, le, a, start, stop):
-            call, first = place[(a, g)]
-            lo = first + le * C
-            at = (le * PASSES + a) * N + c * P
-            nc.tensor.matmul_mx(
-                out=acc[:, column:column + C],
-                lhsT=words[g][:, at:at + P].bitcast(FP8X4),
-                lhsT_scale=w_scale_rows[4 * a:P, g * EG + le, c * P:(c + 1) * P],
-                rhs=codes[call][:, lo:lo + C].bitcast(FP8X4),
-                rhs_scale=scales[call][:, lo:lo + C],
-                start=start,
-                stop=stop,
-            )
-
-        def open_sums(g, c, experts):
-            acc = acc_psum.tile([P, len(experts) * C], F32, name="acc")
-            for i, le in enumerate(experts):
-                product(acc, i * C, g, c, le, 0, i == 0, False)
-            return acc, g, c, experts
-
-        def close_sums(sums):
-            acc, g, c, experts = sums
-            for i, le in enumerate(experts):
-                product(acc, i * C, g, c, le, 1, False, i == len(experts) - 1)
-
-        def add_bias(sums):
-            acc, g, c, experts = sums
-            y = y_head[c] if g == 0 else y_rest[c][:, (g - 1) * GROUP:g * GROUP]
-            columns = bias_head[c] if g == 0 else bias_rest[:, c, (g - 1) * EG:g * EG]
-            for i, le in enumerate(experts):
-                nc.scalar.activation(
-                    y[:, le * C:(le + 1) * C], acc[:, i * C:(i + 1) * C], IDENT, bias=columns[:, le:le + 1]
+                    y[c][:, e * C:(e + 1) * C], acc[:, le * C:(le + 1) * C], IDENT, bias=bias[:, c, e:e + 1]
                 )
 
-        def scatter(c, y, lo, hi):
-            nc.vector.tensor_copy(windows[c][:].indirect(offsets[:, lo // 16:hi // 16]), y)
+        def sums_for_vector(g, c):
+            acc = products(g, c)
+            nc.vector.tensor_tensor(
+                y[c][:, g * GROUP:(g + 1) * GROUP].rearrange("p (e s) -> p e s", e=EG),
+                acc[:].rearrange("p (e s) -> p e s", e=EG),
+                bias[:, c, g * EG:(g + 1) * EG].unsqueeze(2).to_broadcast([P, EG, C]),
+                ADD,
+            )
+
+        def scatter_on_scalar(g, c):
+            lo, hi = g * GROUP, (g + 1) * GROUP
+            nc.scalar.activation(windows[c][:].indirect(listed(lo, hi)), y[c][:, lo:hi], COPY)
+
+        def scatter_on_vector(first, last, c):
+            lo, hi = first * GROUP, (last + 1) * GROUP
+            nc.vector.tensor_copy(windows[c][:].indirect(listed(lo, hi)), y[c][:, lo:hi])
+
+        def store(c):
+            nc.sync.dma_start(out=out[c * P:(c + 1) * P, :], in_=windows[c][:])
 
         scale_words = w_scale_rows[:].bitcast(I32)
+        nc.vector.memset(gate_rows[:], 0.0)
         nc.vector.memset(scale_words, 0)
-        nc.gpsimd.memset(gate_rows[:], 0.0)
         make_identity(nc, identity[:])
 
         nc.sync.dma_start(offsets[:], offs)
+        nc.sync.dma_start(out=gate_rows[0:E, :], in_=gate[0, :].rearrange("(e place) -> e place", place=C))
         nc.sync.dma_start(out=planes[0][:, 0:CUT], in_=rows[0, 0][:, 0:CUT])
         nc.scalar.dma_start(out=planes[0][:, CUT:T], in_=rows[0, 0][:, CUT:T])
-        nc.sync.dma_start(out=gate_rows[0:E, :], in_=gate[0, :].rearrange("(e place) -> e place", place=C))
-        load_plane(1)
-        for i in range(2, 2 * PACK):
-            load_plane(i)
+        for i in range(1, PASSES * PACK):
+            nc.sync.dma_start(out=planes[i][:], in_=rows[i // PACK, i % PACK])
         load_weights(0)
         for quad in range(4):
             for a in range(PASSES):
@@ -203,55 +179,54 @@ def tile_moe_pre_lin_bias_kernel(tc, xT, w_words, w_scales, b, gate, offs, out):
                     out=scale_words[32 * quad + 4 * a:32 * quad + 4 * a + 4, :, :],
                     in_=w_scales[:, a, 4 * quad:4 * quad + 4, :].rearrange("e r n -> r e n").bitcast(I32),
                 )
-        bias_rows = b.rearrange("(c p) e -> p c e", p=P)
-        nc.sync.dma_start(out=bias_tiles02[:], in_=bias_rows[:, 0:NT:2, 0:EG])
-        nc.sync.dma_start(out=bias_held[:], in_=bias_rows[:, 1, 0:EG])
-        nc.sync.dma_start(out=bias_rest[:], in_=bias_rows[:, :, EG:E])
+        nc.sync.dma_start(out=bias[:], in_=b.rearrange("(c p) e -> p c e", p=P))
         for g in range(1, GROUPS):
             load_weights(g)
 
-        spread_gate()
-        for t in range(COPIED):
-            nc.vector.tensor_copy(pass0[:, t * S:(t + 1) * S], planes[t][:].indirect(offsets[:]))
-        for t in range(COPIED):
-            for g in range(GROUPS):
-                gate_copied(t, g)
-        for t in range(COPIED, PACK):
-            gather(t, pass0[:, t * S:(t + 1) * S], 0, S)
-        for g in range(GROUPS):
-            round_pass0(g)
-        for i in (4, 5):
-            gather(i, block(ORDER1[i - PACK], 0, GROUPS), 0, S)
-        for i in (6, 7):
-            gather(i, block(ORDER1[i - PACK], 0, 1), 0, GROUP)
-        round_pass1(0)
-        gather(6, block(ORDER1[2], 1, 2), GROUP, S)
-        quantize(0)
-        every = list(range(EG))
-        first = [open_sums(0, 0, every[:2]), open_sums(0, 0, every[2:]), open_sums(0, 1, every)]
-        quantize(1)
-        gather(7, block(ORDER1[3], 1, 2), GROUP, S)
-        for sums in first:
-            close_sums(sums)
-            add_bias(sums)
-        third = open_sums(0, 2, every)
-        close_sums(third)
-        ahead = [open_sums(g, 0, every) for g in range(1, GROUPS)]
-        for g in range(1, GROUPS):
-            round_pass1(g)
-        scatter(0, y_head[0], 0, GROUP)
-        scatter(1, y_head[1], 0, GROUP)
-        quantize(2)
-        add_bias(third)
-        scatter(2, y_head[2], 0, GROUP)
-        for c in range(NT):
-            for g in range(1, GROUPS):
-                sums = ahead[g - 1] if c == 0 else open_sums(g, c, every)
-                close_sums(sums)
-                add_bias(sums)
-            scatter(c, y_rest[c], GROUP, S)
-            if c < NT - 1:
-                nc.sync.dma_start(out=out[c * P:(c + 1) * P, :], in_=windows[c][:])
-            else:
-                nc.sync.dma_start(out=out[c * P:(c + 1) * P, CUT:T], in_=windows[c][:, CUT:T])
-                nc.scalar.dma_start(out=out[c * P:(c + 1) * P, 0:CUT], in_=windows[c][:, 0:CUT])
+        bank = acc_psum.tile([P, GROUP], F32, name="acc")
+        nc.tensor.transpose(bank[:, 0:P], gate_rows[:], identity[:])
+        nc.vector.tensor_copy(gate_cols[:], bank[:, 0:E])
+        for g in range(VECTOR_GROUPS[0]):
+            bank = acc_psum.tile([P, GROUP], F32, name="acc")
+            spread_gate(g, bank)
+            nc.vector.tensor_copy(gates[:, g * GROUP:(g + 1) * GROUP], bank[:])
+        factor = {1: gates[:, GROUP:2 * GROUP]}
+        for g in range(VECTOR_GROUPS[0], GROUPS):
+            bank = gate_psum.tile([P, GROUP], F32, name="gate_bank%d" % g)
+            spread_gate(g, bank)
+            factor[g] = bank[:]
+
+        for t in range(PACK):
+            gather(0, t)
+        round_gated(0, rounded0[:])
+        quantize(0, 0)
+        quantize(0, 1)
+        for t in range(PACK):
+            gather(1, t)
+        round_gated(1, rounded[(1, 0)])
+        quantize(1, 0)
+        for a, g in ((0, 2), (0, 3), (1, 1), (1, 2), (1, 3)):
+            gate_and_round(a, g, factor[g])
+            quantize(a, g)
+
+        for c in (1, 2, 0):
+            sums_for_scalar(0, c)
+            scatter_on_scalar(0, c)
+        sums_for_scalar(1, 0)
+        scatter_on_scalar(1, 0)
+        sums_for_vector(1, 1)
+        sums_for_vector(1, 2)
+        sums_for_vector(2, 1)
+        scatter_on_vector(1, 2, 1)
+        sums_for_vector(2, 2)
+        sums_for_scalar(2, 0)
+        scatter_on_scalar(2, 0)
+        sums_for_vector(3, 2)
+        scatter_on_vector(1, 3, 2)
+        sums_for_scalar(3, 0)
+        scatter_on_scalar(3, 0)
+        store(0)
+        sums_for_scalar(3, 1)
+        scatter_on_scalar(3, 1)
+        store(1)
+        store(2)

@@ -24,48 +24,45 @@ P = 128
 PACK = 4
 PASSES = 2
 NT = N // P
-EG = 3
-GROUP = EG * C
-GROUPS = S // GROUP
-VECTOR_GROUPS = (2, 1)
+CUT = (6 * C, 2 * C)
+LOADS = (0, 2, 6, 9, 12)
 RUN = 4
+BANK = P * RUN
+PIECES = (
+    (0, 0, 256), (0, 256, 768), (1, 0, 256),
+    (0, 768, 1024), (0, 1024, 1536), (1, 256, 768), (1, 768, 1024), (1, 1024, 1536),
+)
 DMA_ALIGN = 256
-CUT = 512
 
 
 def tile_moe_pre_lin_bias_kernel(tc, xT, w_words, w_scales, b, gate, offs, out):
     nc = tc.nc
     with ExitStack() as ctx:
         keep = ctx.enter_context(tc.tile_pool(name="keep", bufs=1))
-        gate_psum = ctx.enter_context(tc.psum_pool(name="gate_psum", bufs=1))
-        acc_psum = ctx.enter_context(tc.psum_pool(name="acc_psum", bufs=6))
+        psum = ctx.enter_context(tc.psum_pool(name="psum", bufs=8))
 
         offsets = keep.tile([P, S // 16], U16, name="offsets")
         planes = [keep.tile([P, T], F32, name="plane%d" % i, align_bytes=DMA_ALIGN) for i in range(PASSES * PACK)]
         identity = keep.tile([P, P], F32, name="identity")
-        gate_rows = keep.tile([P, C], F32, name="gate_rows")
-        gate_cols = keep.tile([P, E], F32, name="gate_cols")
-        gates = keep.tile([P, VECTOR_GROUPS[0] * GROUP], F32, name="gates")
-        cut = [n * GROUP for n in VECTOR_GROUPS]
-        gated = [keep.tile([P, PACK * cut[a]], F32, name="gated%d" % a, align_bytes=64) for a in range(PASSES)]
-        plain = [keep.tile([P, PACK * (S - cut[a])], F32, name="plain%d" % a) for a in range(PASSES)]
-        rounded0 = keep.tile([P, PACK * cut[0]], BF16, name="rounded0", align_bytes=64)
-        width = PACK * GROUP
-        rounded = {(0, g): rounded0[:, g * width:(g + 1) * width] for g in range(2)}
+        gate_cols = keep.tile([P, S // BANK, RUN], F32, name="gate_cols")
+        gates = keep.tile([P, CUT[0]], F32, name="gates")
+        gated = [keep.tile([P, PACK * CUT[a]], F32, name="gated%d" % a, align_bytes=64) for a in range(PASSES)]
+        plain = [keep.tile([P, PACK * (S - CUT[a])], F32, name="plain%d" % a) for a in range(PASSES)]
+        rounded0 = keep.tile([P, PACK * CUT[0]], BF16, name="rounded0", align_bytes=64)
+        rounded1 = keep.tile([P, PACK * CUT[1]], BF16, name="rounded1", align_bytes=64)
         reused = gated[1][:].bitcast(BF16)
-        rounded[(0, 2)] = reused[:, 0:width]
-        rounded[(0, 3)] = reused[:, width:2 * width]
-        for g in range(GROUPS):
-            rounded[(1, g)] = keep.tile([P, width], BF16, name="rounded1%d" % g, align_bytes=64)[:]
-        codes = {
-            (a, g): keep.tile([P, GROUP], U32, name="codes%d%d" % (a, g), align_bytes=64)
-            for a in range(PASSES) for g in range(GROUPS)
+        rounded, codes, scales = {}, {}, {}
+        for a, lo, hi in PIECES:
+            if a == 0 and lo < CUT[0]:
+                rounded[(a, lo)] = rounded0[:, PACK * lo:PACK * hi]
+            else:
+                rounded[(a, lo)] = reused if hi - lo == BANK else rounded1[:]
+            codes[(a, lo)] = keep.tile([P, hi - lo], U32, name="codes%d_%d" % (a, lo), align_bytes=64)
+            scales[(a, lo)] = keep.tile([P, hi - lo], U8, name="scales%d_%d" % (a, lo), align_bytes=64)
+        words = {
+            lo: keep.tile([P, (hi - lo) * PASSES * N], U32, name="words%d" % lo, align_bytes=64)
+            for lo, hi in zip(LOADS, LOADS[1:])
         }
-        scales = {
-            (a, g): keep.tile([P, GROUP], U8, name="scales%d%d" % (a, g), align_bytes=64)
-            for a in range(PASSES) for g in range(GROUPS)
-        }
-        words = [keep.tile([P, EG * PASSES * N], U32, name="words%d" % g, align_bytes=64) for g in range(GROUPS)]
         w_scale_rows = keep.tile([P, E, N], U8, name="w_scale_rows", align_bytes=64)
         bias = keep.tile([P, NT, E], F32, name="bias")
         y = [keep.tile([P, S], F32, name="y%d" % c) for c in range(NT)]
@@ -73,29 +70,37 @@ def tile_moe_pre_lin_bias_kernel(tc, xT, w_words, w_scales, b, gate, offs, out):
 
         rows = xT.rearrange("(a p t) token -> a t p token", a=PASSES, t=PACK)
 
-        def load_weights(g):
-            source = w_words[g * EG:(g + 1) * EG].rearrange("e a p n t -> p (e a) (n t)")
-            nc.sync.dma_start(
-                out=words[g][:].bitcast(I32).rearrange("p (m n) -> p m n", m=EG * PASSES), in_=source.bitcast(I32)
-            )
+        def load_weights(lo, hi):
+            source = w_words[lo:hi].rearrange("e a p n t -> p (e a) (n t)")
+            nc.sync.dma_start(out=words[lo][:].bitcast(I32).rearrange("p (m n) -> p m n", n=N), in_=source.bitcast(I32))
 
-        def spread_gate(g, bank):
-            for le in range(EG):
-                e = g * EG + le
-                nc.tensor.transpose(
-                    bank[:, le * C:(le + 1) * C], gate_cols[:, e:e + 1].to_broadcast([P, P]), identity[:]
+        def load_scale_rows(a):
+            for quad in range(4):
+                nc.sync.dma_start(
+                    out=scale_words[32 * quad + 4 * a:32 * quad + 4 * a + 4, :, :],
+                    in_=w_scales[:, a, 4 * quad:4 * quad + 4, :].rearrange("e r n -> r e n").bitcast(I32),
                 )
+
+        def spread_gate(n):
+            bank = psum.tile([P, RUN, P], F32, name="bank")
+            for i in range(RUN):
+                nc.tensor.transpose(bank[:, i, :], gate_cols[:, n, i:i + 1].to_broadcast([P, P]), identity[:])
+            return bank[:].rearrange("p i line -> p line i")
 
         def listed(lo, hi):
             return offsets[:, lo // 16:hi // 16]
 
-        def gather(a, t):
-            plane = planes[a * PACK + t]
-            rest = S - cut[a]
+        def gather_gated(a, t):
             nc.vector.tensor_tensor(
-                gated[a][:, t * cut[a]:(t + 1) * cut[a]], plane[:].indirect(listed(0, cut[a])), gates[:, 0:cut[a]], MULT
+                gated[a][:, t * CUT[a]:(t + 1) * CUT[a]],
+                planes[a * PACK + t][:].indirect(listed(0, CUT[a])),
+                gates[:, 0:CUT[a]],
+                MULT,
             )
-            nc.scalar.activation(plain[a][:, t * rest:(t + 1) * rest], plane[:].indirect(listed(cut[a], S)), COPY)
+
+        def gather_plain(a, t, lo, hi):
+            at = t * (S - CUT[a]) - CUT[a]
+            nc.scalar.activation(plain[a][:, at + lo:at + hi], planes[a * PACK + t][:].indirect(listed(lo, hi)), COPY)
 
         def woven(target):
             return target.rearrange("p (line i t) -> p line t i", i=RUN, t=PACK)
@@ -106,127 +111,121 @@ def tile_moe_pre_lin_bias_kernel(tc, xT, w_words, w_scales, b, gate, offs, out):
         def round_gated(a, target):
             nc.vector.tensor_copy(woven(target), by_runs(gated[a][:].rearrange("p (t s) -> p t s", t=PACK)))
 
-        def gate_and_round(a, g, factor):
-            lo = g * GROUP - cut[a]
-            source = plain[a][:].rearrange("p (t s) -> p t s", t=PACK)[:, :, lo:lo + GROUP]
-            spread = factor.rearrange("p (line i) -> p line i", i=RUN).unsqueeze(2)
+        def gate_and_round(a, lo, hi):
+            source = plain[a][:].rearrange("p (t s) -> p t s", t=PACK)[:, :, lo - CUT[a]:hi - CUT[a]]
+            if hi <= CUT[0]:
+                factor = gates[:, lo:hi].rearrange("p (line i) -> p line i", i=RUN)
+            else:
+                first = lo % BANK // RUN
+                factor = spread[lo // BANK][:, first:first + (hi - lo) // RUN, :]
             nc.vector.tensor_tensor(
-                woven(rounded[(a, g)]), by_runs(source), spread.to_broadcast([P, GROUP // RUN, PACK, RUN]), MULT
+                woven(rounded[(a, lo)]),
+                by_runs(source),
+                factor.unsqueeze(2).to_broadcast([P, (hi - lo) // RUN, PACK, RUN]),
+                MULT,
             )
 
-        def quantize(a, g):
-            nc.vector.quantize_mx(out=codes[(a, g)][:].bitcast(FP8X4), scales=scales[(a, g)][:], in_=rounded[(a, g)])
+        def quantize(a, lo):
+            nc.vector.quantize_mx(out=codes[(a, lo)][:].bitcast(FP8X4), scales=scales[(a, lo)][:], in_=rounded[(a, lo)])
 
-        def products(g, c):
-            acc = acc_psum.tile([P, GROUP], F32, name="acc")
+        def products(first, end, c):
+            acc = psum.tile([P, (end - first) * C], F32, name="bank")
             for a in range(PASSES):
-                for le in range(EG):
-                    at = (le * PASSES + a) * N + c * P
+                for e in range(first, end):
+                    load = max(lo for lo in LOADS if lo <= e)
+                    at = ((e - load) * PASSES + a) * N + c * P
+                    lo = max(start for piece, start, stop in PIECES if piece == a and start <= e * C)
                     nc.tensor.matmul_mx(
-                        out=acc[:, le * C:(le + 1) * C],
-                        lhsT=words[g][:, at:at + P].bitcast(FP8X4),
-                        lhsT_scale=w_scale_rows[4 * a:P, g * EG + le, c * P:(c + 1) * P],
-                        rhs=codes[(a, g)][:, le * C:(le + 1) * C].bitcast(FP8X4),
-                        rhs_scale=scales[(a, g)][:, le * C:(le + 1) * C],
-                        start=(a == 0 and le == 0),
-                        stop=(a == PASSES - 1 and le == EG - 1),
+                        out=acc[:, (e - first) * C:(e - first + 1) * C],
+                        lhsT=words[load][:, at:at + P].bitcast(FP8X4),
+                        lhsT_scale=w_scale_rows[4 * a:P, e, c * P:(c + 1) * P],
+                        rhs=codes[(a, lo)][:, e * C - lo:(e + 1) * C - lo].bitcast(FP8X4),
+                        rhs_scale=scales[(a, lo)][:, e * C - lo:(e + 1) * C - lo],
+                        start=(a == 0 and e == first),
+                        stop=(a == PASSES - 1 and e == end - 1),
                     )
             return acc
 
-        def sums_for_scalar(g, c):
-            acc = products(g, c)
-            for le in range(EG):
-                e = g * EG + le
+        def finish_on_scalar(first, end, c):
+            acc = products(first, end, c)
+            for e in range(first, end):
                 nc.scalar.activation(
-                    y[c][:, e * C:(e + 1) * C], acc[:, le * C:(le + 1) * C], IDENT, bias=bias[:, c, e:e + 1]
+                    y[c][:, e * C:(e + 1) * C],
+                    acc[:, (e - first) * C:(e - first + 1) * C],
+                    IDENT,
+                    bias=bias[:, c, e:e + 1],
                 )
+            nc.scalar.activation(windows[c][:].indirect(listed(first * C, end * C)), y[c][:, first * C:end * C], COPY)
 
-        def sums_for_vector(g, c):
-            acc = products(g, c)
+        def sums_for_vector(first, end, c):
+            acc = products(first, end, c)
             nc.vector.tensor_tensor(
-                y[c][:, g * GROUP:(g + 1) * GROUP].rearrange("p (e s) -> p e s", e=EG),
-                acc[:].rearrange("p (e s) -> p e s", e=EG),
-                bias[:, c, g * EG:(g + 1) * EG].unsqueeze(2).to_broadcast([P, EG, C]),
+                y[c][:, first * C:end * C].rearrange("p (e s) -> p e s", s=C),
+                acc[:].rearrange("p (e s) -> p e s", s=C),
+                bias[:, c, first:end].unsqueeze(2).to_broadcast([P, end - first, C]),
                 ADD,
             )
 
-        def scatter_on_scalar(g, c):
-            lo, hi = g * GROUP, (g + 1) * GROUP
-            nc.scalar.activation(windows[c][:].indirect(listed(lo, hi)), y[c][:, lo:hi], COPY)
+        def scatter_on_vector(first, end, c):
+            nc.vector.tensor_copy(windows[c][:].indirect(listed(first * C, end * C)), y[c][:, first * C:end * C])
 
-        def scatter_on_vector(first, last, c):
-            lo, hi = first * GROUP, (last + 1) * GROUP
-            nc.vector.tensor_copy(windows[c][:].indirect(listed(lo, hi)), y[c][:, lo:hi])
-
-        def store(c):
-            nc.sync.dma_start(out=out[c * P:(c + 1) * P, :], in_=windows[c][:])
+        def store(c, queue):
+            queue.dma_start(out=out[c * P:(c + 1) * P, :], in_=windows[c][:])
 
         scale_words = w_scale_rows[:].bitcast(I32)
-        nc.vector.memset(gate_rows[:], 0.0)
         nc.vector.memset(scale_words, 0)
         make_identity(nc, identity[:])
 
+        nc.sync.dma_start(out=gate_cols[:], in_=gate[0, :].rearrange("(n p i) -> p n i", p=P, i=RUN))
         nc.sync.dma_start(offsets[:], offs)
-        nc.sync.dma_start(out=gate_rows[0:E, :], in_=gate[0, :].rearrange("(e place) -> e place", place=C))
-        nc.sync.dma_start(out=planes[0][:, 0:CUT], in_=rows[0, 0][:, 0:CUT])
-        nc.scalar.dma_start(out=planes[0][:, CUT:T], in_=rows[0, 0][:, CUT:T])
-        for i in range(1, PASSES * PACK):
+        for i in range(PASSES * PACK):
             nc.sync.dma_start(out=planes[i][:], in_=rows[i // PACK, i % PACK])
-        load_weights(0)
-        for quad in range(4):
-            for a in range(PASSES):
-                nc.sync.dma_start(
-                    out=scale_words[32 * quad + 4 * a:32 * quad + 4 * a + 4, :, :],
-                    in_=w_scales[:, a, 4 * quad:4 * quad + 4, :].rearrange("e r n -> r e n").bitcast(I32),
-                )
+        load_scale_rows(0)
+        load_weights(LOADS[0], LOADS[1])
+        load_scale_rows(1)
         nc.sync.dma_start(out=bias[:], in_=b.rearrange("(c p) e -> p c e", p=P))
-        for g in range(1, GROUPS):
-            load_weights(g)
+        for lo, hi in zip(LOADS[1:], LOADS[2:]):
+            load_weights(lo, hi)
 
-        bank = acc_psum.tile([P, GROUP], F32, name="acc")
-        nc.tensor.transpose(bank[:, 0:P], gate_rows[:], identity[:])
-        nc.vector.tensor_copy(gate_cols[:], bank[:, 0:E])
-        for g in range(VECTOR_GROUPS[0]):
-            bank = acc_psum.tile([P, GROUP], F32, name="acc")
-            spread_gate(g, bank)
-            nc.vector.tensor_copy(gates[:, g * GROUP:(g + 1) * GROUP], bank[:])
-        factor = {1: gates[:, GROUP:2 * GROUP]}
-        for g in range(VECTOR_GROUPS[0], GROUPS):
-            bank = gate_psum.tile([P, GROUP], F32, name="gate_bank%d" % g)
-            spread_gate(g, bank)
-            factor[g] = bank[:]
+        spread = [spread_gate(n) for n in range(S // BANK)]
+        by_line = gates[:].rearrange("p (line i) -> p line i", i=RUN)
+        nc.vector.tensor_copy(by_line[:, 0:P, :], spread[0])
+        nc.vector.tensor_copy(by_line[:, P:, :], spread[1][:, 0:(CUT[0] - BANK) // RUN, :])
 
         for t in range(PACK):
-            gather(0, t)
+            gather_gated(0, t)
+            gather_plain(0, t, CUT[0], S)
         round_gated(0, rounded0[:])
         quantize(0, 0)
-        quantize(0, 1)
-        for t in range(PACK):
-            gather(1, t)
+        quantize(0, CUT[1])
+        for t in range(PACK - 1):
+            gather_gated(1, t)
+            gather_plain(1, t, CUT[1], S)
+        gather_gated(1, PACK - 1)
+        gather_plain(1, PACK - 1, CUT[1], CUT[0])
+        gather_plain(1, PACK - 1, CUT[0], S)
         round_gated(1, rounded[(1, 0)])
         quantize(1, 0)
-        for a, g in ((0, 2), (0, 3), (1, 1), (1, 2), (1, 3)):
-            gate_and_round(a, g, factor[g])
-            quantize(a, g)
+        for a, lo, hi in PIECES[3:]:
+            gate_and_round(a, lo, hi)
+            quantize(a, lo)
 
         for c in (1, 2, 0):
-            sums_for_scalar(0, c)
-            scatter_on_scalar(0, c)
-        sums_for_scalar(1, 0)
-        scatter_on_scalar(1, 0)
-        sums_for_vector(1, 1)
-        sums_for_vector(1, 2)
-        sums_for_vector(2, 1)
-        scatter_on_vector(1, 2, 1)
-        sums_for_vector(2, 2)
-        sums_for_scalar(2, 0)
-        scatter_on_scalar(2, 0)
-        sums_for_vector(3, 2)
-        scatter_on_vector(1, 3, 2)
-        sums_for_scalar(3, 0)
-        scatter_on_scalar(3, 0)
-        store(0)
-        sums_for_scalar(3, 1)
-        scatter_on_scalar(3, 1)
-        store(1)
-        store(2)
+            finish_on_scalar(0, 2, c)
+        finish_on_scalar(2, 5, 0)
+        sums_for_vector(2, 6, 2)
+        scatter_on_vector(2, 6, 2)
+        sums_for_vector(2, 6, 1)
+        sums_for_vector(6, 7, 1)
+        scatter_on_vector(2, 7, 1)
+        sums_for_vector(6, 9, 2)
+        sums_for_vector(9, 12, 2)
+        scatter_on_vector(6, 12, 2)
+        store(2, nc.sync)
+        finish_on_scalar(5, 8, 0)
+        finish_on_scalar(8, 10, 0)
+        finish_on_scalar(10, 12, 0)
+        store(0, nc.scalar)
+        finish_on_scalar(7, 10, 1)
+        finish_on_scalar(10, 12, 1)
+        store(1, nc.scalar)

@@ -173,6 +173,10 @@ def tile_moe_pre_lin_bias_kernel(tc, xT, w_words, w_scales, b, gate, offs, out):
             queue.dma_start(out=out[c * P:(c + 1) * P, :], in_=windows[c][:])
 
         scale_words = w_scale_rows[:].bitcast(I32)
+        zero = keep.tile([P, 1], F32, name="zero")
+        unread = keep.tile([P, 1], F32, name="unread")
+        nc.gpsimd.memset(zero[:], 0.0)
+        nc.scalar.activation(unread[:], zero[:], COPY)
         nc.vector.memset(scale_words, 0)
         make_identity(nc, identity[:])
 

@@ -74,12 +74,13 @@ def tile_moe_pre_lin_bias_kernel(tc, xT, w_words, w_scales, b, gate, offs, out):
             source = w_words[lo:hi].rearrange("e a p n t -> p (e a) (n t)")
             nc.sync.dma_start(out=words[lo][:].bitcast(I32).rearrange("p (m n) -> p m n", n=N), in_=source.bitcast(I32))
 
-        def load_scale_rows(a):
-            for quad in range(4):
-                nc.sync.dma_start(
-                    out=scale_words[32 * quad + 4 * a:32 * quad + 4 * a + 4, :, :],
-                    in_=w_scales[:, a, 4 * quad:4 * quad + 4, :].rearrange("e r n -> r e n").bitcast(I32),
-                )
+        def load_scale_rows(first, end):
+            for r in range(first, end):
+                for a in range(PASSES):
+                    nc.sync.dma_start(
+                        out=scale_words[4 * a + r:P:32, :, :],
+                        in_=w_scales[:, a, r:16:4, :].rearrange("e q n -> q e n").bitcast(I32),
+                    )
 
         def spread_gate(n):
             bank = psum.tile([P, RUN, P], F32, name="bank")
@@ -184,9 +185,9 @@ def tile_moe_pre_lin_bias_kernel(tc, xT, w_words, w_scales, b, gate, offs, out):
         nc.sync.dma_start(offsets[:], offs)
         for i in range(PASSES * PACK):
             nc.sync.dma_start(out=planes[i][:], in_=rows[i // PACK, i % PACK])
-        load_scale_rows(0)
+        load_scale_rows(0, 2)
         load_weights(LOADS[0], LOADS[1])
-        load_scale_rows(1)
+        load_scale_rows(2, 4)
         nc.sync.dma_start(out=bias[:], in_=b.rearrange("(c p) e -> p c e", p=P))
         for lo, hi in zip(LOADS[1:], LOADS[2:]):
             load_weights(lo, hi)

@@ -63,7 +63,8 @@ def tile_moe_pre_lin_bias_kernel(tc, xT, w_words, w_scales, b, gate, offs, out):
             lo: keep.tile([P, (hi - lo) * PASSES * N], U32, name="words%d" % lo, align_bytes=64)
             for lo, hi in zip(LOADS, LOADS[1:])
         }
-        w_scale_rows = keep.tile([P, E, N], U8, name="w_scale_rows", align_bytes=64)
+        first_scale_rows = keep.tile([P, N], U8, name="first_scale_rows", align_bytes=64)
+        w_scale_rows = keep.tile([P, E - LOADS[1], N], U8, name="w_scale_rows", align_bytes=64)
         bias = keep.tile([P, NT, E], F32, name="bias")
         y = [keep.tile([P, S], F32, name="y%d" % c) for c in range(NT)]
         windows = [keep.tile([P, T], F32, name="window%d" % c, align_bytes=DMA_ALIGN) for c in range(NT)]
@@ -74,13 +75,22 @@ def tile_moe_pre_lin_bias_kernel(tc, xT, w_words, w_scales, b, gate, offs, out):
             source = w_words[lo:hi].rearrange("e a p n t -> p (e a) (n t)")
             nc.sync.dma_start(out=words[lo][:].bitcast(I32).rearrange("p (m n) -> p m n", n=N), in_=source.bitcast(I32))
 
-        def load_scale_rows(first, end):
-            for r in range(first, end):
-                for a in range(PASSES):
-                    nc.sync.dma_start(
-                        out=scale_words[4 * a + r:P:32, :, :],
-                        in_=w_scales[:, a, r:16:4, :].rearrange("e q n -> q e n").bitcast(I32),
-                    )
+        def load_first_scale_rows(quad):
+            nc.sync.dma_start(
+                out=first_scale_rows[32 * quad:32 * quad + 16, :].bitcast(I32),
+                in_=w_scales[0:LOADS[1], :, 4 * quad:4 * quad + 4, :].rearrange("e a r n -> (e a) r n").bitcast(I32),
+            )
+
+        def load_scale_rows(r, a):
+            nc.sync.dma_start(
+                out=scale_words[4 * a + r:P:32, :, :],
+                in_=w_scales[LOADS[1]:E, a, r:16:4, :].rearrange("e q n -> q e n").bitcast(I32),
+            )
+
+        def weight_scales(e, a, c):
+            if e < LOADS[1]:
+                return first_scale_rows[4 * (e * PASSES + a):P, c * P:(c + 1) * P]
+            return w_scale_rows[4 * a:P, e - LOADS[1], c * P:(c + 1) * P]
 
         def spread_gate(n):
             bank = psum.tile([P, RUN, P], F32, name="bank")
@@ -139,7 +149,7 @@ def tile_moe_pre_lin_bias_kernel(tc, xT, w_words, w_scales, b, gate, offs, out):
                     nc.tensor.matmul_mx(
                         out=acc[:, (e - first) * C:(e - first + 1) * C],
                         lhsT=words[load][:, at:at + P].bitcast(FP8X4),
-                        lhsT_scale=w_scale_rows[4 * a:P, e, c * P:(c + 1) * P],
+                        lhsT_scale=weight_scales(e, a, c),
                         rhs=codes[(a, lo)][:, e * C - lo:(e + 1) * C - lo].bitcast(FP8X4),
                         rhs_scale=scales[(a, lo)][:, e * C - lo:(e + 1) * C - lo],
                         start=(a == 0 and e == first),
@@ -179,16 +189,20 @@ def tile_moe_pre_lin_bias_kernel(tc, xT, w_words, w_scales, b, gate, offs, out):
         nc.gpsimd.memset(zero[:], 0.0)
         nc.scalar.activation(unread[:], zero[:], COPY)
         nc.vector.memset(scale_words, 0)
+        nc.vector.memset(first_scale_rows[:].bitcast(I32), 0)
         make_identity(nc, identity[:])
 
         nc.sync.dma_start(out=gate_cols[:], in_=gate[0, :].rearrange("(n p i) -> p n i", p=P, i=RUN))
         nc.sync.dma_start(offsets[:], offs)
         for i in range(PASSES * PACK):
             nc.sync.dma_start(out=planes[i][:], in_=rows[i // PACK, i % PACK])
-        load_scale_rows(0, 2)
+            if i >= PACK:
+                load_first_scale_rows(i - PACK)
         load_weights(LOADS[0], LOADS[1])
-        load_scale_rows(2, 4)
         nc.sync.dma_start(out=bias[:], in_=b.rearrange("(c p) e -> p c e", p=P))
+        for r in range(4):
+            for a in range(PASSES):
+                load_scale_rows(r, a)
         for lo, hi in zip(LOADS[1:], LOADS[2:]):
             load_weights(lo, hi)
 

@@ -28,9 +28,15 @@ CUT = (6 * C, 2 * C)
 LOADS = (0, 2, 6, 9, 12)
 RUN = 4
 BANK = P * RUN
-PIECES = (
-    (0, 0, 256), (0, 256, 768), (1, 0, 256),
-    (0, 768, 1024), (0, 1024, 1536), (1, 256, 768), (1, 768, 1024), (1, 1024, 1536),
+UNIT = 2 * C
+CALLS = (
+    (0, (0, 0, 256)),
+    (256, (0, 256, 768)),
+    (0, (1, 0, 256), (0, 768, 1024)),
+    (0, (0, 1024, 1536)),
+    (0, (1, 256, 768)),
+    (512, (1, 768, 1024)),
+    (384, (1, 1024, 1536)),
 )
 DMA_ALIGN = 256
 
@@ -39,26 +45,36 @@ def tile_moe_pre_lin_bias_kernel(tc, xT, w_words, w_scales, b, gate, offs, out):
     nc = tc.nc
     with ExitStack() as ctx:
         keep = ctx.enter_context(tc.tile_pool(name="keep", bufs=1))
-        psum = ctx.enter_context(tc.psum_pool(name="psum", bufs=8))
+        shared = ctx.enter_context(tc.tile_pool(name="shared", bufs=1))
+        held = ctx.enter_context(tc.psum_pool(name="held", bufs=1))
+        psum = ctx.enter_context(tc.psum_pool(name="psum", bufs=6))
 
         offsets = keep.tile([P, S // 16], U16, name="offsets")
         planes = [keep.tile([P, T], F32, name="plane%d" % i, align_bytes=DMA_ALIGN) for i in range(PASSES * PACK)]
         identity = keep.tile([P, P], F32, name="identity")
         gate_cols = keep.tile([P, S // BANK, RUN], F32, name="gate_cols")
         gates = keep.tile([P, CUT[0]], F32, name="gates")
-        gated = [keep.tile([P, PACK * CUT[a]], F32, name="gated%d" % a, align_bytes=64) for a in range(PASSES)]
+        more_gates = keep.tile([P, 2 * UNIT], F32, name="more_gates")
+        gated = keep.tile([P, PACK * CUT[0]], F32, name="gated")
+        ahead = keep.tile([P, PACK * CUT[1]], F32, name="ahead")
         plain = [keep.tile([P, PACK * (S - CUT[a])], F32, name="plain%d" % a) for a in range(PASSES)]
-        rounded0 = keep.tile([P, PACK * CUT[0]], BF16, name="rounded0", align_bytes=64)
-        rounded1 = keep.tile([P, PACK * CUT[1]], BF16, name="rounded1", align_bytes=64)
-        reused = gated[1][:].bitcast(BF16)
-        rounded, codes, scales = {}, {}, {}
-        for a, lo, hi in PIECES:
-            if a == 0 and lo < CUT[0]:
-                rounded[(a, lo)] = rounded0[:, PACK * lo:PACK * hi]
+        rounded = keep.tile([P, PACK * 7 * C], BF16, name="rounded", align_bytes=64)
+        widths = [sum(hi - lo for a, lo, hi in call[1:]) for call in CALLS]
+        early = [shared.tile([P, UNIT], F32, name="early%d" % n, align_bytes=64, offset=n * 4 * BANK) for n in range(2)]
+        codes = []
+        for q, w in enumerate(widths):
+            if q in (3, 6):
+                codes.append(shared.tile([P, w], U32, name="codes%d" % q, align_bytes=64, offset=q // 6 * 4 * BANK))
             else:
-                rounded[(a, lo)] = reused if hi - lo == BANK else rounded1[:]
-            codes[(a, lo)] = keep.tile([P, hi - lo], U32, name="codes%d_%d" % (a, lo), align_bytes=64)
-            scales[(a, lo)] = keep.tile([P, hi - lo], U8, name="scales%d_%d" % (a, lo), align_bytes=64)
+                codes.append(keep.tile([P, w], U32, name="codes%d" % q, align_bytes=64))
+        scales = [keep.tile([P, w], U8, name="scales%d" % q, align_bytes=64) for q, w in enumerate(widths)]
+        place = {}
+        for q, call in enumerate(CALLS):
+            column = 0
+            for a, lo, hi in call[1:]:
+                for slot in range(lo, hi, C):
+                    place[(a, slot)] = (q, column)
+                    column += C
         words = {
             lo: keep.tile([P, (hi - lo) * PASSES * N], U32, name="words%d" % lo, align_bytes=64)
             for lo, hi in zip(LOADS, LOADS[1:])
@@ -66,7 +82,9 @@ def tile_moe_pre_lin_bias_kernel(tc, xT, w_words, w_scales, b, gate, offs, out):
         first_scale_rows = keep.tile([P, N], U8, name="first_scale_rows", align_bytes=64)
         w_scale_rows = keep.tile([P, E - LOADS[1], N], U8, name="w_scale_rows", align_bytes=64)
         bias = keep.tile([P, NT, E], F32, name="bias")
-        y = [keep.tile([P, S], F32, name="y%d" % c) for c in range(NT)]
+        y = [keep.tile([P, S], F32, name="y%d" % c) for c in range(NT - 1)]
+        late1 = plain[1][:, 2 * UNIT:5 * UNIT]
+        late2 = plain[1][:, 12 * UNIT:16 * UNIT]
         windows = [keep.tile([P, T], F32, name="window%d" % c, align_bytes=DMA_ALIGN) for c in range(NT)]
 
         rows = xT.rearrange("(a p t) token -> a t p token", a=PASSES, t=PACK)
@@ -92,8 +110,7 @@ def tile_moe_pre_lin_bias_kernel(tc, xT, w_words, w_scales, b, gate, offs, out):
                 return first_scale_rows[4 * (e * PASSES + a):P, c * P:(c + 1) * P]
             return w_scale_rows[4 * a:P, e - LOADS[1], c * P:(c + 1) * P]
 
-        def spread_gate(n):
-            bank = psum.tile([P, RUN, P], F32, name="bank")
+        def spread_gate(n, bank):
             for i in range(RUN):
                 nc.tensor.transpose(bank[:, i, :], gate_cols[:, n, i:i + 1].to_broadcast([P, P]), identity[:])
             return bank[:].rearrange("p i line -> p line i")
@@ -101,13 +118,13 @@ def tile_moe_pre_lin_bias_kernel(tc, xT, w_words, w_scales, b, gate, offs, out):
         def listed(lo, hi):
             return offsets[:, lo // 16:hi // 16]
 
-        def gather_gated(a, t):
+        def gather_gated(t):
             nc.vector.tensor_tensor(
-                gated[a][:, t * CUT[a]:(t + 1) * CUT[a]],
-                planes[a * PACK + t][:].indirect(listed(0, CUT[a])),
-                gates[:, 0:CUT[a]],
-                MULT,
+                gated[:, t * CUT[0]:(t + 1) * CUT[0]], planes[t][:].indirect(listed(0, CUT[0])), gates[:], MULT
             )
+
+        def gather_ahead(t):
+            nc.vector.tensor_copy(ahead[:, t * CUT[1]:(t + 1) * CUT[1]], planes[PACK + t][:].indirect(listed(0, CUT[1])))
 
         def gather_plain(a, t, lo, hi):
             at = t * (S - CUT[a]) - CUT[a]
@@ -119,25 +136,43 @@ def tile_moe_pre_lin_bias_kernel(tc, xT, w_words, w_scales, b, gate, offs, out):
         def by_runs(source):
             return source.rearrange("p t (line i) -> p line t i", i=RUN)
 
-        def round_gated(a, target):
-            nc.vector.tensor_copy(woven(target), by_runs(gated[a][:].rearrange("p (t s) -> p t s", t=PACK)))
+        def by_plane(tile):
+            return tile[:].rearrange("p (t s) -> p t s", t=PACK)
 
-        def gate_and_round(a, lo, hi):
-            source = plain[a][:].rearrange("p (t s) -> p t s", t=PACK)[:, :, lo - CUT[a]:hi - CUT[a]]
-            if hi <= CUT[0]:
-                factor = gates[:, lo:hi].rearrange("p (line i) -> p line i", i=RUN)
-            else:
-                first = lo % BANK // RUN
-                factor = spread[lo // BANK][:, first:first + (hi - lo) // RUN, :]
+        def ungated(a, lo, hi):
+            if lo < CUT[a]:
+                return by_plane(ahead)[:, :, lo:hi]
+            return by_plane(plain[a])[:, :, lo - CUT[a]:hi - CUT[a]]
+
+        def target(a, lo, hi):
+            q, column = place[(a, lo)]
+            at = CALLS[q][0] + column
+            return rounded[:, PACK * at:PACK * (at + hi - lo)]
+
+        def gate_on_vector(a, lo, hi):
+            first = lo % BANK // RUN
+            factor = spread[lo // BANK][:, first:first + (hi - lo) // RUN, :]
             nc.vector.tensor_tensor(
-                woven(rounded[(a, lo)]),
-                by_runs(source),
+                woven(target(a, lo, hi)),
+                by_runs(ungated(a, lo, hi)),
                 factor.unsqueeze(2).to_broadcast([P, (hi - lo) // RUN, PACK, RUN]),
                 MULT,
             )
 
-        def quantize(a, lo):
-            nc.vector.quantize_mx(out=codes[(a, lo)][:].bitcast(FP8X4), scales=scales[(a, lo)][:], in_=rounded[(a, lo)])
+        def gate_on_gpsimd(a, lo, hi):
+            factor = gates[:, lo:hi] if hi <= CUT[0] else more_gates[:, lo - CUT[0]:hi - CUT[0]]
+            nc.gpsimd.tensor_tensor(
+                target(a, lo, hi).rearrange("p (s t) -> p s t", t=PACK),
+                ungated(a, lo, hi).rearrange("p t s -> p s t"),
+                factor.unsqueeze(2).to_broadcast([P, hi - lo, PACK]),
+                MULT,
+            )
+
+        def quantize(q):
+            at = CALLS[q][0]
+            nc.vector.quantize_mx(
+                out=codes[q][:].bitcast(FP8X4), scales=scales[q][:], in_=rounded[:, PACK * at:PACK * (at + widths[q])]
+            )
 
         def products(first, end, c):
             acc = psum.tile([P, (end - first) * C], F32, name="bank")
@@ -145,19 +180,19 @@ def tile_moe_pre_lin_bias_kernel(tc, xT, w_words, w_scales, b, gate, offs, out):
                 for e in range(first, end):
                     load = max(lo for lo in LOADS if lo <= e)
                     at = ((e - load) * PASSES + a) * N + c * P
-                    lo = max(start for piece, start, stop in PIECES if piece == a and start <= e * C)
+                    q, column = place[(a, e * C)]
                     nc.tensor.matmul_mx(
                         out=acc[:, (e - first) * C:(e - first + 1) * C],
                         lhsT=words[load][:, at:at + P].bitcast(FP8X4),
                         lhsT_scale=weight_scales(e, a, c),
-                        rhs=codes[(a, lo)][:, e * C - lo:(e + 1) * C - lo].bitcast(FP8X4),
-                        rhs_scale=scales[(a, lo)][:, e * C - lo:(e + 1) * C - lo],
+                        rhs=codes[q][:, column:column + C].bitcast(FP8X4),
+                        rhs_scale=scales[q][:, column:column + C],
                         start=(a == 0 and e == first),
                         stop=(a == PASSES - 1 and e == end - 1),
                     )
             return acc
 
-        def finish_on_scalar(first, end, c):
+        def sums_for_scalar(first, end, c):
             acc = products(first, end, c)
             for e in range(first, end):
                 nc.scalar.activation(
@@ -166,19 +201,25 @@ def tile_moe_pre_lin_bias_kernel(tc, xT, w_words, w_scales, b, gate, offs, out):
                     IDENT,
                     bias=bias[:, c, e:e + 1],
                 )
-            nc.scalar.activation(windows[c][:].indirect(listed(first * C, end * C)), y[c][:, first * C:end * C], COPY)
 
-        def sums_for_vector(first, end, c):
+        def scatter_on_scalar(lo, hi, c):
+            nc.scalar.activation(windows[c][:].indirect(listed(lo, hi)), y[c][:, lo:hi], COPY)
+
+        def finish_on_scalar(first, end, c):
+            sums_for_scalar(first, end, c)
+            scatter_on_scalar(first * C, end * C, c)
+
+        def sums_for_vector(first, end, c, home):
             acc = products(first, end, c)
             nc.vector.tensor_tensor(
-                y[c][:, first * C:end * C].rearrange("p (e s) -> p e s", s=C),
+                home.rearrange("p (e s) -> p e s", s=C),
                 acc[:].rearrange("p (e s) -> p e s", s=C),
                 bias[:, c, first:end].unsqueeze(2).to_broadcast([P, end - first, C]),
                 ADD,
             )
 
-        def scatter_on_vector(first, end, c):
-            nc.vector.tensor_copy(windows[c][:].indirect(listed(first * C, end * C)), y[c][:, first * C:end * C])
+        def scatter_on_vector(first, end, c, home):
+            nc.vector.tensor_copy(windows[c][:].indirect(listed(first * C, end * C)), home)
 
         def store(c, queue):
             queue.dma_start(out=out[c * P:(c + 1) * P, :], in_=windows[c][:])
@@ -196,8 +237,10 @@ def tile_moe_pre_lin_bias_kernel(tc, xT, w_words, w_scales, b, gate, offs, out):
         nc.sync.dma_start(offsets[:], offs)
         for i in range(PASSES * PACK):
             nc.sync.dma_start(out=planes[i][:], in_=rows[i // PACK, i % PACK])
-            if i >= PACK:
-                load_first_scale_rows(i - PACK)
+            if i == PACK:
+                nc.sync.dma_start(out=more_gates[:], in_=gate[0:P, CUT[0]:CUT[0] + 2 * UNIT])
+        for quad in range(4):
+            load_first_scale_rows(quad)
         load_weights(LOADS[0], LOADS[1])
         nc.sync.dma_start(out=bias[:], in_=b.rearrange("(c p) e -> p c e", p=P))
         for r in range(4):
@@ -206,45 +249,60 @@ def tile_moe_pre_lin_bias_kernel(tc, xT, w_words, w_scales, b, gate, offs, out):
         for lo, hi in zip(LOADS[1:], LOADS[2:]):
             load_weights(lo, hi)
 
-        spread = [spread_gate(n) for n in range(S // BANK)]
+        spread = [spread_gate(0, psum.tile([P, RUN, P], F32, name="bank"))]
+        spread.extend(spread_gate(n, held.tile([P, RUN, P], F32, name="gate_bank%d" % n)) for n in (1, 2))
         by_line = gates[:].rearrange("p (line i) -> p line i", i=RUN)
         nc.vector.tensor_copy(by_line[:, 0:P, :], spread[0])
         nc.vector.tensor_copy(by_line[:, P:, :], spread[1][:, 0:(CUT[0] - BANK) // RUN, :])
 
         for t in range(PACK):
-            gather_gated(0, t)
+            gather_gated(t)
             gather_plain(0, t, CUT[0], S)
-        round_gated(0, rounded0[:])
-        quantize(0, 0)
-        quantize(0, CUT[1])
+        nc.vector.tensor_copy(woven(rounded[:, 0:PACK * CUT[0]]), by_runs(by_plane(gated)))
+        quantize(0)
+        quantize(1)
+        gate_on_gpsimd(0, 768, 1024)
         for t in range(PACK - 1):
-            gather_gated(1, t)
+            gather_ahead(t)
             gather_plain(1, t, CUT[1], S)
-        gather_gated(1, PACK - 1)
+        gather_ahead(PACK - 1)
         gather_plain(1, PACK - 1, CUT[1], CUT[0])
         gather_plain(1, PACK - 1, CUT[0], S)
-        round_gated(1, rounded[(1, 0)])
-        quantize(1, 0)
-        for a, lo, hi in PIECES[3:]:
-            gate_and_round(a, lo, hi)
-            quantize(a, lo)
+        gate_on_vector(1, 0, 256)
+        quantize(2)
 
-        for c in (1, 2, 0):
+        gate_on_gpsimd(0, 1024, 1280)
+        gate_on_vector(0, 1280, 1536)
+        sums_for_vector(0, 2, 2, early[0][:])
+        scatter_on_vector(0, 2, 2, early[0][:])
+        for c in (1, 0):
             finish_on_scalar(0, 2, c)
+        quantize(3)
+
+        gate_on_gpsimd(1, 256, 512)
+        gate_on_vector(1, 512, 1024)
+        quantize(4)
+        quantize(5)
+
+        gate_on_gpsimd(1, 1024, 1280)
+        gate_on_vector(1, 1280, 1536)
         finish_on_scalar(2, 5, 0)
-        sums_for_vector(2, 6, 2)
-        scatter_on_vector(2, 6, 2)
-        sums_for_vector(2, 6, 1)
-        sums_for_vector(6, 7, 1)
-        scatter_on_vector(2, 7, 1)
-        sums_for_vector(6, 9, 2)
-        sums_for_vector(9, 12, 2)
-        scatter_on_vector(6, 12, 2)
-        store(2, nc.sync)
+        sums_for_vector(2, 4, 2, early[1][:])
+        scatter_on_vector(2, 4, 2, early[1][:])
+        quantize(6)
+
         finish_on_scalar(5, 8, 0)
+        sums_for_vector(2, 6, 1, late1[:, 0:4 * C])
+        sums_for_vector(6, 8, 1, late1[:, 4 * C:])
+        sums_for_vector(4, 8, 2, late2[:, 0:4 * C])
+        scatter_on_vector(2, 8, 1, late1)
         finish_on_scalar(8, 10, 0)
+        sums_for_vector(8, 12, 2, late2[:, 4 * C:])
+        scatter_on_vector(4, 8, 2, late2[:, 0:4 * C])
+        scatter_on_vector(8, 12, 2, late2[:, 4 * C:])
+        store(2, nc.sync)
         finish_on_scalar(10, 12, 0)
         store(0, nc.scalar)
-        finish_on_scalar(7, 10, 1)
+        finish_on_scalar(8, 10, 1)
         finish_on_scalar(10, 12, 1)
         store(1, nc.scalar)

@@ -30,14 +30,15 @@ RUN = 4
 BANK = P * RUN
 UNIT = 2 * C
 CALLS = (
-    (0, (0, 0, 256)),
-    (256, (0, 256, 768)),
-    (0, (1, 0, 256), (0, 768, 1024)),
-    (0, (0, 1024, 1536)),
-    (0, (1, 256, 768)),
-    (512, (1, 768, 1024)),
-    (384, (1, 1024, 1536)),
+    (128, (0, 0, 256)),
+    (384, (0, 256, 768)),
+    (128, (1, 0, 256), (0, 768, 1024)),
+    (0, (1, 512, 768), (1, 256, 512)),
+    (512, (0, 1024, 1536)),
+    (384, (1, 768, 1024), (1, 1280, 1536)),
+    (512, (1, 1024, 1280)),
 )
+SHARED = 1344
 DMA_ALIGN = 256
 
 
@@ -47,7 +48,7 @@ def tile_moe_pre_lin_bias_kernel(tc, xT, w_words, w_scales, b, gate, offs, out):
         keep = ctx.enter_context(tc.tile_pool(name="keep", bufs=1))
         shared = ctx.enter_context(tc.tile_pool(name="shared", bufs=1))
         held = ctx.enter_context(tc.psum_pool(name="held", bufs=1))
-        psum = ctx.enter_context(tc.psum_pool(name="psum", bufs=6))
+        psum = ctx.enter_context(tc.psum_pool(name="psum", bufs=7))
 
         offsets = keep.tile([P, S // 16], U16, name="offsets")
         planes = [keep.tile([P, T], F32, name="plane%d" % i, align_bytes=DMA_ALIGN) for i in range(PASSES * PACK)]
@@ -56,15 +57,23 @@ def tile_moe_pre_lin_bias_kernel(tc, xT, w_words, w_scales, b, gate, offs, out):
         gates = keep.tile([P, CUT[0]], F32, name="gates")
         more_gates = keep.tile([P, 2 * UNIT], F32, name="more_gates")
         gated = keep.tile([P, PACK * CUT[0]], F32, name="gated")
-        ahead = keep.tile([P, PACK * CUT[1]], F32, name="ahead")
-        plain = [keep.tile([P, PACK * (S - CUT[a])], F32, name="plain%d" % a) for a in range(PASSES)]
-        rounded = keep.tile([P, PACK * 7 * C], BF16, name="rounded", align_bytes=64)
+        ranges = ((0, CUT[0], S), (1, CUT[1], CUT[0]), (1, CUT[0], S))
+        plain = {
+            (a, lo): keep.tile([P, PACK * (hi - lo)], F32, name="plain%d_%d" % (a, lo))[:] for a, lo, hi in ranges
+        }
+        plain[(1, 0)] = plain[(1, CUT[0])][:, PACK * UNIT:2 * PACK * UNIT]
+        ranges = ranges + ((1, 0, CUT[1]),)
+        rounded = keep.tile([P, PACK * 8 * C], BF16, name="rounded", align_bytes=64)
         widths = [sum(hi - lo for a, lo, hi in call[1:]) for call in CALLS]
-        early = [shared.tile([P, UNIT], F32, name="early%d" % n, align_bytes=64, offset=n * 4 * BANK) for n in range(2)]
+        as_sums = rounded[:].bitcast(F32)
+        early = {
+            c: shared.tile([P, BANK], F32, name="early%d" % c, align_bytes=64, offset=at) for c, at in ((2, 1024), (1, 2048))
+        }
+        late = [as_sums[:, (4 + n) * UNIT:(5 + n) * UNIT] for n in range(2)]
         codes = []
         for q, w in enumerate(widths):
-            if q in (3, 6):
-                codes.append(shared.tile([P, w], U32, name="codes%d" % q, align_bytes=64, offset=q // 6 * 4 * BANK))
+            if q == 5:
+                codes.append(shared.tile([P, w], U32, name="codes%d" % q, align_bytes=64, offset=0))
             else:
                 codes.append(keep.tile([P, w], U32, name="codes%d" % q, align_bytes=64))
         scales = [keep.tile([P, w], U8, name="scales%d" % q, align_bytes=64) for q, w in enumerate(widths)]
@@ -82,9 +91,7 @@ def tile_moe_pre_lin_bias_kernel(tc, xT, w_words, w_scales, b, gate, offs, out):
         first_scale_rows = keep.tile([P, N], U8, name="first_scale_rows", align_bytes=64)
         w_scale_rows = keep.tile([P, E - LOADS[1], N], U8, name="w_scale_rows", align_bytes=64)
         bias = keep.tile([P, NT, E], F32, name="bias")
-        y = [keep.tile([P, S], F32, name="y%d" % c) for c in range(NT - 1)]
-        late1 = plain[1][:, 2 * UNIT:5 * UNIT]
-        late2 = plain[1][:, 12 * UNIT:16 * UNIT]
+        y = [keep.tile([P, S], F32, name="y%d" % c) for c in range(NT)]
         windows = [keep.tile([P, T], F32, name="window%d" % c, align_bytes=DMA_ALIGN) for c in range(NT)]
 
         rows = xT.rearrange("(a p t) token -> a t p token", a=PASSES, t=PACK)
@@ -124,11 +131,12 @@ def tile_moe_pre_lin_bias_kernel(tc, xT, w_words, w_scales, b, gate, offs, out):
             )
 
         def gather_ahead(t):
-            nc.vector.tensor_copy(ahead[:, t * CUT[1]:(t + 1) * CUT[1]], planes[PACK + t][:].indirect(listed(0, CUT[1])))
+            target = plain[(1, 0)][:, t * CUT[1]:(t + 1) * CUT[1]]
+            nc.vector.tensor_copy(target, planes[PACK + t][:].indirect(listed(0, CUT[1])))
 
         def gather_plain(a, t, lo, hi):
-            at = t * (S - CUT[a]) - CUT[a]
-            nc.scalar.activation(plain[a][:, at + lo:at + hi], planes[a * PACK + t][:].indirect(listed(lo, hi)), COPY)
+            target = plain[(a, lo)][:, t * (hi - lo):(t + 1) * (hi - lo)]
+            nc.scalar.activation(target, planes[a * PACK + t][:].indirect(listed(lo, hi)), COPY)
 
         def woven(target):
             return target.rearrange("p (line i t) -> p line t i", i=RUN, t=PACK)
@@ -136,13 +144,12 @@ def tile_moe_pre_lin_bias_kernel(tc, xT, w_words, w_scales, b, gate, offs, out):
         def by_runs(source):
             return source.rearrange("p t (line i) -> p line t i", i=RUN)
 
-        def by_plane(tile):
-            return tile[:].rearrange("p (t s) -> p t s", t=PACK)
+        def by_plane(staged):
+            return staged.rearrange("p (t s) -> p t s", t=PACK)
 
         def ungated(a, lo, hi):
-            if lo < CUT[a]:
-                return by_plane(ahead)[:, :, lo:hi]
-            return by_plane(plain[a])[:, :, lo - CUT[a]:hi - CUT[a]]
+            first = max(start for piece, start, stop in ranges if piece == a and start <= lo)
+            return by_plane(plain[(a, first)])[:, :, lo - first:hi - first]
 
         def target(a, lo, hi):
             q, column = place[(a, lo)]
@@ -213,13 +220,13 @@ def tile_moe_pre_lin_bias_kernel(tc, xT, w_words, w_scales, b, gate, offs, out):
             acc = products(first, end, c)
             nc.vector.tensor_tensor(
                 home.rearrange("p (e s) -> p e s", s=C),
-                acc[:].rearrange("p (e s) -> p e s", s=C),
                 bias[:, c, first:end].unsqueeze(2).to_broadcast([P, end - first, C]),
+                acc[:].rearrange("p (e s) -> p e s", s=C),
                 ADD,
             )
 
-        def scatter_on_vector(first, end, c, home):
-            nc.vector.tensor_copy(windows[c][:].indirect(listed(first * C, end * C)), home)
+        def scatter_on_vector(lo, hi, c, home):
+            nc.vector.tensor_copy(windows[c][:].indirect(listed(lo, hi)), home)
 
         def store(c, queue):
             queue.dma_start(out=out[c * P:(c + 1) * P, :], in_=windows[c][:])
@@ -238,7 +245,7 @@ def tile_moe_pre_lin_bias_kernel(tc, xT, w_words, w_scales, b, gate, offs, out):
         for i in range(PASSES * PACK):
             nc.sync.dma_start(out=planes[i][:], in_=rows[i // PACK, i % PACK])
             if i == PACK:
-                nc.sync.dma_start(out=more_gates[:], in_=gate[0:P, CUT[0]:CUT[0] + 2 * UNIT])
+                nc.sync.dma_start(out=more_gates[:, 0:UNIT], in_=gate[0:P, CUT[0]:CUT[0] + UNIT])
         for quad in range(4):
             load_first_scale_rows(quad)
         load_weights(LOADS[0], LOADS[1])
@@ -246,11 +253,13 @@ def tile_moe_pre_lin_bias_kernel(tc, xT, w_words, w_scales, b, gate, offs, out):
         for r in range(4):
             for a in range(PASSES):
                 load_scale_rows(r, a)
-        for lo, hi in zip(LOADS[1:], LOADS[2:]):
+        load_weights(LOADS[1], LOADS[2])
+        nc.sync.dma_start(out=more_gates[:, UNIT:], in_=gate[0:P, CUT[0] + UNIT:CUT[0] + 2 * UNIT])
+        for lo, hi in zip(LOADS[2:], LOADS[3:]):
             load_weights(lo, hi)
 
-        spread = [spread_gate(0, psum.tile([P, RUN, P], F32, name="bank"))]
-        spread.extend(spread_gate(n, held.tile([P, RUN, P], F32, name="gate_bank%d" % n)) for n in (1, 2))
+        spread = [spread_gate(n, psum.tile([P, RUN, P], F32, name="bank")) for n in range(2)]
+        spread.append(spread_gate(2, held.tile([P, RUN, P], F32, name="gate_bank")))
         by_line = gates[:].rearrange("p (line i) -> p line i", i=RUN)
         nc.vector.tensor_copy(by_line[:, 0:P, :], spread[0])
         nc.vector.tensor_copy(by_line[:, P:, :], spread[1][:, 0:(CUT[0] - BANK) // RUN, :])
@@ -258,51 +267,50 @@ def tile_moe_pre_lin_bias_kernel(tc, xT, w_words, w_scales, b, gate, offs, out):
         for t in range(PACK):
             gather_gated(t)
             gather_plain(0, t, CUT[0], S)
-        nc.vector.tensor_copy(woven(rounded[:, 0:PACK * CUT[0]]), by_runs(by_plane(gated)))
+        nc.vector.tensor_copy(woven(target(0, 0, CUT[0])), by_runs(by_plane(gated[:])))
         quantize(0)
         quantize(1)
         gate_on_gpsimd(0, 768, 1024)
-        for t in range(PACK - 1):
+        for t in range(PACK):
             gather_ahead(t)
-            gather_plain(1, t, CUT[1], S)
-        gather_ahead(PACK - 1)
-        gather_plain(1, PACK - 1, CUT[1], CUT[0])
-        gather_plain(1, PACK - 1, CUT[0], S)
+            gather_plain(1, t, CUT[1], CUT[0])
         gate_on_vector(1, 0, 256)
+        for t in (0, 3, 1, 2):
+            gather_plain(1, t, CUT[0], S)
         quantize(2)
 
-        gate_on_gpsimd(0, 1024, 1280)
-        gate_on_vector(0, 1280, 1536)
-        sums_for_vector(0, 2, 2, early[0][:])
-        scatter_on_vector(0, 2, 2, early[0][:])
-        for c in (1, 0):
-            finish_on_scalar(0, 2, c)
-        quantize(3)
-
         gate_on_gpsimd(1, 256, 512)
-        gate_on_vector(1, 512, 1024)
+        gate_on_vector(1, 512, 768)
+        gate_on_vector(0, 1024, 1536)
+        quantize(3)
         quantize(4)
+        for c in (0, 1):
+            finish_on_scalar(0, 2, c)
+
+        gate_on_gpsimd(1, 768, 1024)
+        gate_on_vector(1, 1280, 1536)
+        sums_for_vector(2, 6, 2, early[2][:])
+        scatter_on_vector(2 * C, 6 * C, 2, early[2][:])
+        finish_on_scalar(2, 5, 0)
+        sums_for_vector(2, 6, 1, early[1][:])
         quantize(5)
+        finish_on_scalar(0, 2, 2)
 
         gate_on_gpsimd(1, 1024, 1280)
-        gate_on_vector(1, 1280, 1536)
-        finish_on_scalar(2, 5, 0)
-        sums_for_vector(2, 4, 2, early[1][:])
-        scatter_on_vector(2, 4, 2, early[1][:])
+        scatter_on_vector(2 * C, 6 * C, 1, early[1][:])
         quantize(6)
-
         finish_on_scalar(5, 8, 0)
-        sums_for_vector(2, 6, 1, late1[:, 0:4 * C])
-        sums_for_vector(6, 8, 1, late1[:, 4 * C:])
-        sums_for_vector(4, 8, 2, late2[:, 0:4 * C])
-        scatter_on_vector(2, 8, 1, late1)
-        finish_on_scalar(8, 10, 0)
-        sums_for_vector(8, 12, 2, late2[:, 4 * C:])
-        scatter_on_vector(4, 8, 2, late2[:, 0:4 * C])
-        scatter_on_vector(8, 12, 2, late2[:, 4 * C:])
+        sums_for_vector(10, 12, 2, y[2][:, 10 * C:S])
+        scatter_on_scalar(SHARED, S, 2)
+        sums_for_vector(6, 8, 1, late[0])
+        sums_for_vector(10, 12, 1, late[1])
+        scatter_on_vector(6 * C, 8 * C, 1, late[0])
+        sums_for_vector(6, 10, 2, y[2][:, 6 * C:10 * C])
+        scatter_on_vector(10 * C, S, 1, late[1])
+        scatter_on_vector(6 * C, SHARED, 2, y[2][:, 6 * C:SHARED])
         store(2, nc.sync)
         finish_on_scalar(10, 12, 0)
+        finish_on_scalar(8, 10, 0)
         store(0, nc.scalar)
         finish_on_scalar(8, 10, 1)
-        finish_on_scalar(10, 12, 1)
         store(1, nc.scalar)

@@ -61,7 +61,7 @@ def tile_moe_pre_lin_bias_kernel(tc, xT, w_words, w_scales, b, gate, offs, out):
         plain = {
             (a, lo): keep.tile([P, PACK * (hi - lo)], F32, name="plain%d_%d" % (a, lo))[:] for a, lo, hi in ranges
         }
-        plain[(1, 0)] = plain[(1, CUT[0])][:, PACK * UNIT:2 * PACK * UNIT]
+        plain[(1, 0)] = plain[(1, CUT[0])][:, 2 * CUT[0]:2 * CUT[0] + PACK * UNIT]
         ranges = ranges + ((1, 0, CUT[1]),)
         rounded = keep.tile([P, PACK * 8 * C], BF16, name="rounded", align_bytes=64)
         widths = [sum(hi - lo for a, lo, hi in call[1:]) for call in CALLS]
@@ -275,13 +275,13 @@ def tile_moe_pre_lin_bias_kernel(tc, xT, w_words, w_scales, b, gate, offs, out):
             gather_ahead(t)
             gather_plain(1, t, CUT[1], CUT[0])
         gate_on_vector(1, 0, 256)
-        for t in (0, 3, 1, 2):
+        for t in range(PACK):
             gather_plain(1, t, CUT[0], S)
         quantize(2)
 
         gate_on_gpsimd(1, 256, 512)
-        gate_on_vector(1, 512, 768)
         gate_on_vector(0, 1024, 1536)
+        gate_on_vector(1, 512, 768)
         quantize(3)
         quantize(4)
         for c in (0, 1):

@@ -24,21 +24,22 @@ P = 128
 PACK = 4
 PASSES = 2
 NT = N // P
-CUT = (6 * C, 2 * C)
-LOADS = (0, 2, 6, 9, 12)
 RUN = 4
 BANK = P * RUN
-UNIT = 2 * C
+HALF = 6
+CUT = 192
+LOADS = (0, 3, 7, 12)
 CALLS = (
-    (128, (0, 0, 256)),
-    (384, (0, 256, 768)),
-    (128, (1, 0, 256), (0, 768, 1024)),
-    (0, (1, 512, 768), (1, 256, 512)),
-    (512, (0, 1024, 1536)),
-    (384, (1, 768, 1024), (1, 1280, 1536)),
-    (512, (1, 1024, 1280)),
+    ("short", 0, (0, 0, 2), (1, 0, 2)),
+    ("long", 0, (1, 2, 3), (0, 2, 5)),
+    ("short", 2, (1, 3, 5)),
+    ("long", 4, (0, 5, 8)),
+    ("long", 1, (1, 5, 8)),
+    ("short", 3, (0, 8, 10)),
+    ("long", 1, (1, 8, 12)),
+    ("long", 2, (0, 11, 12)),
+    ("long", 1, (0, 10, 11)),
 )
-SHARED = 1344
 DMA_ALIGN = 256
 
 
@@ -47,49 +48,44 @@ def tile_moe_pre_lin_bias_kernel(tc, xT, w_words, w_scales, b, gate, offs, out):
     with ExitStack() as ctx:
         keep = ctx.enter_context(tc.tile_pool(name="keep", bufs=1))
         shared = ctx.enter_context(tc.tile_pool(name="shared", bufs=1))
-        held = ctx.enter_context(tc.psum_pool(name="held", bufs=1))
-        psum = ctx.enter_context(tc.psum_pool(name="psum", bufs=7))
+        psum = ctx.enter_context(tc.psum_pool(name="psum", bufs=8))
 
         offsets = keep.tile([P, S // 16], U16, name="offsets")
         planes = [keep.tile([P, T], F32, name="plane%d" % i, align_bytes=DMA_ALIGN) for i in range(PASSES * PACK)]
         identity = keep.tile([P, P], F32, name="identity")
         gate_cols = keep.tile([P, S // BANK, RUN], F32, name="gate_cols")
-        gates = keep.tile([P, CUT[0]], F32, name="gates")
-        more_gates = keep.tile([P, 2 * UNIT], F32, name="more_gates")
-        gated = keep.tile([P, PACK * CUT[0]], F32, name="gated")
-        ranges = ((0, CUT[0], S), (1, CUT[1], CUT[0]), (1, CUT[0], S))
-        plain = {
-            (a, lo): keep.tile([P, PACK * (hi - lo)], F32, name="plain%d_%d" % (a, lo))[:] for a, lo, hi in ranges
-        }
-        plain[(1, 0)] = plain[(1, CUT[0])][:, 2 * CUT[0]:2 * CUT[0] + PACK * UNIT]
-        ranges = ranges + ((1, 0, CUT[1]),)
-        rounded = keep.tile([P, PACK * 8 * C], BF16, name="rounded", align_bytes=64)
-        widths = [sum(hi - lo for a, lo, hi in call[1:]) for call in CALLS]
-        as_sums = rounded[:].bitcast(F32)
-        early = {
-            c: shared.tile([P, BANK], F32, name="early%d" % c, align_bytes=64, offset=at) for c, at in ((2, 1024), (1, 2048))
-        }
-        late = [as_sums[:, (4 + n) * UNIT:(5 + n) * UNIT] for n in range(2)]
-        codes = []
+        gates = {lo: keep.tile([P, (hi - lo) * C], F32, name="gates%d" % lo) for lo, hi in ((0, 8), (8, 12))}
+        gated = keep.tile([P, PACK * HALF * C], F32, name="gated")
+        ranges = ((0, 6, 12), (1, 0, 3), (1, 3, 8), (1, 8, 12))
+        plain = {(a, lo): keep.tile([P, PACK * (hi - lo) * C], F32, name="plain%d_%d" % (a, lo)) for a, lo, hi in ranges}
+        lanes = {"long": keep.tile([P, PACK * 7 * C], BF16, name="long_lane", align_bytes=64)}
+        lanes["short"] = shared.tile([P, PACK * 5 * C], BF16, name="short_lane", align_bytes=64, offset=0)
+        as_sums = lanes["long"][:].bitcast(F32)
+        widths = [sum(hi - lo for a, lo, hi in call[2:]) * C for call in CALLS]
+        codes = [keep.tile([P, w], U32, name="codes%d" % q, align_bytes=64) for q, w in enumerate(widths)]
+        early = [
+            shared.tile([P, 2 * C], F32, name="early%d" % n, align_bytes=64, offset=at) for n, at in enumerate((5120, 6144))
+        ]
+        early.append(lanes["short"][:].bitcast(F32)[:, 3 * 2 * C:4 * 2 * C])
+        held_at = {2: 5120, 3: 5120 + 256, 4: 5120 + 640, 5: 6144, 6: 6144 + 256, 7: 0, 8: 128}
+        scales = []
         for q, w in enumerate(widths):
-            if q == 5:
-                codes.append(shared.tile([P, w], U32, name="codes%d" % q, align_bytes=64, offset=0))
+            if q in held_at:
+                scales.append(shared.tile([P, w], U8, name="scales%d" % q, align_bytes=64, offset=held_at[q]))
             else:
-                codes.append(keep.tile([P, w], U32, name="codes%d" % q, align_bytes=64))
-        scales = [keep.tile([P, w], U8, name="scales%d" % q, align_bytes=64) for q, w in enumerate(widths)]
+                scales.append(keep.tile([P, w], U8, name="scales%d" % q, align_bytes=64))
         place = {}
         for q, call in enumerate(CALLS):
-            column = 0
-            for a, lo, hi in call[1:]:
-                for slot in range(lo, hi, C):
-                    place[(a, slot)] = (q, column)
-                    column += C
+            block = 0
+            for a, lo, hi in call[2:]:
+                for e in range(lo, hi):
+                    place[(a, e)] = (q, block)
+                    block += 1
         words = {
             lo: keep.tile([P, (hi - lo) * PASSES * N], U32, name="words%d" % lo, align_bytes=64)
             for lo, hi in zip(LOADS, LOADS[1:])
         }
-        first_scale_rows = keep.tile([P, N], U8, name="first_scale_rows", align_bytes=64)
-        w_scale_rows = keep.tile([P, E - LOADS[1], N], U8, name="w_scale_rows", align_bytes=64)
+        scale_rows = [keep.tile([P, N], U8, name="scale_rows%d" % pair, align_bytes=64) for pair in range(E // 2)]
         bias = keep.tile([P, NT, E], F32, name="bias")
         y = [keep.tile([P, S], F32, name="y%d" % c) for c in range(NT)]
         windows = [keep.tile([P, T], F32, name="window%d" % c, align_bytes=DMA_ALIGN) for c in range(NT)]
@@ -100,124 +96,124 @@ def tile_moe_pre_lin_bias_kernel(tc, xT, w_words, w_scales, b, gate, offs, out):
             source = w_words[lo:hi].rearrange("e a p n t -> p (e a) (n t)")
             nc.sync.dma_start(out=words[lo][:].bitcast(I32).rearrange("p (m n) -> p m n", n=N), in_=source.bitcast(I32))
 
-        def load_first_scale_rows(quad):
-            nc.sync.dma_start(
-                out=first_scale_rows[32 * quad:32 * quad + 16, :].bitcast(I32),
-                in_=w_scales[0:LOADS[1], :, 4 * quad:4 * quad + 4, :].rearrange("e a r n -> (e a) r n").bitcast(I32),
-            )
+        def load_scale_rows(pair):
+            for quad in range(4):
+                source = w_scales[2 * pair:2 * pair + 2, :, 4 * quad:4 * quad + 4, :]
+                nc.sync.dma_start(
+                    out=scale_rows[pair][32 * quad:32 * quad + 16, :].bitcast(I32),
+                    in_=source.rearrange("e a r n -> (e a) r n").bitcast(I32),
+                )
 
-        def load_scale_rows(r, a):
-            nc.sync.dma_start(
-                out=scale_words[4 * a + r:P:32, :, :],
-                in_=w_scales[LOADS[1]:E, a, r:16:4, :].rearrange("e q n -> q e n").bitcast(I32),
-            )
+        def load_gates(lo, hi):
+            first = max(start for start in gates if start <= lo)
+            nc.sync.dma_start(out=gates[first][:, (lo - first) * C:(hi - first) * C], in_=gate[0:P, lo * C:hi * C])
 
         def weight_scales(e, a, c):
-            if e < LOADS[1]:
-                return first_scale_rows[4 * (e * PASSES + a):P, c * P:(c + 1) * P]
-            return w_scale_rows[4 * a:P, e - LOADS[1], c * P:(c + 1) * P]
+            return scale_rows[e // 2][4 * (e % 2 * PASSES + a):P, c * P:(c + 1) * P]
 
-        def spread_gate(n, bank):
+        def spread_gate(n):
+            bank = psum.tile([P, RUN, P], F32, name="bank")
             for i in range(RUN):
                 nc.tensor.transpose(bank[:, i, :], gate_cols[:, n, i:i + 1].to_broadcast([P, P]), identity[:])
             return bank[:].rearrange("p i line -> p line i")
 
-        def listed(lo, hi):
+        def slots(lo, hi):
             return offsets[:, lo // 16:hi // 16]
 
-        def gather_gated(t):
-            nc.vector.tensor_tensor(
-                gated[:, t * CUT[0]:(t + 1) * CUT[0]], planes[t][:].indirect(listed(0, CUT[0])), gates[:], MULT
-            )
-
-        def gather_ahead(t):
-            target = plain[(1, 0)][:, t * CUT[1]:(t + 1) * CUT[1]]
-            nc.vector.tensor_copy(target, planes[PACK + t][:].indirect(listed(0, CUT[1])))
-
-        def gather_plain(a, t, lo, hi):
-            target = plain[(a, lo)][:, t * (hi - lo):(t + 1) * (hi - lo)]
-            nc.scalar.activation(target, planes[a * PACK + t][:].indirect(listed(lo, hi)), COPY)
-
-        def woven(target):
-            return target.rearrange("p (line i t) -> p line t i", i=RUN, t=PACK)
-
-        def by_runs(source):
-            return source.rearrange("p t (line i) -> p line t i", i=RUN)
+        def listed(lo, hi):
+            return slots(lo * C, hi * C)
 
         def by_plane(staged):
             return staged.rearrange("p (t s) -> p t s", t=PACK)
 
         def ungated(a, lo, hi):
             first = max(start for piece, start, stop in ranges if piece == a and start <= lo)
-            return by_plane(plain[(a, first)])[:, :, lo - first:hi - first]
+            return by_plane(plain[(a, first)][:])[:, :, (lo - first) * C:(hi - first) * C]
 
-        def target(a, lo, hi):
-            q, column = place[(a, lo)]
-            at = CALLS[q][0] + column
-            return rounded[:, PACK * at:PACK * (at + hi - lo)]
+        def gather_gated(t):
+            nc.vector.tensor_tensor(
+                by_plane(gated[:])[:, t, :], planes[t][:].indirect(listed(0, HALF)), gates[0][:, 0:HALF * C], MULT
+            )
+
+        def gather_on_vector(a, t, lo, hi):
+            nc.vector.tensor_copy(ungated(a, lo, hi)[:, t, :], planes[a * PACK + t][:].indirect(listed(lo, hi)))
+
+        def gather_on_scalar(a, t, lo, hi):
+            nc.scalar.activation(ungated(a, lo, hi)[:, t, :], planes[a * PACK + t][:].indirect(listed(lo, hi)), COPY)
+
+        def woven(a, lo, hi):
+            q, block = place[(a, lo)]
+            at = (CALLS[q][1] + block) * C
+            return lanes[CALLS[q][0]][:, PACK * at:PACK * (at + (hi - lo) * C)].rearrange("p (line i t) -> p line t i", i=RUN, t=PACK)
+
+        def by_runs(source):
+            return source.rearrange("p t (line i) -> p line t i", i=RUN)
+
+        def times_gate(engine, factor, a, lo, hi):
+            lines = (hi - lo) * C // RUN
+            engine.tensor_tensor(
+                woven(a, lo, hi), by_runs(ungated(a, lo, hi)), factor.unsqueeze(2).to_broadcast([P, lines, PACK, RUN]), MULT
+            )
 
         def gate_on_vector(a, lo, hi):
-            first = lo % BANK // RUN
-            factor = spread[lo // BANK][:, first:first + (hi - lo) // RUN, :]
+            first = lo * C % BANK // RUN
+            times_gate(nc.vector, spread[lo * C // BANK][:, first:first + (hi - lo) * C // RUN, :], a, lo, hi)
+
+        def gate_half_on_vector(e, half):
+            lines = C // RUN // 2
+            part = slice(half * lines, (half + 1) * lines)
+            first = e * C % BANK // RUN
+            factor = spread[e * C // BANK][:, first:first + 2 * lines, :][:, part]
             nc.vector.tensor_tensor(
-                woven(target(a, lo, hi)),
-                by_runs(ungated(a, lo, hi)),
-                factor.unsqueeze(2).to_broadcast([P, (hi - lo) // RUN, PACK, RUN]),
+                woven(0, e, e + 1)[:, part],
+                by_runs(ungated(0, e, e + 1))[:, part],
+                factor.unsqueeze(2).to_broadcast([P, lines, PACK, RUN]),
                 MULT,
             )
+
+        def round_on_gpsimd(lo, hi):
+            nc.gpsimd.tensor_scalar(woven(0, lo, hi), by_runs(by_plane(gated[:])[:, :, lo * C:hi * C]), 1.0, 0.0, MULT, ADD)
 
         def gate_on_gpsimd(a, lo, hi):
-            factor = gates[:, lo:hi] if hi <= CUT[0] else more_gates[:, lo - CUT[0]:hi - CUT[0]]
-            nc.gpsimd.tensor_tensor(
-                target(a, lo, hi).rearrange("p (s t) -> p s t", t=PACK),
-                ungated(a, lo, hi).rearrange("p t s -> p s t"),
-                factor.unsqueeze(2).to_broadcast([P, hi - lo, PACK]),
-                MULT,
-            )
+            first = max(start for start in gates if start <= lo)
+            factor = gates[first][:, (lo - first) * C:(hi - first) * C].rearrange("p (line i) -> p line i", i=RUN)
+            times_gate(nc.gpsimd, factor, a, lo, hi)
 
         def quantize(q):
-            at = CALLS[q][0]
-            nc.vector.quantize_mx(
-                out=codes[q][:].bitcast(FP8X4), scales=scales[q][:], in_=rounded[:, PACK * at:PACK * (at + widths[q])]
-            )
+            at = CALLS[q][1] * C
+            source = lanes[CALLS[q][0]][:, PACK * at:PACK * (at + widths[q])]
+            nc.vector.quantize_mx(out=codes[q][:].bitcast(FP8X4), scales=scales[q][:], in_=source)
 
-        def products(first, end, c):
+        def products(c, first, end):
             acc = psum.tile([P, (end - first) * C], F32, name="bank")
             for a in range(PASSES):
                 for e in range(first, end):
                     load = max(lo for lo in LOADS if lo <= e)
                     at = ((e - load) * PASSES + a) * N + c * P
-                    q, column = place[(a, e * C)]
+                    q, block = place[(a, e)]
                     nc.tensor.matmul_mx(
                         out=acc[:, (e - first) * C:(e - first + 1) * C],
                         lhsT=words[load][:, at:at + P].bitcast(FP8X4),
                         lhsT_scale=weight_scales(e, a, c),
-                        rhs=codes[q][:, column:column + C].bitcast(FP8X4),
-                        rhs_scale=scales[q][:, column:column + C],
+                        rhs=codes[q][:, block * C:(block + 1) * C].bitcast(FP8X4),
+                        rhs_scale=scales[q][:, block * C:(block + 1) * C],
                         start=(a == 0 and e == first),
                         stop=(a == PASSES - 1 and e == end - 1),
                     )
             return acc
 
-        def sums_for_scalar(first, end, c):
-            acc = products(first, end, c)
+        def sums_on_scalar(c, first, end):
+            acc = products(c, first, end)
             for e in range(first, end):
                 nc.scalar.activation(
-                    y[c][:, e * C:(e + 1) * C],
-                    acc[:, (e - first) * C:(e - first + 1) * C],
-                    IDENT,
-                    bias=bias[:, c, e:e + 1],
+                    y[c][:, e * C:(e + 1) * C], acc[:, (e - first) * C:(e - first + 1) * C], IDENT, bias=bias[:, c, e:e + 1]
                 )
 
-        def scatter_on_scalar(lo, hi, c):
-            nc.scalar.activation(windows[c][:].indirect(listed(lo, hi)), y[c][:, lo:hi], COPY)
+        def scatter_on_scalar(c, first, end):
+            nc.scalar.activation(windows[c][:].indirect(listed(first, end)), y[c][:, first * C:end * C], COPY)
 
-        def finish_on_scalar(first, end, c):
-            sums_for_scalar(first, end, c)
-            scatter_on_scalar(first * C, end * C, c)
-
-        def sums_for_vector(first, end, c, home):
-            acc = products(first, end, c)
+        def sums_on_vector(c, first, end, home):
+            acc = products(c, first, end)
             nc.vector.tensor_tensor(
                 home.rearrange("p (e s) -> p e s", s=C),
                 bias[:, c, first:end].unsqueeze(2).to_broadcast([P, end - first, C]),
@@ -225,92 +221,136 @@ def tile_moe_pre_lin_bias_kernel(tc, xT, w_words, w_scales, b, gate, offs, out):
                 ADD,
             )
 
-        def scatter_on_vector(lo, hi, c, home):
-            nc.vector.tensor_copy(windows[c][:].indirect(listed(lo, hi)), home)
+        def scatter_on_vector(c, first, end, home):
+            nc.vector.tensor_copy(windows[c][:].indirect(listed(first, end)), home)
+
+        def finish_on_vector(c, first, end, home):
+            sums_on_vector(c, first, end, home)
+            scatter_on_vector(c, first, end, home)
+
+        def finish_on_scalar(c, first, end):
+            sums_on_scalar(c, first, end)
+            scatter_on_scalar(c, first, end)
+
+        def in_rounded(block, experts):
+            at = block * C * PACK // 2
+            return as_sums[:, at:at + experts * C]
 
         def store(c, queue):
             queue.dma_start(out=out[c * P:(c + 1) * P, :], in_=windows[c][:])
 
-        scale_words = w_scale_rows[:].bitcast(I32)
         zero = keep.tile([P, 1], F32, name="zero")
         unread = keep.tile([P, 1], F32, name="unread")
         nc.gpsimd.memset(zero[:], 0.0)
         nc.scalar.activation(unread[:], zero[:], COPY)
-        nc.vector.memset(scale_words, 0)
-        nc.vector.memset(first_scale_rows[:].bitcast(I32), 0)
+        for rows_of_pair in scale_rows:
+            nc.vector.memset(rows_of_pair[:].bitcast(I32), 0)
         make_identity(nc, identity[:])
 
         nc.sync.dma_start(out=gate_cols[:], in_=gate[0, :].rearrange("(n p i) -> p n i", p=P, i=RUN))
         nc.sync.dma_start(offsets[:], offs)
         for i in range(PASSES * PACK):
             nc.sync.dma_start(out=planes[i][:], in_=rows[i // PACK, i % PACK])
-            if i == PACK:
-                nc.sync.dma_start(out=more_gates[:, 0:UNIT], in_=gate[0:P, CUT[0]:CUT[0] + UNIT])
-        for quad in range(4):
-            load_first_scale_rows(quad)
-        load_weights(LOADS[0], LOADS[1])
         nc.sync.dma_start(out=bias[:], in_=b.rearrange("(c p) e -> p c e", p=P))
-        for r in range(4):
-            for a in range(PASSES):
-                load_scale_rows(r, a)
+        load_scale_rows(0)
+        load_weights(LOADS[0], LOADS[1])
+        load_scale_rows(1)
         load_weights(LOADS[1], LOADS[2])
-        nc.sync.dma_start(out=more_gates[:, UNIT:], in_=gate[0:P, CUT[0] + UNIT:CUT[0] + 2 * UNIT])
-        for lo, hi in zip(LOADS[2:], LOADS[3:]):
-            load_weights(lo, hi)
+        load_gates(8, 12)
+        load_scale_rows(2)
+        load_scale_rows(3)
+        load_weights(LOADS[2], LOADS[3])
+        load_scale_rows(4)
+        load_scale_rows(5)
 
-        spread = [spread_gate(n, psum.tile([P, RUN, P], F32, name="bank")) for n in range(2)]
-        spread.append(spread_gate(2, held.tile([P, RUN, P], F32, name="gate_bank")))
-        by_line = gates[:].rearrange("p (line i) -> p line i", i=RUN)
-        nc.vector.tensor_copy(by_line[:, 0:P, :], spread[0])
-        nc.vector.tensor_copy(by_line[:, P:, :], spread[1][:, 0:(CUT[0] - BANK) // RUN, :])
+        spread = [spread_gate(n) for n in range(S // BANK)]
+        by_line = gates[0][:].rearrange("p (line i) -> p line i", i=RUN)
+        for n in range(2):
+            nc.vector.tensor_copy(by_line[:, n * P:(n + 1) * P, :], spread[n])
 
         for t in range(PACK):
             gather_gated(t)
-            gather_plain(0, t, CUT[0], S)
-        nc.vector.tensor_copy(woven(target(0, 0, CUT[0])), by_runs(by_plane(gated[:])))
+            gather_on_scalar(0, t, HALF, E)
+        round_on_gpsimd(0, 2)
+        round_on_gpsimd(2, HALF)
+        gate_on_gpsimd(0, 6, 8)
+        gate_on_vector(0, 9, 10)
+
+        gather_on_vector(1, 0, 0, 3)
+        gather_on_vector(1, 0, 3, 6)
+        gather_on_scalar(1, 0, 6, 8)
+        gather_on_scalar(1, 0, 8, 12)
+        gather_on_vector(1, 1, 0, 3)
+        gather_on_scalar(1, 1, 3, 8)
+        gather_on_scalar(1, 1, 8, 12)
+        gather_on_vector(1, 2, 0, 3)
+        gather_on_vector(1, 3, 0, 2)
+        gather_on_vector(1, 3, 2, 3)
+        for t in (2, 3):
+            gather_on_scalar(1, t, 3, 8)
+            gather_on_scalar(1, t, 8, 12)
+        gate_on_vector(1, 0, 2)
+        gate_on_vector(1, 2, 3)
         quantize(0)
         quantize(1)
-        gate_on_gpsimd(0, 768, 1024)
-        for t in range(PACK):
-            gather_ahead(t)
-            gather_plain(1, t, CUT[1], CUT[0])
-        gate_on_vector(1, 0, 256)
-        for t in range(PACK):
-            gather_plain(1, t, CUT[0], S)
-        quantize(2)
 
-        gate_on_gpsimd(1, 256, 512)
-        gate_on_vector(0, 1024, 1536)
-        gate_on_vector(1, 512, 768)
-        quantize(3)
-        quantize(4)
-        for c in (0, 1):
-            finish_on_scalar(0, 2, c)
+        gate_on_gpsimd(1, 5, 8)
+        gate_on_vector(1, 3, 4)
+        gate_on_vector(1, 4, 5)
+        acc = products(0, 0, 2)
+        for e, lo, hi, home in ((0, 0, C, early[0]), (1, C, CUT, early[0]), (1, CUT, 2 * C, y[0])):
+            nc.scalar.activation(home[:, lo:hi], acc[:, lo:hi], IDENT, bias=bias[:, 0, e:e + 1])
+        sums_on_vector(2, 0, 2, y[2][:, 0:2 * C])
+        sums_on_scalar(1, 0, 3)
+        sums_on_scalar(0, 2, 3)
+        sums_on_scalar(2, 2, 3)
+        nc.vector.tensor_copy(windows[0][:].indirect(slots(0, CUT)), early[0][:, 0:CUT])
+        nc.vector.tensor_copy(windows[2][:].indirect(slots(0, CUT)), y[2][:, 0:CUT])
+        scatter_on_scalar(1, 0, 3)
+        for c in (0, 2):
+            nc.scalar.activation(windows[c][:].indirect(slots(CUT, 3 * C)), y[c][:, CUT:3 * C], COPY)
+        for q in (2, 3, 4):
+            quantize(q)
 
-        gate_on_gpsimd(1, 768, 1024)
-        gate_on_vector(1, 1280, 1536)
-        sums_for_vector(2, 6, 2, early[2][:])
-        scatter_on_vector(2 * C, 6 * C, 2, early[2][:])
-        finish_on_scalar(2, 5, 0)
-        sums_for_vector(2, 6, 1, early[1][:])
+        gate_on_gpsimd(1, 8, 12)
+        gate_on_vector(0, 8, 9)
+        sums_on_vector(0, 3, 5, early[1][:])
+        sums_on_vector(2, 3, 5, y[2][:, 3 * C:5 * C])
+        sums_on_scalar(1, 3, 6)
+        sums_on_scalar(2, 5, 8)
+        scatter_on_vector(0, 3, 5, early[1][:])
+        scatter_on_vector(2, 3, 5, y[2][:, 3 * C:5 * C])
+        scatter_on_scalar(1, 3, 6)
+        sums_on_scalar(1, 6, 8)
         quantize(5)
-        finish_on_scalar(0, 2, 2)
-
-        gate_on_gpsimd(1, 1024, 1280)
-        scatter_on_vector(2 * C, 6 * C, 1, early[1][:])
         quantize(6)
-        finish_on_scalar(5, 8, 0)
-        sums_for_vector(10, 12, 2, y[2][:, 10 * C:S])
-        scatter_on_scalar(SHARED, S, 2)
-        sums_for_vector(6, 8, 1, late[0])
-        sums_for_vector(10, 12, 1, late[1])
-        scatter_on_vector(6 * C, 8 * C, 1, late[0])
-        sums_for_vector(6, 10, 2, y[2][:, 6 * C:10 * C])
-        scatter_on_vector(10 * C, S, 1, late[1])
-        scatter_on_vector(6 * C, SHARED, 2, y[2][:, 6 * C:SHARED])
-        store(2, nc.sync)
-        finish_on_scalar(10, 12, 0)
-        finish_on_scalar(8, 10, 0)
-        store(0, nc.scalar)
-        finish_on_scalar(8, 10, 1)
+
+        gate_on_gpsimd(0, 11, 12)
+        sums_on_vector(0, 5, 7, early[2])
+        gate_half_on_vector(10, 0)
+        scatter_on_vector(0, 5, 7, early[2])
+        gate_half_on_vector(10, 1)
+        scatter_on_scalar(2, 5, 8)
+        sums_on_scalar(1, 8, 9)
+        scatter_on_scalar(1, 6, 9)
+        quantize(7)
+        quantize(8)
+
+        handed = in_rounded(2, 4)
+        sums_on_vector(2, 8, 10, handed[:, 0:2 * C])
+        sums_on_vector(0, 7, 9, in_rounded(1, 2))
+        nc.vector.tensor_copy(windows[2][:].indirect(slots(8 * C, 8 * C + CUT)), handed[:, 0:CUT])
+        acc = products(2, 10, 12)
+        for e in (10, 11):
+            nc.scalar.activation(
+                handed[:, (e - 8) * C:(e - 7) * C], acc[:, (e - 10) * C:(e - 9) * C], IDENT, bias=bias[:, 2, e:e + 1]
+            )
+        sums_on_scalar(1, 9, 12)
+        sums_on_vector(0, 9, 12, y[0][:, 9 * C:S])
+        scatter_on_vector(0, 7, 9, in_rounded(1, 2))
+        nc.scalar.activation(windows[2][:].indirect(slots(8 * C + CUT, S)), handed[:, CUT:], COPY)
+        scatter_on_scalar(1, 9, 12)
+        scatter_on_vector(0, 9, 12, y[0][:, 9 * C:S])
+        store(2, nc.scalar)
+        store(0, nc.sync)
         store(1, nc.scalar)

@@ -28,17 +28,17 @@ RUN = 4
 BANK = P * RUN
 HALF = 6
 CUT = 192
-LOADS = (0, 3, 7, 12)
+LOADS = (0, 2, 3, 5, 8, 12)
 CALLS = (
     ("short", 0, (0, 0, 2), (1, 0, 2)),
     ("long", 0, (1, 2, 3), (0, 2, 5)),
     ("short", 2, (1, 3, 5)),
-    ("long", 4, (0, 5, 8)),
+    ("long", 4, (0, 5, 9)),
     ("long", 1, (1, 5, 8)),
-    ("short", 3, (0, 8, 10)),
+    ("short", 3, (0, 9, 10)),
     ("long", 1, (1, 8, 12)),
-    ("long", 2, (0, 11, 12)),
     ("long", 1, (0, 10, 11)),
+    ("long", 2, (0, 11, 12)),
 )
 DMA_ALIGN = 256
 
@@ -54,12 +54,15 @@ def tile_moe_pre_lin_bias_kernel(tc, xT, w_words, w_scales, b, gate, offs, out):
         planes = [keep.tile([P, T], F32, name="plane%d" % i, align_bytes=DMA_ALIGN) for i in range(PASSES * PACK)]
         identity = keep.tile([P, P], F32, name="identity")
         gate_cols = keep.tile([P, S // BANK, RUN], F32, name="gate_cols")
-        gates = {lo: keep.tile([P, (hi - lo) * C], F32, name="gates%d" % lo) for lo, hi in ((0, 8), (8, 12))}
+        gates = {lo: keep.tile([P, (hi - lo) * C], F32, name="gates%d" % lo) for lo, hi in ((0, 9), (8, 12))}
         gated = keep.tile([P, PACK * HALF * C], F32, name="gated")
         ranges = ((0, 6, 12), (1, 0, 3), (1, 3, 8), (1, 8, 12))
-        plain = {(a, lo): keep.tile([P, PACK * (hi - lo) * C], F32, name="plain%d_%d" % (a, lo)) for a, lo, hi in ranges}
-        lanes = {"long": keep.tile([P, PACK * 7 * C], BF16, name="long_lane", align_bytes=64)}
-        lanes["short"] = shared.tile([P, PACK * 5 * C], BF16, name="short_lane", align_bytes=64, offset=0)
+        plain = {(a, lo): keep.tile([P, PACK * (hi - lo) * C], F32, name="plain%d_%d" % (a, lo))[:] for a, lo, hi in ranges[0::2]}
+        last = keep.tile([P, (2 * 4 + PACK * 3) * C], F32, name="last")
+        plain[(1, 0)] = last[:, 2 * 4 * C:]
+        plain[(1, 8)] = last[:, 0:PACK * 4 * C]
+        lanes = {"long": keep.tile([P, PACK * 8 * C], BF16, name="long_lane", align_bytes=64)}
+        lanes["short"] = shared.tile([P, PACK * 4 * C], BF16, name="short_lane", align_bytes=64, offset=0)
         as_sums = lanes["long"][:].bitcast(F32)
         widths = [sum(hi - lo for a, lo, hi in call[2:]) * C for call in CALLS]
         codes = [keep.tile([P, w], U32, name="codes%d" % q, align_bytes=64) for q, w in enumerate(widths)]
@@ -67,7 +70,7 @@ def tile_moe_pre_lin_bias_kernel(tc, xT, w_words, w_scales, b, gate, offs, out):
             shared.tile([P, 2 * C], F32, name="early%d" % n, align_bytes=64, offset=at) for n, at in enumerate((5120, 6144))
         ]
         early.append(lanes["short"][:].bitcast(F32)[:, 3 * 2 * C:4 * 2 * C])
-        held_at = {2: 5120, 3: 5120 + 256, 4: 5120 + 640, 5: 6144, 6: 6144 + 256, 7: 0, 8: 128}
+        held_at = {2: 5120 - 128, 3: 5120 + 128, 4: 5120 + 640, 5: 6144, 6: 6144 + 256, 7: 0, 8: 128}
         scales = []
         for q, w in enumerate(widths):
             if q in held_at:
@@ -128,7 +131,7 @@ def tile_moe_pre_lin_bias_kernel(tc, xT, w_words, w_scales, b, gate, offs, out):
 
         def ungated(a, lo, hi):
             first = max(start for piece, start, stop in ranges if piece == a and start <= lo)
-            return by_plane(plain[(a, first)][:])[:, :, (lo - first) * C:(hi - first) * C]
+            return by_plane(plain[(a, first)])[:, :, (lo - first) * C:(hi - first) * C]
 
         def gather_gated(t):
             nc.vector.tensor_tensor(
@@ -159,23 +162,11 @@ def tile_moe_pre_lin_bias_kernel(tc, xT, w_words, w_scales, b, gate, offs, out):
             first = lo * C % BANK // RUN
             times_gate(nc.vector, spread[lo * C // BANK][:, first:first + (hi - lo) * C // RUN, :], a, lo, hi)
 
-        def gate_half_on_vector(e, half):
-            lines = C // RUN // 2
-            part = slice(half * lines, (half + 1) * lines)
-            first = e * C % BANK // RUN
-            factor = spread[e * C // BANK][:, first:first + 2 * lines, :][:, part]
-            nc.vector.tensor_tensor(
-                woven(0, e, e + 1)[:, part],
-                by_runs(ungated(0, e, e + 1))[:, part],
-                factor.unsqueeze(2).to_broadcast([P, lines, PACK, RUN]),
-                MULT,
-            )
-
         def round_on_gpsimd(lo, hi):
             nc.gpsimd.tensor_scalar(woven(0, lo, hi), by_runs(by_plane(gated[:])[:, :, lo * C:hi * C]), 1.0, 0.0, MULT, ADD)
 
         def gate_on_gpsimd(a, lo, hi):
-            first = max(start for start in gates if start <= lo)
+            first = 0 if hi <= 9 else 8
             factor = gates[first][:, (lo - first) * C:(hi - first) * C].rearrange("p (line i) -> p line i", i=RUN)
             times_gate(nc.gpsimd, factor, a, lo, hi)
 
@@ -251,15 +242,17 @@ def tile_moe_pre_lin_bias_kernel(tc, xT, w_words, w_scales, b, gate, offs, out):
         nc.sync.dma_start(offsets[:], offs)
         for i in range(PASSES * PACK):
             nc.sync.dma_start(out=planes[i][:], in_=rows[i // PACK, i % PACK])
-        nc.sync.dma_start(out=bias[:], in_=b.rearrange("(c p) e -> p c e", p=P))
         load_scale_rows(0)
-        load_weights(LOADS[0], LOADS[1])
+        load_weights(0, 2)
+        nc.sync.dma_start(out=bias[:], in_=b.rearrange("(c p) e -> p c e", p=P))
         load_scale_rows(1)
-        load_weights(LOADS[1], LOADS[2])
+        load_weights(2, 3)
+        load_weights(3, 5)
         load_gates(8, 12)
         load_scale_rows(2)
+        load_weights(5, 8)
         load_scale_rows(3)
-        load_weights(LOADS[2], LOADS[3])
+        load_weights(8, 12)
         load_scale_rows(4)
         load_scale_rows(5)
 
@@ -267,14 +260,14 @@ def tile_moe_pre_lin_bias_kernel(tc, xT, w_words, w_scales, b, gate, offs, out):
         by_line = gates[0][:].rearrange("p (line i) -> p line i", i=RUN)
         for n in range(2):
             nc.vector.tensor_copy(by_line[:, n * P:(n + 1) * P, :], spread[n])
+        nc.vector.tensor_copy(by_line[:, 2 * P:, :], spread[2][:, 0:C // RUN, :])
 
         for t in range(PACK):
             gather_gated(t)
             gather_on_scalar(0, t, HALF, E)
         round_on_gpsimd(0, 2)
         round_on_gpsimd(2, HALF)
-        gate_on_gpsimd(0, 6, 8)
-        gate_on_vector(0, 9, 10)
+        gate_on_gpsimd(0, 6, 9)
 
         gather_on_vector(1, 0, 0, 3)
         gather_on_vector(1, 0, 3, 6)
@@ -288,24 +281,27 @@ def tile_moe_pre_lin_bias_kernel(tc, xT, w_words, w_scales, b, gate, offs, out):
         gather_on_vector(1, 3, 2, 3)
         for t in (2, 3):
             gather_on_scalar(1, t, 3, 8)
-            gather_on_scalar(1, t, 8, 12)
         gate_on_vector(1, 0, 2)
         gate_on_vector(1, 2, 3)
+        for t in (2, 3):
+            gather_on_scalar(1, t, 8, 12)
         quantize(0)
         quantize(1)
 
         gate_on_gpsimd(1, 5, 8)
         gate_on_vector(1, 3, 4)
         gate_on_vector(1, 4, 5)
-        acc = products(0, 0, 2)
-        for e, lo, hi, home in ((0, 0, C, early[0]), (1, C, CUT, early[0]), (1, CUT, 2 * C, y[0])):
-            nc.scalar.activation(home[:, lo:hi], acc[:, lo:hi], IDENT, bias=bias[:, 0, e:e + 1])
-        sums_on_vector(2, 0, 2, y[2][:, 0:2 * C])
+        first_banks = {c: products(c, 0, 2) for c in (2, 0)}
+        for c, home in ((2, early[0]), (0, y[0])):
+            for lo, hi in ((0, C), (C, CUT)):
+                spread_bias = bias[:, c, lo // C:lo // C + 1].to_broadcast([P, hi - lo])
+                nc.vector.tensor_tensor(home[:, lo:hi], spread_bias, first_banks[c][:, lo:hi], ADD)
         sums_on_scalar(1, 0, 3)
-        sums_on_scalar(0, 2, 3)
-        sums_on_scalar(2, 2, 3)
-        nc.vector.tensor_copy(windows[0][:].indirect(slots(0, CUT)), early[0][:, 0:CUT])
-        nc.vector.tensor_copy(windows[2][:].indirect(slots(0, CUT)), y[2][:, 0:CUT])
+        for c in (2, 0):
+            nc.scalar.activation(y[c][:, CUT:2 * C], first_banks[c][:, CUT:2 * C], IDENT, bias=bias[:, c, 1:2])
+            sums_on_scalar(c, 2, 3)
+        nc.vector.tensor_copy(windows[2][:].indirect(slots(0, CUT)), early[0][:, 0:CUT])
+        nc.vector.tensor_copy(windows[0][:].indirect(slots(0, CUT)), y[0][:, 0:CUT])
         scatter_on_scalar(1, 0, 3)
         for c in (0, 2):
             nc.scalar.activation(windows[c][:].indirect(slots(CUT, 3 * C)), y[c][:, CUT:3 * C], COPY)
@@ -313,7 +309,7 @@ def tile_moe_pre_lin_bias_kernel(tc, xT, w_words, w_scales, b, gate, offs, out):
             quantize(q)
 
         gate_on_gpsimd(1, 8, 12)
-        gate_on_vector(0, 8, 9)
+        gate_on_vector(0, 9, 10)
         sums_on_vector(0, 3, 5, early[1][:])
         sums_on_vector(2, 3, 5, y[2][:, 3 * C:5 * C])
         sums_on_scalar(1, 3, 6)
@@ -321,36 +317,31 @@ def tile_moe_pre_lin_bias_kernel(tc, xT, w_words, w_scales, b, gate, offs, out):
         scatter_on_vector(0, 3, 5, early[1][:])
         scatter_on_vector(2, 3, 5, y[2][:, 3 * C:5 * C])
         scatter_on_scalar(1, 3, 6)
-        sums_on_scalar(1, 6, 8)
         quantize(5)
         quantize(6)
 
-        gate_on_gpsimd(0, 11, 12)
+        gate_on_gpsimd(0, 10, 12)
         sums_on_vector(0, 5, 7, early[2])
-        gate_half_on_vector(10, 0)
+        sums_on_vector(1, 6, 8, in_rounded(4, 2))
         scatter_on_vector(0, 5, 7, early[2])
-        gate_half_on_vector(10, 1)
         scatter_on_scalar(2, 5, 8)
-        sums_on_scalar(1, 8, 9)
-        scatter_on_scalar(1, 6, 9)
+        nc.scalar.activation(windows[1][:].indirect(listed(6, 8)), in_rounded(4, 2), COPY)
+        sums_on_vector(2, 8, 10, y[2][:, 8 * C:10 * C])
+        sums_on_scalar(1, 8, 10)
         quantize(7)
         quantize(8)
+        last_sums = as_sums[:, C:PACK * C]
 
-        handed = in_rounded(2, 4)
-        sums_on_vector(2, 8, 10, handed[:, 0:2 * C])
-        sums_on_vector(0, 7, 9, in_rounded(1, 2))
-        nc.vector.tensor_copy(windows[2][:].indirect(slots(8 * C, 8 * C + CUT)), handed[:, 0:CUT])
-        acc = products(2, 10, 12)
-        for e in (10, 11):
-            nc.scalar.activation(
-                handed[:, (e - 8) * C:(e - 7) * C], acc[:, (e - 10) * C:(e - 9) * C], IDENT, bias=bias[:, 2, e:e + 1]
-            )
-        sums_on_scalar(1, 9, 12)
-        sums_on_vector(0, 9, 12, y[0][:, 9 * C:S])
-        scatter_on_vector(0, 7, 9, in_rounded(1, 2))
-        nc.scalar.activation(windows[2][:].indirect(slots(8 * C + CUT, S)), handed[:, CUT:], COPY)
-        scatter_on_scalar(1, 9, 12)
-        scatter_on_vector(0, 9, 12, y[0][:, 9 * C:S])
+        sums_on_vector(0, 7, 10, last_sums)
+        scatter_on_vector(2, 8, 10, y[2][:, 8 * C:10 * C])
+        scatter_on_scalar(1, 8, 10)
+        sums_on_scalar(2, 10, 12)
+        sums_on_vector(0, 10, 12, y[0][:, 10 * C:S])
+        sums_on_scalar(1, 10, 12)
+        scatter_on_vector(0, 7, 10, last_sums)
+        scatter_on_scalar(2, 10, 12)
+        scatter_on_scalar(1, 10, 12)
+        scatter_on_vector(0, 10, 12, y[0][:, 10 * C:S])
         store(2, nc.scalar)
-        store(0, nc.sync)
         store(1, nc.scalar)
+        store(0, nc.sync)

@@ -28,6 +28,8 @@ RUN = 4
 BANK = P * RUN
 HALF = 6
 CUT = 192
+SHARED = 7.5
+MID = 5.5
 LOADS = (0, 2, 3, 5, 8, 12)
 CALLS = (
     ("short", 0, (0, 0, 2), (1, 0, 2)),
@@ -35,12 +37,16 @@ CALLS = (
     ("short", 2, (1, 3, 5)),
     ("long", 4, (0, 5, 9)),
     ("long", 1, (1, 5, 8)),
-    ("short", 3, (0, 9, 10)),
+    ("short", 4, (0, 9, 10)),
     ("long", 1, (1, 8, 12)),
     ("long", 1, (0, 10, 11)),
     ("long", 2, (0, 11, 12)),
 )
 DMA_ALIGN = 256
+
+
+def at(e):
+    return int(e * C)
 
 
 def tile_moe_pre_lin_bias_kernel(tc, xT, w_words, w_scales, b, gate, offs, out):
@@ -55,22 +61,22 @@ def tile_moe_pre_lin_bias_kernel(tc, xT, w_words, w_scales, b, gate, offs, out):
         identity = keep.tile([P, P], F32, name="identity")
         gate_cols = keep.tile([P, S // BANK, RUN], F32, name="gate_cols")
         gates = {lo: keep.tile([P, (hi - lo) * C], F32, name="gates%d" % lo) for lo, hi in ((0, 9), (8, 12))}
-        gated = keep.tile([P, PACK * HALF * C], F32, name="gated")
-        ranges = ((0, 6, 12), (1, 0, 3), (1, 3, 8), (1, 8, 12))
-        plain = {(a, lo): keep.tile([P, PACK * (hi - lo) * C], F32, name="plain%d_%d" % (a, lo))[:] for a, lo, hi in ranges[0::2]}
-        last = keep.tile([P, (2 * 4 + PACK * 3) * C], F32, name="last")
+        gated = keep.tile([P, PACK * at(HALF)], F32, name="gated")
+        ranges = ((0, HALF, 12), (1, 0, 3), (1, 3, 8), (1, 8, 12))
+        plain = {(a, lo): keep.tile([P, PACK * at(hi - lo)], F32, name="plain%d_%d" % (a, lo))[:] for a, lo, hi in ranges[0::2]}
+        last = keep.tile([P, (2 * 4 + PACK * 8) * C], F32, name="last")
         plain[(1, 0)] = last[:, 2 * 4 * C:]
         plain[(1, 8)] = last[:, 0:PACK * 4 * C]
         lanes = {"long": keep.tile([P, PACK * 8 * C], BF16, name="long_lane", align_bytes=64)}
-        lanes["short"] = shared.tile([P, PACK * 4 * C], BF16, name="short_lane", align_bytes=64, offset=0)
+        lanes["short"] = shared.tile([P, PACK * 5 * C + C], BF16, name="short_lane", align_bytes=64, offset=0)
         as_sums = lanes["long"][:].bitcast(F32)
         widths = [sum(hi - lo for a, lo, hi in call[2:]) * C for call in CALLS]
         codes = [keep.tile([P, w], U32, name="codes%d" % q, align_bytes=64) for q, w in enumerate(widths)]
         early = [
-            shared.tile([P, 2 * C], F32, name="early%d" % n, align_bytes=64, offset=at) for n, at in enumerate((5120, 6144))
+            shared.tile([P, 3 * C], F32, name="early%d" % n, align_bytes=64, offset=spot) for n, spot in enumerate((6144, 8192))
         ]
-        early.append(lanes["short"][:].bitcast(F32)[:, 3 * 2 * C:4 * 2 * C])
-        held_at = {2: 5120 - 128, 3: 5120 + 128, 4: 5120 + 640, 5: 6144, 6: 6144 + 256, 7: 0, 8: 128}
+        early.append(lanes["short"][:].bitcast(F32)[:, 4 * 2 * C:4 * 2 * C + at(8 - MID)])
+        held_at = {2: 6144 - 128, 3: 6144 + 128, 4: 6144 + 640, 5: 8192, 6: 8192 + 256, 7: 0, 8: 128}
         scales = []
         for q, w in enumerate(widths):
             if q in held_at:
@@ -124,18 +130,18 @@ def tile_moe_pre_lin_bias_kernel(tc, xT, w_words, w_scales, b, gate, offs, out):
             return offsets[:, lo // 16:hi // 16]
 
         def listed(lo, hi):
-            return slots(lo * C, hi * C)
+            return slots(at(lo), at(hi))
 
         def by_plane(staged):
             return staged.rearrange("p (t s) -> p t s", t=PACK)
 
         def ungated(a, lo, hi):
             first = max(start for piece, start, stop in ranges if piece == a and start <= lo)
-            return by_plane(plain[(a, first)])[:, :, (lo - first) * C:(hi - first) * C]
+            return by_plane(plain[(a, first)])[:, :, at(lo - first):at(hi - first)]
 
         def gather_gated(t):
             nc.vector.tensor_tensor(
-                by_plane(gated[:])[:, t, :], planes[t][:].indirect(listed(0, HALF)), gates[0][:, 0:HALF * C], MULT
+                by_plane(gated[:])[:, t, :], planes[t][:].indirect(listed(0, HALF)), gates[0][:, 0:at(HALF)], MULT
             )
 
         def gather_on_vector(a, t, lo, hi):
@@ -145,15 +151,15 @@ def tile_moe_pre_lin_bias_kernel(tc, xT, w_words, w_scales, b, gate, offs, out):
             nc.scalar.activation(ungated(a, lo, hi)[:, t, :], planes[a * PACK + t][:].indirect(listed(lo, hi)), COPY)
 
         def woven(a, lo, hi):
-            q, block = place[(a, lo)]
-            at = (CALLS[q][1] + block) * C
-            return lanes[CALLS[q][0]][:, PACK * at:PACK * (at + (hi - lo) * C)].rearrange("p (line i t) -> p line t i", i=RUN, t=PACK)
+            q, block = place[(a, int(lo))]
+            first = at(CALLS[q][1] + block + lo - int(lo))
+            return lanes[CALLS[q][0]][:, PACK * first:PACK * (first + at(hi - lo))].rearrange("p (line i t) -> p line t i", i=RUN, t=PACK)
 
         def by_runs(source):
             return source.rearrange("p t (line i) -> p line t i", i=RUN)
 
         def times_gate(engine, factor, a, lo, hi):
-            lines = (hi - lo) * C // RUN
+            lines = at(hi - lo) // RUN
             engine.tensor_tensor(
                 woven(a, lo, hi), by_runs(ungated(a, lo, hi)), factor.unsqueeze(2).to_broadcast([P, lines, PACK, RUN]), MULT
             )
@@ -163,16 +169,16 @@ def tile_moe_pre_lin_bias_kernel(tc, xT, w_words, w_scales, b, gate, offs, out):
             times_gate(nc.vector, spread[lo * C // BANK][:, first:first + (hi - lo) * C // RUN, :], a, lo, hi)
 
         def round_on_gpsimd(lo, hi):
-            nc.gpsimd.tensor_scalar(woven(0, lo, hi), by_runs(by_plane(gated[:])[:, :, lo * C:hi * C]), 1.0, 0.0, MULT, ADD)
+            nc.gpsimd.tensor_scalar(woven(0, lo, hi), by_runs(by_plane(gated[:])[:, :, at(lo):at(hi)]), 1.0, 0.0, MULT, ADD)
 
         def gate_on_gpsimd(a, lo, hi):
             first = 0 if hi <= 9 else 8
-            factor = gates[first][:, (lo - first) * C:(hi - first) * C].rearrange("p (line i) -> p line i", i=RUN)
+            factor = gates[first][:, at(lo - first):at(hi - first)].rearrange("p (line i) -> p line i", i=RUN)
             times_gate(nc.gpsimd, factor, a, lo, hi)
 
         def quantize(q):
-            at = CALLS[q][1] * C
-            source = lanes[CALLS[q][0]][:, PACK * at:PACK * (at + widths[q])]
+            first = CALLS[q][1] * C
+            source = lanes[CALLS[q][0]][:, PACK * first:PACK * (first + widths[q])]
             nc.vector.quantize_mx(out=codes[q][:].bitcast(FP8X4), scales=scales[q][:], in_=source)
 
         def products(c, first, end):
@@ -180,11 +186,11 @@ def tile_moe_pre_lin_bias_kernel(tc, xT, w_words, w_scales, b, gate, offs, out):
             for a in range(PASSES):
                 for e in range(first, end):
                     load = max(lo for lo in LOADS if lo <= e)
-                    at = ((e - load) * PASSES + a) * N + c * P
+                    column = ((e - load) * PASSES + a) * N + c * P
                     q, block = place[(a, e)]
                     nc.tensor.matmul_mx(
                         out=acc[:, (e - first) * C:(e - first + 1) * C],
-                        lhsT=words[load][:, at:at + P].bitcast(FP8X4),
+                        lhsT=words[load][:, column:column + P].bitcast(FP8X4),
                         lhsT_scale=weight_scales(e, a, c),
                         rhs=codes[q][:, block * C:(block + 1) * C].bitcast(FP8X4),
                         rhs_scale=scales[q][:, block * C:(block + 1) * C],
@@ -201,7 +207,7 @@ def tile_moe_pre_lin_bias_kernel(tc, xT, w_words, w_scales, b, gate, offs, out):
                 )
 
         def scatter_on_scalar(c, first, end):
-            nc.scalar.activation(windows[c][:].indirect(listed(first, end)), y[c][:, first * C:end * C], COPY)
+            nc.scalar.activation(windows[c][:].indirect(listed(first, end)), y[c][:, at(first):at(end)], COPY)
 
         def sums_on_vector(c, first, end, home):
             acc = products(c, first, end)
@@ -211,6 +217,10 @@ def tile_moe_pre_lin_bias_kernel(tc, xT, w_words, w_scales, b, gate, offs, out):
                 acc[:].rearrange("p (e s) -> p e s", s=C),
                 ADD,
             )
+
+        def part_on_vector(c, acc, first, lo, hi, home):
+            spread_bias = bias[:, c, int(lo):int(lo) + 1].to_broadcast([P, at(hi - lo)])
+            nc.vector.tensor_tensor(home, spread_bias, acc[:, at(lo - first):at(hi - first)], ADD)
 
         def scatter_on_vector(c, first, end, home):
             nc.vector.tensor_copy(windows[c][:].indirect(listed(first, end)), home)
@@ -224,8 +234,8 @@ def tile_moe_pre_lin_bias_kernel(tc, xT, w_words, w_scales, b, gate, offs, out):
             scatter_on_scalar(c, first, end)
 
         def in_rounded(block, experts):
-            at = block * C * PACK // 2
-            return as_sums[:, at:at + experts * C]
+            first = block * C * PACK // 2
+            return as_sums[:, first:first + experts * C]
 
         def store(c, queue):
             queue.dma_start(out=out[c * P:(c + 1) * P, :], in_=windows[c][:])
@@ -265,9 +275,10 @@ def tile_moe_pre_lin_bias_kernel(tc, xT, w_words, w_scales, b, gate, offs, out):
         for t in range(PACK):
             gather_gated(t)
             gather_on_scalar(0, t, HALF, E)
+        gate_on_gpsimd(0, HALF, 9)
         round_on_gpsimd(0, 2)
         round_on_gpsimd(2, HALF)
-        gate_on_gpsimd(0, 6, 9)
+        gate_on_vector(0, 9, 10)
 
         gather_on_vector(1, 0, 0, 3)
         gather_on_vector(1, 0, 3, 6)
@@ -283,65 +294,75 @@ def tile_moe_pre_lin_bias_kernel(tc, xT, w_words, w_scales, b, gate, offs, out):
             gather_on_scalar(1, t, 3, 8)
         gate_on_vector(1, 0, 2)
         gate_on_vector(1, 2, 3)
-        for t in (2, 3):
-            gather_on_scalar(1, t, 8, 12)
+        gather_on_vector(1, 3, 8, 9)
+        gather_on_scalar(1, 3, 9, 12)
+        gather_on_scalar(1, 2, 8, 12)
         quantize(0)
         quantize(1)
 
         gate_on_gpsimd(1, 5, 8)
         gate_on_vector(1, 3, 4)
         gate_on_vector(1, 4, 5)
+        sums_on_scalar(1, 0, 2)
         first_banks = {c: products(c, 0, 2) for c in (2, 0)}
         for c, home in ((2, early[0]), (0, y[0])):
             for lo, hi in ((0, C), (C, CUT)):
                 spread_bias = bias[:, c, lo // C:lo // C + 1].to_broadcast([P, hi - lo])
                 nc.vector.tensor_tensor(home[:, lo:hi], spread_bias, first_banks[c][:, lo:hi], ADD)
-        sums_on_scalar(1, 0, 3)
-        for c in (2, 0):
-            nc.scalar.activation(y[c][:, CUT:2 * C], first_banks[c][:, CUT:2 * C], IDENT, bias=bias[:, c, 1:2])
+        nc.scalar.activation(y[2][:, CUT:2 * C], first_banks[2][:, CUT:2 * C], IDENT, bias=bias[:, 2, 1:2])
+        scatter_on_scalar(1, 0, 2)
+        nc.scalar.activation(y[0][:, CUT:2 * C], first_banks[0][:, CUT:2 * C], IDENT, bias=bias[:, 0, 1:2])
+        for c in (2, 0, 1):
             sums_on_scalar(c, 2, 3)
         nc.vector.tensor_copy(windows[2][:].indirect(slots(0, CUT)), early[0][:, 0:CUT])
         nc.vector.tensor_copy(windows[0][:].indirect(slots(0, CUT)), y[0][:, 0:CUT])
-        scatter_on_scalar(1, 0, 3)
-        for c in (0, 2):
+        for c in (2, 0):
             nc.scalar.activation(windows[c][:].indirect(slots(CUT, 3 * C)), y[c][:, CUT:3 * C], COPY)
         for q in (2, 3, 4):
             quantize(q)
 
         gate_on_gpsimd(1, 8, 12)
-        gate_on_vector(0, 9, 10)
-        sums_on_vector(0, 3, 5, early[1][:])
         sums_on_vector(2, 3, 5, y[2][:, 3 * C:5 * C])
-        sums_on_scalar(1, 3, 6)
-        sums_on_scalar(2, 5, 8)
-        scatter_on_vector(0, 3, 5, early[1][:])
+        sums_on_scalar(1, 3, 5)
+        sums_on_vector(0, 3, 5, early[1][:, 0:2 * C])
         scatter_on_vector(2, 3, 5, y[2][:, 3 * C:5 * C])
-        scatter_on_scalar(1, 3, 6)
+        split = products(0, 5, 6)
+        part_on_vector(0, split, 5, 5, MID, early[1][:, 2 * C:at(MID - 3)])
+        sums_on_vector(2, 5, 6, y[2][:, 5 * C:6 * C])
+        scatter_on_scalar(1, 2, 5)
+        sums_on_scalar(2, 6, 8)
+        sums_on_scalar(1, 5, 6)
+        scatter_on_vector(0, 3, MID, early[1][:, 0:at(MID - 3)])
+        scatter_on_scalar(2, 5, 8)
+        kept = products(1, 6, 8)
+        part_on_vector(1, kept, 6, 6, 7, y[1][:, 6 * C:7 * C])
         quantize(5)
         quantize(6)
 
         gate_on_gpsimd(0, 10, 12)
-        sums_on_vector(0, 5, 7, early[2])
-        sums_on_vector(1, 6, 8, in_rounded(4, 2))
-        scatter_on_vector(0, 5, 7, early[2])
-        scatter_on_scalar(2, 5, 8)
-        nc.scalar.activation(windows[1][:].indirect(listed(6, 8)), in_rounded(4, 2), COPY)
-        sums_on_vector(2, 8, 10, y[2][:, 8 * C:10 * C])
-        sums_on_scalar(1, 8, 10)
+        part_on_vector(0, split, 5, MID, 6, early[2][:, 0:at(6 - MID)])
+        sums_on_vector(0, 6, 8, early[2][:, at(6 - MID):])
+        part_on_vector(1, kept, 6, 7, SHARED, y[1][:, 7 * C:at(SHARED)])
+        scatter_on_vector(0, MID, 8, early[2])
+        sums_on_scalar(2, 8, 10)
+        scatter_on_scalar(1, 5, SHARED)
+        scatter_on_scalar(2, 8, 10)
         quantize(7)
         quantize(8)
-        last_sums = as_sums[:, C:PACK * C]
 
-        sums_on_vector(0, 7, 10, last_sums)
-        scatter_on_vector(2, 8, 10, y[2][:, 8 * C:10 * C])
-        scatter_on_scalar(1, 8, 10)
+        handed = in_rounded(2, 2)[:, 0:at(9 - SHARED)]
+        sums_on_vector(0, 8, 10, in_rounded(1, 2))
+        part_on_vector(1, kept, 6, SHARED, 8, handed[:, 0:at(8 - SHARED)])
+        sums_on_vector(1, 8, 9, handed[:, at(8 - SHARED):])
+        scatter_on_vector(0, 8, 10, in_rounded(1, 2))
         sums_on_scalar(2, 10, 12)
+        sums_on_scalar(1, 9, 10)
         sums_on_vector(0, 10, 12, y[0][:, 10 * C:S])
-        sums_on_scalar(1, 10, 12)
-        scatter_on_vector(0, 7, 10, last_sums)
+        scatter_on_vector(1, SHARED, 9, handed)
         scatter_on_scalar(2, 10, 12)
-        scatter_on_scalar(1, 10, 12)
+        sums_on_scalar(1, 10, 12)
         scatter_on_vector(0, 10, 12, y[0][:, 10 * C:S])
-        store(2, nc.scalar)
-        store(1, nc.scalar)
+        scatter_on_scalar(1, 9, 12)
+        store(2, nc.sync)
         store(0, nc.sync)
+        store(1, nc.scalar)

@@ -294,8 +294,7 @@ def tile_moe_pre_lin_bias_kernel(tc, xT, w_words, w_scales, b, gate, offs, out):
             gather_on_scalar(1, t, 3, 8)
         gate_on_vector(1, 0, 2)
         gate_on_vector(1, 2, 3)
-        gather_on_vector(1, 3, 8, 9)
-        gather_on_scalar(1, 3, 9, 12)
+        gather_on_scalar(1, 3, 8, 12)
         gather_on_scalar(1, 2, 8, 12)
         quantize(0)
         quantize(1)

@@ -28,19 +28,16 @@ RUN = 4
 BANK = P * RUN
 HALF = 6
 CUT = 192
-SHARED = 7.5
-MID = 5.5
+SHARED = 6.5
 LOADS = (0, 2, 3, 5, 8, 12)
 CALLS = (
     ("short", 0, (0, 0, 2), (1, 0, 2)),
     ("long", 0, (1, 2, 3), (0, 2, 5)),
-    ("short", 2, (1, 3, 5)),
+    ("short", 2, (1, 3, 5), (0, 9, 11)),
     ("long", 4, (0, 5, 9)),
     ("long", 1, (1, 5, 8)),
-    ("short", 4, (0, 9, 10)),
-    ("long", 1, (1, 8, 12)),
-    ("long", 1, (0, 10, 11)),
-    ("long", 2, (0, 11, 12)),
+    ("long", 1, (1, 8, 10)),
+    ("long", 3, (1, 10, 12), (0, 11, 12)),
 )
 DMA_ALIGN = 256
 
@@ -68,15 +65,14 @@ def tile_moe_pre_lin_bias_kernel(tc, xT, w_words, w_scales, b, gate, offs, out):
         plain[(1, 0)] = last[:, 2 * 4 * C:]
         plain[(1, 8)] = last[:, 0:PACK * 4 * C]
         lanes = {"long": keep.tile([P, PACK * 8 * C], BF16, name="long_lane", align_bytes=64)}
-        lanes["short"] = shared.tile([P, PACK * 5 * C + C], BF16, name="short_lane", align_bytes=64, offset=0)
-        as_sums = lanes["long"][:].bitcast(F32)
+        lanes["short"] = keep.tile([P, PACK * 6 * C], BF16, name="short_lane", align_bytes=64)
         widths = [sum(hi - lo for a, lo, hi in call[2:]) * C for call in CALLS]
         codes = [keep.tile([P, w], U32, name="codes%d" % q, align_bytes=64) for q, w in enumerate(widths)]
         early = [
-            shared.tile([P, 3 * C], F32, name="early%d" % n, align_bytes=64, offset=spot) for n, spot in enumerate((6144, 8192))
+            shared.tile([P, CUT], F32, name="early0", align_bytes=64, offset=384),
+            shared.tile([P, 4 * C], F32, name="early1", align_bytes=64, offset=2048),
         ]
-        early.append(lanes["short"][:].bitcast(F32)[:, 4 * 2 * C:4 * 2 * C + at(8 - MID)])
-        held_at = {2: 6144 - 128, 3: 6144 + 128, 4: 6144 + 640, 5: 8192, 6: 8192 + 256, 7: 0, 8: 128}
+        held_at = {2: 0, 3: 512, 4: 1024, 5: 2048, 6: 2048 + 256}
         scales = []
         for q, w in enumerate(widths):
             if q in held_at:
@@ -233,10 +229,6 @@ def tile_moe_pre_lin_bias_kernel(tc, xT, w_words, w_scales, b, gate, offs, out):
             sums_on_scalar(c, first, end)
             scatter_on_scalar(c, first, end)
 
-        def in_rounded(block, experts):
-            first = block * C * PACK // 2
-            return as_sums[:, first:first + experts * C]
-
         def store(c, queue):
             queue.dma_start(out=out[c * P:(c + 1) * P, :], in_=windows[c][:])
 
@@ -278,7 +270,7 @@ def tile_moe_pre_lin_bias_kernel(tc, xT, w_words, w_scales, b, gate, offs, out):
         gate_on_gpsimd(0, HALF, 9)
         round_on_gpsimd(0, 2)
         round_on_gpsimd(2, HALF)
-        gate_on_vector(0, 9, 10)
+        gate_on_vector(0, 9, 11)
 
         gather_on_vector(1, 0, 0, 3)
         gather_on_vector(1, 0, 3, 6)
@@ -320,48 +312,36 @@ def tile_moe_pre_lin_bias_kernel(tc, xT, w_words, w_scales, b, gate, offs, out):
         for q in (2, 3, 4):
             quantize(q)
 
+        gate_on_gpsimd(0, 11, 12)
         gate_on_gpsimd(1, 8, 12)
         sums_on_vector(2, 3, 5, y[2][:, 3 * C:5 * C])
         sums_on_scalar(1, 3, 5)
         sums_on_vector(0, 3, 5, early[1][:, 0:2 * C])
         scatter_on_vector(2, 3, 5, y[2][:, 3 * C:5 * C])
-        split = products(0, 5, 6)
-        part_on_vector(0, split, 5, 5, MID, early[1][:, 2 * C:at(MID - 3)])
-        sums_on_vector(2, 5, 6, y[2][:, 5 * C:6 * C])
+        sums_on_vector(0, 5, 7, early[1][:, 2 * C:])
         scatter_on_scalar(1, 2, 5)
-        sums_on_scalar(2, 6, 8)
-        sums_on_scalar(1, 5, 6)
-        scatter_on_vector(0, 3, MID, early[1][:, 0:at(MID - 3)])
+        sums_on_scalar(1, 5, 7)
+        sums_on_scalar(2, 5, 8)
+        scatter_on_vector(0, 3, 7, early[1][:])
+        scatter_on_scalar(1, 5, SHARED)
         scatter_on_scalar(2, 5, 8)
-        kept = products(1, 6, 8)
-        part_on_vector(1, kept, 6, 6, 7, y[1][:, 6 * C:7 * C])
+        sums_on_vector(1, 7, 8, y[1][:, 7 * C:8 * C])
         quantize(5)
         quantize(6)
 
-        gate_on_gpsimd(0, 10, 12)
-        part_on_vector(0, split, 5, MID, 6, early[2][:, 0:at(6 - MID)])
-        sums_on_vector(0, 6, 8, early[2][:, at(6 - MID):])
-        part_on_vector(1, kept, 6, 7, SHARED, y[1][:, 7 * C:at(SHARED)])
-        scatter_on_vector(0, MID, 8, early[2])
+        scatter_on_vector(1, SHARED, 8, y[1][:, at(SHARED):8 * C])
         sums_on_scalar(2, 8, 10)
-        scatter_on_scalar(1, 5, SHARED)
+        sums_on_scalar(1, 8, 10)
+        sums_on_vector(0, 7, 10, y[0][:, 7 * C:10 * C])
         scatter_on_scalar(2, 8, 10)
-        quantize(7)
-        quantize(8)
-
-        handed = in_rounded(2, 2)[:, 0:at(9 - SHARED)]
-        sums_on_vector(0, 8, 10, in_rounded(1, 2))
-        part_on_vector(1, kept, 6, SHARED, 8, handed[:, 0:at(8 - SHARED)])
-        sums_on_vector(1, 8, 9, handed[:, at(8 - SHARED):])
-        scatter_on_vector(0, 8, 10, in_rounded(1, 2))
         sums_on_scalar(2, 10, 12)
-        sums_on_scalar(1, 9, 10)
-        sums_on_vector(0, 10, 12, y[0][:, 10 * C:S])
-        scatter_on_vector(1, SHARED, 9, handed)
-        scatter_on_scalar(2, 10, 12)
         sums_on_scalar(1, 10, 12)
+        sums_on_vector(0, 10, 12, y[0][:, 10 * C:S])
+        scatter_on_vector(0, 7, 10, y[0][:, 7 * C:10 * C])
+        scatter_on_scalar(2, 10, 12)
         scatter_on_vector(0, 10, 12, y[0][:, 10 * C:S])
-        scatter_on_scalar(1, 9, 12)
+        scatter_on_scalar(1, 10, 12)
+        scatter_on_scalar(1, 8, 10)
         store(2, nc.sync)
         store(0, nc.sync)
         store(1, nc.scalar)

from contextlib import ExitStack

import concourse.mybir as mybir
from concourse.masks import make_identity

K, T, E, C, N = 1024, 1536, 12, 128, 384
S = E * C
FLOPS = 2 * K * N * S
BYTES = 4 * K * T + E * K * N + E * K * N // 32 + 4 * N * E + 4 * S + 2 * S + 4 * N * T

F32 = mybir.dt.float32
BF16 = mybir.dt.bfloat16
I32 = mybir.dt.int32
U32 = mybir.dt.uint32
U16 = mybir.dt.uint16
U8 = mybir.dt.uint8
FP8X4 = mybir.dt.float8_e4m3fn_x4
COPY = mybir.ActivationFunctionType.Copy
IDENT = mybir.ActivationFunctionType.Identity
MULT = mybir.AluOpType.mult
ADD = mybir.AluOpType.add

P = 128
PACK = 4
PASSES = 2
NT = N // P
RUN = 4
BANK = P * RUN
HALF = 6
CUT = 192
SHARED = 6.5
LOADS = (0, 2, 3, 5, 8, 12)
CALLS = (
    ("short", 0, (0, 0, 2), (1, 0, 2)),
    ("long", 0, (1, 2, 3), (0, 2, 5)),
    ("short", 2, (1, 3, 5), (0, 9, 11)),
    ("long", 4, (0, 5, 9)),
    ("long", 1, (1, 5, 8)),
    ("long", 1, (1, 8, 10)),
    ("long", 3, (1, 10, 12), (0, 11, 12)),
)
DMA_ALIGN = 256


def at(e):
    return int(e * C)


def tile_moe_pre_lin_bias_kernel(tc, xT, w_words, w_scales, b, gate, offs, out):
    nc = tc.nc
    with ExitStack() as ctx:
        keep = ctx.enter_context(tc.tile_pool(name="keep", bufs=1))
        shared = ctx.enter_context(tc.tile_pool(name="shared", bufs=1))
        psum = ctx.enter_context(tc.psum_pool(name="psum", bufs=8))

        offsets = keep.tile([P, S // 16], U16, name="offsets")
        planes = [keep.tile([P, T], F32, name="plane%d" % i, align_bytes=DMA_ALIGN) for i in range(PASSES * PACK)]
        identity = keep.tile([P, P], F32, name="identity")
        gate_cols = keep.tile([P, S // BANK, RUN], F32, name="gate_cols")
        gates = {lo: keep.tile([P, (hi - lo) * C], F32, name="gates%d" % lo) for lo, hi in ((0, 9), (8, 12))}
        gated = keep.tile([P, PACK * at(HALF)], F32, name="gated")
        ranges = ((0, HALF, 12), (1, 0, 3), (1, 3, 8), (1, 8, 12))
        plain = {(a, lo): keep.tile([P, PACK * at(hi - lo)], F32, name="plain%d_%d" % (a, lo))[:] for a, lo, hi in ranges[0::2]}
        last = keep.tile([P, (2 * 4 + PACK * 8) * C], F32, name="last")
        plain[(1, 0)] = last[:, 2 * 4 * C:]
        plain[(1, 8)] = last[:, 0:PACK * 4 * C]
        lanes = {"long": keep.tile([P, PACK * 8 * C], BF16, name="long_lane", align_bytes=64)}
        lanes["short"] = keep.tile([P, PACK * 6 * C], BF16, name="short_lane", align_bytes=64)
        widths = [sum(hi - lo for a, lo, hi in call[2:]) * C for call in CALLS]
        codes = [keep.tile([P, w], U32, name="codes%d" % q, align_bytes=64) for q, w in enumerate(widths)]
        early = [
            shared.tile([P, CUT], F32, name="early0", align_bytes=64, offset=384),
            shared.tile([P, 4 * C], F32, name="early1", align_bytes=64, offset=2048),
        ]
        held_at = {2: 0, 3: 512, 4: 1024, 5: 2048, 6: 2048 + 256}
        scales = []
        for q, w in enumerate(widths):
            if q in held_at:
                scales.append(shared.tile([P, w], U8, name="scales%d" % q, align_bytes=64, offset=held_at[q]))
            else:
                scales.append(keep.tile([P, w], U8, name="scales%d" % q, align_bytes=64))
        place = {}
        for q, call in enumerate(CALLS):
            block = 0
            for a, lo, hi in call[2:]:
                for e in range(lo, hi):
                    place[(a, e)] = (q, block)
                    block += 1
        words = {
            lo: keep.tile([P, (hi - lo) * PASSES * N], U32, name="words%d" % lo, align_bytes=64)
            for lo, hi in zip(LOADS, LOADS[1:])
        }
        scale_rows = [keep.tile([P, N], U8, name="scale_rows%d" % pair, align_bytes=64) for pair in range(E // 2)]
        bias = keep.tile([P, NT, E], F32, name="bias")
        y = [keep.tile([P, S], F32, name="y%d" % c) for c in range(NT)]
        windows = [keep.tile([P, T], F32, name="window%d" % c, align_bytes=DMA_ALIGN) for c in range(NT)]

        rows = xT.rearrange("(a p t) token -> a t p token", a=PASSES, t=PACK)

        def load_weights(lo, hi):
            source = w_words[lo:hi].rearrange("e a p n t -> p (e a) (n t)")
            nc.sync.dma_start(out=words[lo][:].bitcast(I32).rearrange("p (m n) -> p m n", n=N), in_=source.bitcast(I32))

        def load_scale_rows(pair):
            for quad in range(4):
                source = w_scales[2 * pair:2 * pair + 2, :, 4 * quad:4 * quad + 4, :]
                nc.sync.dma_start(
                    out=scale_rows[pair][32 * quad:32 * quad + 16, :].bitcast(I32),
                    in_=source.rearrange("e a r n -> (e a) r n").bitcast(I32),
                )

        def load_gates(lo, hi):
            first = max(start for start in gates if start <= lo)
            nc.sync.dma_start(out=gates[first][:, (lo - first) * C:(hi - first) * C], in_=gate[0:P, lo * C:hi * C])

        def weight_scales(e, a, c):
            return scale_rows[e // 2][4 * (e % 2 * PASSES + a):P, c * P:(c + 1) * P]

        def spread_gate(n):
            bank = psum.tile([P, RUN, P], F32, name="bank")
            for i in range(RUN):
                nc.tensor.transpose(bank[:, i, :], gate_cols[:, n, i:i + 1].to_broadcast([P, P]), identity[:])
            return bank[:].rearrange("p i line -> p line i")

        def slots(lo, hi):
            return offsets[:, lo // 16:hi // 16]

        def listed(lo, hi):
            return slots(at(lo), at(hi))

        def by_plane(staged):
            return staged.rearrange("p (t s) -> p t s", t=PACK)

        def ungated(a, lo, hi):
            first = max(start for piece, start, stop in ranges if piece == a and start <= lo)
            return by_plane(plain[(a, first)])[:, :, at(lo - first):at(hi - first)]

        def gather_gated(t):
            nc.vector.tensor_tensor(
                by_plane(gated[:])[:, t, :], planes[t][:].indirect(listed(0, HALF)), gates[0][:, 0:at(HALF)], MULT
            )

        def gather_on_vector(a, t, lo, hi):
            nc.vector.tensor_copy(ungated(a, lo, hi)[:, t, :], planes[a * PACK + t][:].indirect(listed(lo, hi)))

        def gather_on_scalar(a, t, lo, hi):
            nc.scalar.activation(ungated(a, lo, hi)[:, t, :], planes[a * PACK + t][:].indirect(listed(lo, hi)), COPY)

        def woven(a, lo, hi):
            q, block = place[(a, int(lo))]
            first = at(CALLS[q][1] + block + lo - int(lo))
            return lanes[CALLS[q][0]][:, PACK * first:PACK * (first + at(hi - lo))].rearrange("p (line i t) -> p line t i", i=RUN, t=PACK)

        def by_runs(source):
            return source.rearrange("p t (line i) -> p line t i", i=RUN)

        def times_gate(engine, factor, a, lo, hi):
            lines = at(hi - lo) // RUN
            engine.tensor_tensor(
                woven(a, lo, hi), by_runs(ungated(a, lo, hi)), factor.unsqueeze(2).to_broadcast([P, lines, PACK, RUN]), MULT
            )

        def gate_on_vector(a, lo, hi):
            first = lo * C % BANK // RUN
            times_gate(nc.vector, spread[lo * C // BANK][:, first:first + (hi - lo) * C // RUN, :], a, lo, hi)

        def round_on_gpsimd(lo, hi):
            nc.gpsimd.tensor_scalar(woven(0, lo, hi), by_runs(by_plane(gated[:])[:, :, at(lo):at(hi)]), 1.0, 0.0, MULT, ADD)

        def gate_on_gpsimd(a, lo, hi):
            first = 0 if hi <= 9 else 8
            factor = gates[first][:, at(lo - first):at(hi - first)].rearrange("p (line i) -> p line i", i=RUN)
            times_gate(nc.gpsimd, factor, a, lo, hi)

        def quantize(q):
            first = CALLS[q][1] * C
            source = lanes[CALLS[q][0]][:, PACK * first:PACK * (first + widths[q])]
            nc.vector.quantize_mx(out=codes[q][:].bitcast(FP8X4), scales=scales[q][:], in_=source)

        def products(c, first, end):
            acc = psum.tile([P, (end - first) * C], F32, name="bank")
            for a in range(PASSES):
                for e in range(first, end):
                    load = max(lo for lo in LOADS if lo <= e)
                    column = ((e - load) * PASSES + a) * N + c * P
                    q, block = place[(a, e)]
                    nc.tensor.matmul_mx(
                        out=acc[:, (e - first) * C:(e - first + 1) * C],
                        lhsT=words[load][:, column:column + P].bitcast(FP8X4),
                        lhsT_scale=weight_scales(e, a, c),
                        rhs=codes[q][:, block * C:(block + 1) * C].bitcast(FP8X4),
                        rhs_scale=scales[q][:, block * C:(block + 1) * C],
                        start=(a == 0 and e == first),
                        stop=(a == PASSES - 1 and e == end - 1),
                    )
            return acc

        def sums_on_scalar(c, first, end):
            acc = products(c, first, end)
            for e in range(first, end):
                nc.scalar.activation(
                    y[c][:, e * C:(e + 1) * C], acc[:, (e - first) * C:(e - first + 1) * C], IDENT, bias=bias[:, c, e:e + 1]
                )

        def scatter_on_scalar(c, first, end):
            nc.scalar.activation(windows[c][:].indirect(listed(first, end)), y[c][:, at(first):at(end)], COPY)

        def sums_on_vector(c, first, end, home):
            acc = products(c, first, end)
            nc.vector.tensor_tensor(
                home.rearrange("p (e s) -> p e s", s=C),
                bias[:, c, first:end].unsqueeze(2).to_broadcast([P, end - first, C]),
                acc[:].rearrange("p (e s) -> p e s", s=C),
                ADD,
            )

        def part_on_vector(c, acc, first, lo, hi, home):
            spread_bias = bias[:, c, int(lo):int(lo) + 1].to_broadcast([P, at(hi - lo)])
            nc.vector.tensor_tensor(home, spread_bias, acc[:, at(lo - first):at(hi - first)], ADD)

        def scatter_on_vector(c, first, end, home):
            nc.vector.tensor_copy(windows[c][:].indirect(listed(first, end)), home)

        def finish_on_vector(c, first, end, home):
            sums_on_vector(c, first, end, home)
            scatter_on_vector(c, first, end, home)

        def finish_on_scalar(c, first, end):
            sums_on_scalar(c, first, end)
            scatter_on_scalar(c, first, end)

        def store(c, queue):
            queue.dma_start(out=out[c * P:(c + 1) * P, :], in_=windows[c][:])

        zero = keep.tile([P, 1], F32, name="zero")
        unread = keep.tile([P, 1], F32, name="unread")
        nc.gpsimd.memset(zero[:], 0.0)
        nc.scalar.activation(unread[:], zero[:], COPY)
        for rows_of_pair in scale_rows:
            nc.vector.memset(rows_of_pair[:].bitcast(I32), 0)
        make_identity(nc, identity[:])

        nc.sync.dma_start(out=gate_cols[:], in_=gate[0, :].rearrange("(n p i) -> p n i", p=P, i=RUN))
        nc.sync.dma_start(offsets[:], offs)
        for i in range(PASSES * PACK):
            nc.sync.dma_start(out=planes[i][:], in_=rows[i // PACK, i % PACK])
        load_scale_rows(0)
        load_weights(0, 2)
        nc.sync.dma_start(out=bias[:], in_=b.rearrange("(c p) e -> p c e", p=P))
        load_scale_rows(1)
        load_weights(2, 3)
        load_weights(3, 5)
        load_gates(8, 12)
        load_scale_rows(2)
        load_weights(5, 8)
        load_scale_rows(3)
        load_weights(8, 12)
        load_scale_rows(4)
        load_scale_rows(5)

        spread = [spread_gate(n) for n in range(S // BANK)]
        by_line = gates[0][:].rearrange("p (line i) -> p line i", i=RUN)
        for n in range(2):
            nc.vector.tensor_copy(by_line[:, n * P:(n + 1) * P, :], spread[n])
        nc.vector.tensor_copy(by_line[:, 2 * P:, :], spread[2][:, 0:C // RUN, :])

        for t in range(PACK):
            gather_gated(t)
            gather_on_scalar(0, t, HALF, E)
        gate_on_gpsimd(0, HALF, 9)
        round_on_gpsimd(0, 2)
        round_on_gpsimd(2, HALF)
        gate_on_vector(0, 9, 11)

        gather_on_vector(1, 0, 0, 3)
        gather_on_vector(1, 0, 3, 6)
        gather_on_scalar(1, 0, 6, 8)
        gather_on_scalar(1, 0, 8, 12)
        gather_on_vector(1, 1, 0, 3)
        gather_on_scalar(1, 1, 3, 8)
        gather_on_scalar(1, 1, 8, 12)
        gather_on_vector(1, 2, 0, 3)
        gather_on_vector(1, 3, 0, 2)
        gather_on_vector(1, 3, 2, 3)
        for t in (2, 3):
            gather_on_scalar(1, t, 3, 8)
        gate_on_vector(1, 0, 2)
        gate_on_vector(1, 2, 3)
        gather_on_scalar(1, 3, 8, 12)
        gather_on_scalar(1, 2, 8, 12)
        quantize(0)
        quantize(1)

        gate_on_gpsimd(1, 5, 8)
        gate_on_vector(1, 3, 4)
        gate_on_vector(1, 4, 5)
        sums_on_scalar(1, 0, 2)
        first_banks = {c: products(c, 0, 2) for c in (2, 0)}
        for c, home in ((2, early[0]), (0, y[0])):
            for lo, hi in ((0, C), (C, CUT)):
                spread_bias = bias[:, c, lo // C:lo // C + 1].to_broadcast([P, hi - lo])
                nc.vector.tensor_tensor(home[:, lo:hi], spread_bias, first_banks[c][:, lo:hi], ADD)
        nc.scalar.activation(y[2][:, CUT:2 * C], first_banks[2][:, CUT:2 * C], IDENT, bias=bias[:, 2, 1:2])
        scatter_on_scalar(1, 0, 2)
        nc.scalar.activation(y[0][:, CUT:2 * C], first_banks[0][:, CUT:2 * C], IDENT, bias=bias[:, 0, 1:2])
        for c in (2, 0, 1):
            sums_on_scalar(c, 2, 3)
        nc.vector.tensor_copy(windows[2][:].indirect(slots(0, CUT)), early[0][:, 0:CUT])
        nc.vector.tensor_copy(windows[0][:].indirect(slots(0, CUT)), y[0][:, 0:CUT])
        for c in (2, 0):
            nc.scalar.activation(windows[c][:].indirect(slots(CUT, 3 * C)), y[c][:, CUT:3 * C], COPY)
        for q in (2, 3, 4):
            quantize(q)

        gate_on_gpsimd(0, 11, 12)
        gate_on_gpsimd(1, 8, 12)
        sums_on_vector(2, 3, 5, y[2][:, 3 * C:5 * C])
        sums_on_scalar(1, 3, 5)
        sums_on_vector(0, 3, 5, early[1][:, 0:2 * C])
        scatter_on_vector(2, 3, 5, y[2][:, 3 * C:5 * C])
        sums_on_vector(0, 5, 7, early[1][:, 2 * C:])
        scatter_on_scalar(1, 2, 5)
        sums_on_scalar(1, 5, 7)
        sums_on_scalar(2, 5, 8)
        scatter_on_vector(0, 3, 7, early[1][:])
        scatter_on_scalar(1, 5, SHARED)
        scatter_on_scalar(2, 5, 8)
        sums_on_vector(1, 7, 8, y[1][:, 7 * C:8 * C])
        quantize(5)
        quantize(6)

        scatter_on_vector(1, SHARED, 8, y[1][:, at(SHARED):8 * C])
        sums_on_scalar(2, 8, 10)
        sums_on_scalar(1, 8, 10)
        sums_on_vector(0, 7, 10, y[0][:, 7 * C:10 * C])
        scatter_on_scalar(2, 8, 10)
        sums_on_scalar(2, 10, 12)
        sums_on_scalar(1, 10, 12)
        sums_on_vector(0, 10, 12, y[0][:, 10 * C:S])
        scatter_on_vector(0, 7, 10, y[0][:, 7 * C:10 * C])
        scatter_on_scalar(2, 10, 12)
        scatter_on_vector(0, 10, 12, y[0][:, 10 * C:S])
        scatter_on_scalar(1, 10, 12)
        scatter_on_scalar(1, 8, 10)
        store(2, nc.sync)
        store(0, nc.sync)
        store(1, nc.scalar)
